import numpy as np
import ml_dtypes


def mxq(x, axis, fmt="e4m3"):
    dtype, down = {"e4m3": (ml_dtypes.float8_e4m3fn, 7), "e5m2": (ml_dtypes.float8_e5m2, 14)}[fmt]
    v = np.moveaxis(np.asarray(x, np.float32).astype(ml_dtypes.bfloat16).astype(np.float64), axis, -1)
    blocks = v.reshape(v.shape[:-1] + (-1, 32))
    amax = np.abs(blocks).max(-1, keepdims=True)
    byte = np.maximum(np.where(amax > 0, np.frexp(amax)[1] - 1 + 127, 0) - down, 1)
    scale = np.exp2(byte - 127.0)
    codes = (blocks / scale).astype(np.float32).astype(dtype).astype(np.float64)
    return np.moveaxis((codes * scale).reshape(v.shape), -1, axis)


WIDE = False


def mx_kscale(k):
    if not WIDE:
        return np.ones(k)
    levels = np.array([30, -30])
    if k % 512:
        return np.exp2(np.random.permutation(np.resize(levels, k // 32))).repeat(32)
    a = np.empty((k // 512, 16))
    for p in range(k // 512):
        a[p, :8] = np.random.permutation(np.resize(levels, 8))
        for g in range(8):
            far = levels[np.abs(levels - a[p, g]) >= 10]
            a[p, g + 8] = far[np.random.randint(len(far))]
    return np.exp2(a.ravel()).repeat(32)


BF16 = ml_dtypes.bfloat16


def bf(x):
    return np.asarray(x, np.float32).astype(BF16)


def f64(x):
    return np.asarray(x).astype(np.float64)


M, N, E, J = 1024, 2048, 1024, 1536


def setup_inputs():
    s = mx_kscale(E)
    t = mx_kscale(J)
    queries = np.random.standard_normal((M, E)) * s
    corpus = np.random.standard_normal((N, E)) / np.sqrt(E) / s
    relevance = np.random.standard_normal((J, M)) ** 3 / 4 * t[:, None]
    sim = np.random.standard_normal((J, N)) / np.sqrt(J) / t[:, None]
    return {"queries": bf(queries),
            "corpus": bf(corpus),
            "relevance": bf(relevance),
            "sim": bf(sim),
            "gain": bf(1 + 0.1 * np.random.standard_normal(M)),
            "prior": bf(0.3 * np.random.standard_normal(N))}


def reference(queries, corpus, relevance, sim, gain, prior):
    qq = mxq(f64(queries), 1, "e4m3")
    cq = mxq(f64(corpus), 1, "e4m3")
    rq = mxq(f64(relevance), 0, "e5m2")
    sq = mxq(f64(sim), 0, "e4m3")
    score = (qq @ cq.T) + (rq.T @ sq)
    return score * f64(gain)[:, None] + f64(prior)[None, :]

@@ -1,0 +1,444 @@
+from contextlib import ExitStack
+
+import concourse.mybir as mybir
+from concourse.masks import make_identity
+
+F32 = mybir.dt.float32
+BF16 = mybir.dt.bfloat16
+U32 = mybir.dt.uint32
+U8 = mybir.dt.uint8
+E4M3X4 = mybir.dt.float8_e4m3fn_x4
+E5M2X4 = mybir.dt.float8_e5m2_x4
+MULT = mybir.AluOpType.mult
+ADD = mybir.AluOpType.add
+
+M, N, E, J = 1024, 2048, 1024, 1536
+FLOPS = 2 * M * N * (E + J)
+
+P = 128
+K_PASS = 512
+E_PASSES = E // K_PASS
+J_PASSES = J // K_PASS
+NB = 512
+M_TILES = M // P
+N_BLOCKS = N // NB
+WORDS = E // 2
+
+
+def tile_rocchio_feedback_rescore_s2_kernel(tc, queries, corpus, relevance, sim, gain, prior, out):
+    nc = tc.nc
+    with ExitStack() as ctx:
+        keep = ctx.enter_context(tc.tile_pool(name="keep", bufs=1))
+        raw = ctx.enter_context(tc.tile_pool(name="raw", bufs=1))
+        stage = ctx.enter_context(tc.tile_pool(name="stage", bufs=3))
+        psum = ctx.enter_context(tc.psum_pool(name="psum", bufs=1))
+        ctx.enter_context(tc.manual_schedule())
+
+        ident = keep.tile([P, P], F32, name="ident")
+        ident_bf = keep.tile([P, P], BF16, name="ident_bf")
+        rows = keep.tile([P, P], BF16, name="rows")
+        cols = keep.tile([P, 24], BF16, name="cols")
+        gain_col = keep.tile([P, M_TILES], F32, name="gain_col")
+        prior_bc = keep.tile([P, N_BLOCKS, NB], BF16, name="prior_bc")
+
+        q_codes = keep.tile([P, M_TILES, E_PASSES, P], U32, name="q_codes", align_bytes=256)
+        q_scales = keep.tile([P, M_TILES, E_PASSES, P], U8, name="q_scales", align_bytes=256)
+        r_codes = keep.tile([P, J_PASSES, M], U32, name="r_codes", align_bytes=256)
+        r_scales = keep.tile([P, J_PASSES, M], U8, name="r_scales", align_bytes=256)
+        q_raw = raw.tile([P, M_TILES, E], BF16, name="q_raw", align_bytes=256)
+        r_raw, c_raw, s_raw, c_codes, c_scales, s_codes, s_scales = {}, {}, {}, {}, {}, {}, {}
+
+        q_view = queries.rearrange("(t p) e -> p t e", p=P)
+        c_view = corpus.rearrange("(t p) e -> p t e", p=P)
+        r_view = relevance.rearrange("(c p j) m -> c p j m", p=P, j=4)
+        s_view = sim.rearrange("(c p j) n -> c p j n", p=P, j=4)
+
+        def load_q(t0, t1):
+            nc.sync.dma_start(out=q_raw[:, t0:t1, :], in_=q_view[:, t0:t1, :])
+
+        def load_r(c):
+            r_raw[c] = raw.tile([P, 4, M], BF16, name="wide_raw_t", bufs=3, align_bytes=256)
+            nc.sync.dma_start(out=r_raw[c][:], in_=r_view[c])
+
+        def load_c(n):
+            c_raw[n] = raw.tile([P, 4, E], BF16, name="c_raw_t", bufs=3, align_bytes=256)
+            step = 1 if n == 0 else 2
+            for t in range(0, 4, step):
+                nc.sync.dma_start(out=c_raw[n][:, t : t + step, :], in_=c_view[:, 4 * n + t : 4 * n + t + step, :])
+
+        def load_s(c, n):
+            tile_s = raw.tile([P, 4, NB], BF16, name="s_raw_t", bufs=6, align_bytes=256)
+            nc.sync.dma_start(out=tile_s[:], in_=s_view[c, :, :, n * NB : (n + 1) * NB])
+            s_raw[c, n] = tile_s[:]
+
+        def load_s_wide(c):
+            wide = raw.tile([P, 4, 2 * NB], BF16, name="wide_raw_t", bufs=3, align_bytes=256)
+            nc.sync.dma_start(out=wide[:], in_=s_view[c, :, :, 2 * NB :])
+            for h in range(2):
+                s_raw[c, 2 + h] = wide[:, :, h * NB : (h + 1) * NB]
+
+        def bank_tile(b, shape=(P, NB), dtype=F32):
+            return psum.tile(list(shape), dtype, name="bank_t", tag=f"bank{b}")
+
+        def copy_words(engine, dst, src):
+            if engine == "S":
+                nc.scalar.copy(out=dst, in_=src)
+            else:
+                nc.vector.tensor_copy(out=dst, in_=src)
+
+        def turn(words, bank):
+            for g in range(E_PASSES):
+                for u in range(2):
+                    s = 2 * g + u
+                    nc.tensor.transpose(
+                        bank[:, s * P : (s + 1) * P], words[:, 256 * g + u : 256 * (g + 1) : 2], ident[:]
+                    )
+
+        c_sort = {}
+
+        def sort_c(n, t, engine="V"):
+            if t == 0:
+                c_sort[n] = raw.tile([P, 4, WORDS], F32, name="c_sort_t", bufs=1, align_bytes=256)
+            copy_words(
+                engine,
+                c_sort[n][:, t, :].rearrange("p (g u w) -> p g u w", g=2, u=2),
+                c_raw[n][:, t, :].bitcast(F32).rearrange("p (g w u) -> p g u w", g=2, u=2),
+            )
+
+        q_bank, q_grp = {}, {}
+
+        def turn_q(m, b):
+            q_bank[m] = bank_tile(b)
+            turn(q_raw[:, m, :].bitcast(F32), q_bank[m])
+
+        def copy_q(m, engine):
+            q_grp[m] = stage.tile([P, E_PASSES, P, 4], BF16, name="q_grp_t", bufs=6, align_bytes=256)
+            copy_words(
+                engine,
+                q_grp[m][:].rearrange("p g r j -> p (g r j)").bitcast(F32).rearrange("p (g r u) -> p g r u", g=2, u=2),
+                q_bank[m][:].rearrange("p (g u r) -> p g r u", g=2, u=2),
+            )
+
+        def quant_q(m):
+            nc.vector.quantize_mx(
+                out=q_codes[:, m, :, :].rearrange("p g r -> p (g r)").bitcast(E4M3X4),
+                scales=q_scales[:, m, :, :].rearrange("p g r -> p (g r)"),
+                in_=q_grp[m][:].rearrange("p g r j -> p (g r j)"),
+            )
+
+        c_bank, c_grp = {}, {}
+
+        def turn_c(n, t, b):
+            c_bank[n, t] = bank_tile(b)
+            if n == 0:
+                turn(c_raw[n][:, t, :].bitcast(F32), c_bank[n, t])
+            else:
+                for s in range(4):
+                    nc.tensor.transpose(
+                        c_bank[n, t][:, s * P : (s + 1) * P], c_sort[n][:, t, s * P : (s + 1) * P], ident[:]
+                    )
+
+        def copy_c(n, t, engine):
+            if t == 0:
+                c_grp[n] = stage.tile([P, E_PASSES, NB, 4], BF16, name="c_grp_t", bufs=2, align_bytes=256)
+            words = c_grp[n][:].rearrange("p g r j -> p (g r j)").bitcast(F32)
+            copy_words(
+                engine,
+                words.rearrange("p (g r u) -> p g r u", g=2, u=2)[:, :, t * P : (t + 1) * P, :],
+                c_bank[n, t][:].rearrange("p (g u r) -> p g r u", g=2, u=2),
+            )
+
+        def quant_c(n, g, h):
+            if g == 0 and h == 0:
+                c_codes[n] = stage.tile([P, E_PASSES, NB], U32, name="c_codes_t", bufs=2, align_bytes=256)
+                c_scales[n] = stage.tile([P, E_PASSES, NB], U8, name="c_scales_t", bufs=2, align_bytes=256)
+            cs = slice(h * 256, (h + 1) * 256)
+            nc.vector.quantize_mx(
+                out=c_codes[n][:, g, cs].bitcast(E4M3X4),
+                scales=c_scales[n][:, g, cs],
+                in_=c_grp[n][:, g, cs, :].rearrange("p r j -> p (r j)"),
+            )
+
+        r_grp, s_grp = {}, {}
+
+        def interleave(engine, dst, src):
+            copy_words(
+                engine,
+                dst.rearrange("p (c i) j -> p c j i", i=4),
+                src.rearrange("p j (c i) -> p c j i", i=4),
+            )
+
+        def copy_r(c, h, engine):
+            r_grp[c, h] = stage.tile([P, NB, 4], BF16, name="k_grp_t", bufs=6, align_bytes=256)
+            interleave(engine, r_grp[c, h][:], r_raw[c][:, :, h * NB : (h + 1) * NB])
+
+        def quant_r(c, h):
+            nc.vector.quantize_mx(
+                out=r_codes[:, c, h * NB : (h + 1) * NB].bitcast(E5M2X4),
+                scales=r_scales[:, c, h * NB : (h + 1) * NB],
+                in_=r_grp[c, h][:].rearrange("p w j -> p (w j)"),
+            )
+
+        def copy_s(c, n, engines):
+            s_grp[c, n] = stage.tile([P, NB, 4], BF16, name="k_grp_t", bufs=6, align_bytes=256)
+            w = NB // len(engines)
+            for i, engine in enumerate(engines):
+                cs = slice(i * w, (i + 1) * w)
+                interleave(engine, s_grp[c, n][:, cs, :], s_raw[c, n][:, :, cs])
+
+        def quant_s(c, n):
+            s_codes[c, n] = stage.tile([P, NB], U32, name="s_codes_t", bufs=7, align_bytes=256)
+            s_scales[c, n] = stage.tile([P, NB], U8, name="s_scales_t", bufs=7, align_bytes=256)
+            nc.vector.quantize_mx(
+                out=s_codes[c, n][:].bitcast(E4M3X4),
+                scales=s_scales[c, n][:],
+                in_=s_grp[c, n][:].rearrange("p w j -> p (w j)"),
+            )
+
+        acc = {}
+
+        def pass_qc(n, m, g, b):
+            if g == 0:
+                acc[n, m] = bank_tile(b)
+            nc.tensor.matmul_mx(
+                out=acc[n, m][:],
+                lhsT=q_codes[:, m, g, :].bitcast(E4M3X4),
+                lhsT_scale=q_scales[:, m, g, :],
+                rhs=c_codes[n][:, g, :].bitcast(E4M3X4),
+                rhs_scale=c_scales[n][:, g, :],
+                start=(g == 0),
+                stop=False,
+            )
+
+        def pass_rs(n, m, c):
+            nc.tensor.matmul_mx(
+                out=acc[n, m][:],
+                lhsT=r_codes[:, c, m * P : (m + 1) * P].bitcast(E5M2X4),
+                lhsT_scale=r_scales[:, c, m * P : (m + 1) * P],
+                rhs=s_codes[c, n][:].bitcast(E4M3X4),
+                rhs_scale=s_scales[c, n][:],
+                start=False,
+                stop=(c == J_PASSES - 1),
+            )
+
+        def load_vectors():
+            nc.sync.dma_start(out=rows[0:16, :], in_=prior.rearrange("(a b) -> a b", b=P))
+            nc.sync.dma_start(out=rows[16:24, :], in_=gain.rearrange("(a b) -> a b", b=P))
+
+        vec = {}
+
+        def turn_vectors():
+            vec["rows"] = bank_tile(7, (P, P), BF16)
+            nc.tensor.transpose(vec["rows"][:], rows[:], ident_bf[:])
+
+        def copy_vectors():
+            nc.vector.tensor_copy(out=cols[:], in_=vec["rows"][:, 0:24])
+            nc.vector.tensor_copy(out=gain_col[:], in_=vec["rows"][:, 16:24])
+
+        def turn_prior(h):
+            vec[h] = bank_tile(4 + h, (P, M), BF16)
+            for i in range(8):
+                nc.tensor.transpose(
+                    vec[h][:, i * P : (i + 1) * P], cols[:, 8 * h + i : 8 * h + i + 1].to_broadcast([P, P]), ident_bf[:]
+                )
+
+        def copy_prior(h, engine):
+            copy_words(engine, prior_bc[:, 2 * h : 2 * h + 2, :].rearrange("p n w -> p (n w)"), vec[h][:])
+
+        def keep_busy(passes):
+            spare = bank_tile(5)
+            for i in range(passes):
+                nc.tensor.matmul_mx(
+                    out=spare[:],
+                    lhsT=q_codes[:, 0, 0, :].bitcast(E4M3X4),
+                    lhsT_scale=q_scales[:, 0, 0, :],
+                    rhs=q_codes[:, 0:2, :, :].rearrange("p m g r -> p (m g r)").bitcast(E4M3X4),
+                    rhs_scale=q_scales[:, 0:2, :, :].rearrange("p m g r -> p (m g r)"),
+                    start=True,
+                    stop=True,
+                )
+
+        def finish(n, m, pieces=1):
+            res = stage.tile([P, NB], F32, name="res_t", bufs=12)
+            w = NB // pieces
+            for i in range(pieces):
+                cs = slice(i * w, (i + 1) * w)
+                oc = slice(n * NB + i * w, n * NB + (i + 1) * w)
+                nc.vector.scalar_tensor_tensor(
+                    out=res[:, cs],
+                    in0=acc[n, m][:, cs],
+                    scalar=gain_col[:, m : m + 1],
+                    in1=prior_bc[:, n, cs],
+                    op0=MULT,
+                    op1=ADD,
+                )
+                nc.sync.dma_start(out=out[m * P : (m + 1) * P, oc], in_=res[:, cs])
+
+        V, S = "V", "S"
+        halves = (range(0, 4), range(4, 8))
+
+        nc.vector.memset(rows[:], 0.0)
+        load_q(0, 1)
+        load_q(1, 2)
+        load_vectors()
+        load_q(2, 4)
+        load_r(0)
+        load_q(4, 6)
+        load_q(6, 8)
+        load_c(0)
+        load_r(1)
+        load_s(0, 0)
+        load_s(1, 0)
+        load_r(2)
+        load_s(2, 0)
+        load_c(1)
+        for c in range(3):
+            load_s(c, 1)
+
+        make_identity(nc, ident[:])
+        nc.vector.tensor_copy(out=ident_bf[:], in_=ident[:])
+
+        for m in (0, 1):
+            turn_q(m, m)
+            copy_q(m, S)
+        turn_vectors()
+        copy_vectors()
+        quant_q(0)
+        quant_q(1)
+        for m in (2, 3):
+            turn_q(m, m)
+            copy_q(m, (S, V)[m % 2])
+        for h in range(2):
+            turn_prior(h)
+            copy_prior(h, (V, S)[h])
+        copy_r(0, 0, V)
+        copy_r(0, 1, S)
+        quant_r(0, 0)
+        for m in range(4, 8):
+            turn_q(m, m)
+            copy_q(m, S)
+        quant_q(2)
+        quant_q(3)
+        quant_r(0, 1)
+        quant_q(4)
+        quant_q(5)
+        quant_q(6)
+        for t in range(4):
+            turn_c(0, t, 1 + t)
+            copy_c(0, t, (S, V)[t % 2])
+            if t == 2:
+                quant_q(7)
+                quant_c(0, 0, 0)
+        quant_c(0, 0, 1)
+        quant_c(0, 1, 0)
+        quant_c(0, 1, 1)
+        keep_busy(3)
+        for g in range(2):
+            for m in range(8):
+                pass_qc(0, m, g, m)
+        copy_r(1, 0, S)
+        copy_r(1, 1, V)
+        copy_s(0, 0, V)
+        quant_r(1, 1)
+        quant_s(0, 0)
+        quant_r(1, 0)
+        copy_s(1, 0, S)
+        for m in range(8):
+            pass_rs(0, m, 0)
+        copy_r(2, 0, V)
+        copy_r(2, 1, S)
+        quant_s(1, 0)
+        copy_s(2, 0, V + S)
+        quant_r(2, 0)
+        for m in range(8):
+            pass_rs(0, m, 1)
+        quant_s(2, 0)
+        quant_r(2, 1)
+        load_c(2)
+        for c in range(3):
+            load_s_wide(c)
+        for m in range(0, 4):
+            pass_rs(0, m, 2)
+        sort_c(1, 0, S)
+        sort_c(1, 1, S)
+        sort_c(1, 2)
+        sort_c(1, 3)
+        finish(0, 0)
+        finish(0, 1)
+        finish(0, 2)
+        finish(0, 3)
+        load_c(3)
+        copy_s(0, 1, S)
+        for h in range(2):
+            for t in (2 * h, 2 * h + 1):
+                turn_c(1, t, t)
+                copy_c(1, t, S)
+            for m in (4 + 2 * h, 5 + 2 * h):
+                pass_rs(0, m, 2)
+        finish(0, 4)
+        for g in range(2):
+            quant_c(1, g, 0)
+        finish(0, 5)
+        for g in range(2):
+            quant_c(1, g, 1)
+        finish(0, 6)
+        finish(0, 7)
+        quant_s(0, 1)
+        copy_s(1, 1, V + S)
+        copy_s(2, 1, V + S)
+        quant_s(1, 1)
+
+        for n in range(1, N_BLOCKS):
+            more = n + 1 < N_BLOCKS
+            if n == 1:
+                for g in range(2):
+                    for m in range(6):
+                        pass_qc(n, m, g, m)
+                quant_s(2, 1)
+                for t in range(4):
+                    sort_c(2, t)
+                copy_s(0, 2, S)
+                for c in range(2):
+                    for m in range(4):
+                        pass_rs(n, m, c)
+                for h in range(2):
+                    for t in (2 * h, 2 * h + 1):
+                        turn_c(2, t, 6 + t % 2)
+                        copy_c(2, t, S)
+                    for m in (2 * h, 2 * h + 1):
+                        pass_rs(n, m, 2)
+                        finish(n, m)
+                    for g in range(2):
+                        quant_c(2, g, h)
+            for m in range(M_TILES):
+                if n > 1 or m > 5:
+                    for g in range(2):
+                        pass_qc(n, m, g, m)
+                if n > 1 or m > 3:
+                    for c in range(3):
+                        pass_rs(n, m, c)
+                if more:
+                    if m == 0 and n == 2:
+                        copy_s(0, n + 1, S)
+                    if m == 2:
+                        copy_s(1, n + 1, S)
+                    if m == 3:
+                        quant_s(0, n + 1)
+                    if m < 4 and n == 2:
+                        sort_c(n + 1, m)
+                    if m == 3 and n == 2:
+                        for t in range(4):
+                            turn_c(n + 1, t, t if t < 3 else 7)
+                            copy_c(n + 1, t, S)
+                if n > 1 or m > 3:
+                    finish(n, m, 2 if m == 7 and not more else 1)
+                if more:
+                    if m == 4:
+                        copy_s(2, n + 1, V + S)
+                        if n == 2:
+                            for h in range(2):
+                                for g in range(2):
+                                    quant_c(n + 1, g, h)
+                    if m == 5:
+                        quant_s(1, n + 1)
+                        quant_s(2, n + 1)

@@ -16,13 +16,14 @@ M, N, E, J = 1024, 2048, 1024, 1536
 FLOPS = 2 * M * N * (E + J)
 
 P = 128
-K_PASS = 512
-E_PASSES = E // K_PASS
-J_PASSES = J // K_PASS
+E_PASSES = 2
+J_PASSES = 3
 NB = 512
 M_TILES = M // P
 N_BLOCKS = N // NB
+PAIR = 2 * P
 WORDS = E // 2
+AL = 256
 
 
 def tile_rocchio_feedback_rescore_s2_kernel(tc, queries, corpus, relevance, sim, gain, prior, out):
@@ -30,415 +31,384 @@ def tile_rocchio_feedback_rescore_s2_kernel(tc, queries, corpus, relevance, sim,
     with ExitStack() as ctx:
         keep = ctx.enter_context(tc.tile_pool(name="keep", bufs=1))
         raw = ctx.enter_context(tc.tile_pool(name="raw", bufs=1))
-        stage = ctx.enter_context(tc.tile_pool(name="stage", bufs=3))
+        stage = ctx.enter_context(tc.tile_pool(name="stage", bufs=1))
         psum = ctx.enter_context(tc.psum_pool(name="psum", bufs=1))
         ctx.enter_context(tc.manual_schedule())
+        V, S = "V", "S"
 
         ident = keep.tile([P, P], F32, name="ident")
         ident_bf = keep.tile([P, P], BF16, name="ident_bf")
         rows = keep.tile([P, P], BF16, name="rows")
-        cols = keep.tile([P, 24], BF16, name="cols")
         gain_col = keep.tile([P, M_TILES], F32, name="gain_col")
-        prior_bc = keep.tile([P, N_BLOCKS, NB], BF16, name="prior_bc")
+        prior_raw = keep.tile([P, 16], BF16, name="prior_raw")
+        prior_words = keep.tile([P, P, 8], F32, name="prior_words")
 
-        q_codes = keep.tile([P, M_TILES, E_PASSES, P], U32, name="q_codes", align_bytes=256)
-        q_scales = keep.tile([P, M_TILES, E_PASSES, P], U8, name="q_scales", align_bytes=256)
-        r_codes = keep.tile([P, J_PASSES, M], U32, name="r_codes", align_bytes=256)
-        r_scales = keep.tile([P, J_PASSES, M], U8, name="r_scales", align_bytes=256)
-        q_raw = raw.tile([P, M_TILES, E], BF16, name="q_raw", align_bytes=256)
-        r_raw, c_raw, s_raw, c_codes, c_scales, s_codes, s_scales = {}, {}, {}, {}, {}, {}, {}
+        q_codes = keep.tile([P, 4, E_PASSES, PAIR], U32, name="q_codes", align_bytes=AL)
+        q_scales = keep.tile([P, 4, E_PASSES, PAIR], U8, name="q_scales", align_bytes=AL)
+        r_codes = keep.tile([P, J_PASSES, M], U32, name="r_codes", align_bytes=AL)
+        r_scales = keep.tile([P, J_PASSES, M], U8, name="r_scales", align_bytes=AL)
 
-        q_view = queries.rearrange("(t p) e -> p t e", p=P)
-        c_view = corpus.rearrange("(t p) e -> p t e", p=P)
+        pair_view = {
+            "q": queries.rearrange("(a p t) e -> a p t e", p=P, t=2),
+            "c": corpus.rearrange("(a p t) e -> a p t e", p=P, t=2),
+        }
         r_view = relevance.rearrange("(c p j) m -> c p j m", p=P, j=4)
         s_view = sim.rearrange("(c p j) n -> c p j n", p=P, j=4)
 
-        def load_q(t0, t1):
-            nc.sync.dma_start(out=q_raw[:, t0:t1, :], in_=q_view[:, t0:t1, :])
+        pair_raw, k_raw = {}, {}
 
-        def load_r(c):
-            r_raw[c] = raw.tile([P, 4, M], BF16, name="wide_raw_t", bufs=3, align_bytes=256)
-            nc.sync.dma_start(out=r_raw[c][:], in_=r_view[c])
+        def load_pair(x, a):
+            pair_raw[x, a] = raw.tile([P, 2, E], BF16, name="pair_raw_t", bufs=8, align_bytes=AL)
+            nc.sync.dma_start(out=pair_raw[x, a][:], in_=pair_view[x][a])
 
-        def load_c(n):
-            c_raw[n] = raw.tile([P, 4, E], BF16, name="c_raw_t", bufs=3, align_bytes=256)
-            step = 1 if n == 0 else 2
-            for t in range(0, 4, step):
-                nc.sync.dma_start(out=c_raw[n][:, t : t + step, :], in_=c_view[:, 4 * n + t : 4 * n + t + step, :])
+        def load_k(x, c, b, blocks=1):
+            view = r_view if x == "r" else s_view
+            if blocks == 1:
+                rows4 = raw.tile([P, 4, NB], BF16, name="narrow_raw_t", bufs=6, align_bytes=AL)
+            else:
+                rows4 = raw.tile([P, 4, 2 * NB], BF16, name="wide_raw_t", bufs=3, align_bytes=AL)
+            nc.sync.dma_start(out=rows4[:], in_=view[c, :, :, b * NB : (b + blocks) * NB])
+            for i in range(blocks):
+                k_raw[x, c, b + i] = rows4[:, :, i * NB : (i + 1) * NB]
 
-        def load_s(c, n):
-            tile_s = raw.tile([P, 4, NB], BF16, name="s_raw_t", bufs=6, align_bytes=256)
-            nc.sync.dma_start(out=tile_s[:], in_=s_view[c, :, :, n * NB : (n + 1) * NB])
-            s_raw[c, n] = tile_s[:]
+        def load_prior():
+            nc.sync.dma_start(out=prior_raw[:], in_=prior.rearrange("(p i) -> p i", p=P))
 
-        def load_s_wide(c):
-            wide = raw.tile([P, 4, 2 * NB], BF16, name="wide_raw_t", bufs=3, align_bytes=256)
-            nc.sync.dma_start(out=wide[:], in_=s_view[c, :, :, 2 * NB :])
-            for h in range(2):
-                s_raw[c, 2 + h] = wide[:, :, h * NB : (h + 1) * NB]
+        def load_gain():
+            nc.sync.dma_start(out=rows[0:M_TILES, :], in_=gain.rearrange("(a b) -> a b", b=P))
 
         def bank_tile(b, shape=(P, NB), dtype=F32):
             return psum.tile(list(shape), dtype, name="bank_t", tag=f"bank{b}")
 
-        def copy_words(engine, dst, src):
-            if engine == "S":
+        def copy(engine, dst, src):
+            if engine == S:
                 nc.scalar.copy(out=dst, in_=src)
             else:
                 nc.vector.tensor_copy(out=dst, in_=src)
 
-        def turn(words, bank):
-            for g in range(E_PASSES):
+        pair_sorted, turned, grouped = {}, {}, {}
+
+        def sort(x, a, engine):
+            pair_sorted[x, a] = raw.tile([P, 4, 2, P], F32, name="sorted_t", bufs=2, align_bytes=AL)
+            copy(
+                engine,
+                pair_sorted[x, a][:],
+                pair_raw[x, a][:].rearrange("p t e -> p (t e)").bitcast(F32).rearrange("p (s w u) -> p s u w", s=4, u=2),
+            )
+
+        def turn(x, a, g, b):
+            turned[x, a, g] = bank_tile(b)
+            for t in range(2):
                 for u in range(2):
-                    s = 2 * g + u
-                    nc.tensor.transpose(
-                        bank[:, s * P : (s + 1) * P], words[:, 256 * g + u : 256 * (g + 1) : 2], ident[:]
-                    )
+                    if (x, a) in pair_sorted:
+                        src = pair_sorted[x, a][:, 2 * t + g, u, :]
+                    else:
+                        src = pair_raw[x, a][:, t, :].bitcast(F32)[:, 256 * g + u : 256 * (g + 1) : 2]
+                    s = 2 * t + u
+                    nc.tensor.transpose(turned[x, a, g][:, s * P : (s + 1) * P], src, ident[:])
 
-        c_sort = {}
-
-        def sort_c(n, t, engine="V"):
-            if t == 0:
-                c_sort[n] = raw.tile([P, 4, WORDS], F32, name="c_sort_t", bufs=1, align_bytes=256)
-            copy_words(
+        def drain(x, a, g, engine):
+            grouped[x, a, g] = stage.tile([P, PAIR * 4], BF16, name="turned_grp_t", bufs=6, align_bytes=AL)
+            copy(
                 engine,
-                c_sort[n][:, t, :].rearrange("p (g u w) -> p g u w", g=2, u=2),
-                c_raw[n][:, t, :].bitcast(F32).rearrange("p (g w u) -> p g u w", g=2, u=2),
+                grouped[x, a, g][:].bitcast(F32).rearrange("p (r s) -> p r s", s=4),
+                turned[x, a, g][:].rearrange("p (s r) -> p r s", s=4),
             )
 
-        q_bank, q_grp = {}, {}
+        c_codes, c_scales, s_codes, s_scales = {}, {}, {}, {}
 
-        def turn_q(m, b):
-            q_bank[m] = bank_tile(b)
-            turn(q_raw[:, m, :].bitcast(F32), q_bank[m])
-
-        def copy_q(m, engine):
-            q_grp[m] = stage.tile([P, E_PASSES, P, 4], BF16, name="q_grp_t", bufs=6, align_bytes=256)
-            copy_words(
-                engine,
-                q_grp[m][:].rearrange("p g r j -> p (g r j)").bitcast(F32).rearrange("p (g r u) -> p g r u", g=2, u=2),
-                q_bank[m][:].rearrange("p (g u r) -> p g r u", g=2, u=2),
-            )
-
-        def quant_q(m):
-            nc.vector.quantize_mx(
-                out=q_codes[:, m, :, :].rearrange("p g r -> p (g r)").bitcast(E4M3X4),
-                scales=q_scales[:, m, :, :].rearrange("p g r -> p (g r)"),
-                in_=q_grp[m][:].rearrange("p g r j -> p (g r j)"),
-            )
-
-        c_bank, c_grp = {}, {}
-
-        def turn_c(n, t, b):
-            c_bank[n, t] = bank_tile(b)
-            if n == 0:
-                turn(c_raw[n][:, t, :].bitcast(F32), c_bank[n, t])
+        def quant_pair(x, a, g):
+            if x == "q":
+                codes, scales = q_codes[:, a, g, :], q_scales[:, a, g, :]
             else:
-                for s in range(4):
-                    nc.tensor.transpose(
-                        c_bank[n, t][:, s * P : (s + 1) * P], c_sort[n][:, t, s * P : (s + 1) * P], ident[:]
-                    )
+                n, h = divmod(a, 2)
+                if h == 0:
+                    c_codes[n, g] = stage.tile([P, NB], U32, name="c_codes_t", bufs=4, align_bytes=AL)
+                    c_scales[n, g] = stage.tile([P, NB], U8, name="c_scales_t", bufs=4, align_bytes=AL)
+                cs = slice(h * PAIR, (h + 1) * PAIR)
+                codes, scales = c_codes[n, g][:, cs], c_scales[n, g][:, cs]
+            nc.vector.quantize_mx(out=codes.bitcast(E4M3X4), scales=scales, in_=grouped[x, a, g][:])
 
-        def copy_c(n, t, engine):
-            if t == 0:
-                c_grp[n] = stage.tile([P, E_PASSES, NB, 4], BF16, name="c_grp_t", bufs=2, align_bytes=256)
-            words = c_grp[n][:].rearrange("p g r j -> p (g r j)").bitcast(F32)
-            copy_words(
+        woven = {}
+
+        def weave(x, c, b, engine, lo=0, hi=NB):
+            if (x, c, b) not in woven:
+                woven[x, c, b] = stage.tile([P, NB, 4], BF16, name="woven_t", bufs=5, align_bytes=AL)
+            copy(
                 engine,
-                words.rearrange("p (g r u) -> p g r u", g=2, u=2)[:, :, t * P : (t + 1) * P, :],
-                c_bank[n, t][:].rearrange("p (g u r) -> p g r u", g=2, u=2),
+                woven[x, c, b][:, lo:hi, :].rearrange("p (w i) j -> p w j i", i=4),
+                k_raw[x, c, b][:, :, lo:hi].rearrange("p j (w i) -> p w j i", i=4),
             )
 
-        def quant_c(n, g, h):
-            if g == 0 and h == 0:
-                c_codes[n] = stage.tile([P, E_PASSES, NB], U32, name="c_codes_t", bufs=2, align_bytes=256)
-                c_scales[n] = stage.tile([P, E_PASSES, NB], U8, name="c_scales_t", bufs=2, align_bytes=256)
-            cs = slice(h * 256, (h + 1) * 256)
-            nc.vector.quantize_mx(
-                out=c_codes[n][:, g, cs].bitcast(E4M3X4),
-                scales=c_scales[n][:, g, cs],
-                in_=c_grp[n][:, g, cs, :].rearrange("p r j -> p (r j)"),
-            )
+        def weave2(x, c, b, cut):
+            weave(x, c, b, S, 0, cut)
+            weave(x, c, b, V, cut, NB)
 
-        r_grp, s_grp = {}, {}
+        def quant_k(x, c, b):
+            if x == "r":
+                cs = slice(b * NB, (b + 1) * NB)
+                codes, scales = r_codes[:, c, cs].bitcast(E5M2X4), r_scales[:, c, cs]
+            else:
+                s_codes[c, b] = stage.tile([P, NB], U32, name="s_codes_t", bufs=7, align_bytes=AL)
+                s_scales[c, b] = stage.tile([P, NB], U8, name="s_scales_t", bufs=7, align_bytes=AL)
+                codes, scales = s_codes[c, b][:].bitcast(E4M3X4), s_scales[c, b][:]
+            nc.vector.quantize_mx(out=codes, scales=scales, in_=woven[x, c, b][:].rearrange("p w j -> p (w j)"))
 
-        def interleave(engine, dst, src):
-            copy_words(
-                engine,
-                dst.rearrange("p (c i) j -> p c j i", i=4),
-                src.rearrange("p j (c i) -> p c j i", i=4),
-            )
+        acc, done = {}, {}
 
-        def copy_r(c, h, engine):
-            r_grp[c, h] = stage.tile([P, NB, 4], BF16, name="k_grp_t", bufs=6, align_bytes=256)
-            interleave(engine, r_grp[c, h][:], r_raw[c][:, :, h * NB : (h + 1) * NB])
-
-        def quant_r(c, h):
-            nc.vector.quantize_mx(
-                out=r_codes[:, c, h * NB : (h + 1) * NB].bitcast(E5M2X4),
-                scales=r_scales[:, c, h * NB : (h + 1) * NB],
-                in_=r_grp[c, h][:].rearrange("p w j -> p (w j)"),
-            )
-
-        def copy_s(c, n, engines):
-            s_grp[c, n] = stage.tile([P, NB, 4], BF16, name="k_grp_t", bufs=6, align_bytes=256)
-            w = NB // len(engines)
-            for i, engine in enumerate(engines):
-                cs = slice(i * w, (i + 1) * w)
-                interleave(engine, s_grp[c, n][:, cs, :], s_raw[c, n][:, :, cs])
-
-        def quant_s(c, n):
-            s_codes[c, n] = stage.tile([P, NB], U32, name="s_codes_t", bufs=7, align_bytes=256)
-            s_scales[c, n] = stage.tile([P, NB], U8, name="s_scales_t", bufs=7, align_bytes=256)
-            nc.vector.quantize_mx(
-                out=s_codes[c, n][:].bitcast(E4M3X4),
-                scales=s_scales[c, n][:],
-                in_=s_grp[c, n][:].rearrange("p w j -> p (w j)"),
-            )
-
-        acc = {}
-
-        def pass_qc(n, m, g, b):
-            if g == 0:
-                acc[n, m] = bank_tile(b)
+        def mx_pass(n, m, lhsT, lhsT_scale, rhs, rhs_scale):
+            if (n, m) not in acc:
+                acc[n, m] = bank_tile(acc_bank(n, m))
+                done[n, m] = 0
+            done[n, m] = done[n, m] + 1
             nc.tensor.matmul_mx(
                 out=acc[n, m][:],
-                lhsT=q_codes[:, m, g, :].bitcast(E4M3X4),
-                lhsT_scale=q_scales[:, m, g, :],
-                rhs=c_codes[n][:, g, :].bitcast(E4M3X4),
-                rhs_scale=c_scales[n][:, g, :],
-                start=(g == 0),
-                stop=False,
+                lhsT=lhsT,
+                lhsT_scale=lhsT_scale,
+                rhs=rhs,
+                rhs_scale=rhs_scale,
+                start=(done[n, m] == 1),
+                stop=(done[n, m] == E_PASSES + J_PASSES),
             )
 
-        def pass_rs(n, m, c):
-            nc.tensor.matmul_mx(
-                out=acc[n, m][:],
-                lhsT=r_codes[:, c, m * P : (m + 1) * P].bitcast(E5M2X4),
-                lhsT_scale=r_scales[:, c, m * P : (m + 1) * P],
-                rhs=s_codes[c, n][:].bitcast(E4M3X4),
-                rhs_scale=s_scales[c, n][:],
-                start=False,
-                stop=(c == J_PASSES - 1),
+        def qc(n, tiles, g):
+            for m in tiles:
+                cs = slice((m % 2) * P, (m % 2 + 1) * P)
+                mx_pass(
+                    n, m, q_codes[:, m // 2, g, cs].bitcast(E4M3X4), q_scales[:, m // 2, g, cs],
+                    c_codes[n, g][:].bitcast(E4M3X4), c_scales[n, g][:],
+                )
+
+        def rs(n, tiles, c):
+            for m in tiles:
+                cs = slice(m * P, (m + 1) * P)
+                mx_pass(
+                    n, m, r_codes[:, c, cs].bitcast(E5M2X4), r_scales[:, c, cs],
+                    s_codes[c, n][:].bitcast(E4M3X4), s_scales[c, n][:],
+                )
+
+        def whole(n, m):
+            for g in range(E_PASSES):
+                qc(n, [m], g)
+            for c in range(J_PASSES):
+                rs(n, [m], c)
+
+        def spread_gain(b):
+            bank = bank_tile(b, (P, P), BF16)
+            nc.tensor.transpose(bank[:], rows[:], ident_bf[:])
+            nc.vector.tensor_copy(out=gain_col[:], in_=bank[:, 0:M_TILES])
+
+        def spread_prior(h, b, engine):
+            bank = bank_tile(b)
+            words = prior_raw[:].bitcast(F32)
+            for i in range(4):
+                col = words[:, 4 * h + i : 4 * h + i + 1]
+                nc.tensor.transpose(bank[:, i * P : (i + 1) * P], col.to_broadcast([P, P]), ident[:])
+            copy(engine, prior_words[:, :, 4 * h : 4 * h + 4], bank[:].rearrange("p (i w) -> p w i", i=4))
+
+        prior_bc = prior_words[:].rearrange("p w i -> p (w i)").bitcast(BF16)
+
+        res = {}
+
+        def finish(n, m, lo=0, hi=NB):
+            if n == 0:
+                both = stage.tile([P, 2 * NB], F32, name="res_pair_t", bufs=M_TILES)
+                res[0, m], res[1, m], res["pair", m] = both[:, :NB], both[:, NB:], both[:]
+            elif n > 1 and lo == 0:
+                one = stage.tile([P, NB], F32, name="res_t", bufs=RES_BUFS)
+                res[n, m] = one[:]
+            nc.vector.scalar_tensor_tensor(
+                out=res[n, m][:, lo:hi],
+                in0=acc[n, m][:, lo:hi],
+                scalar=gain_col[:, m : m + 1],
+                in1=prior_bc[:, n * NB + lo : n * NB + hi],
+                op0=MULT,
+                op1=ADD,
             )
 
-        def load_vectors():
-            nc.sync.dma_start(out=rows[0:16, :], in_=prior.rearrange("(a b) -> a b", b=P))
-            nc.sync.dma_start(out=rows[16:24, :], in_=gain.rearrange("(a b) -> a b", b=P))
+        def store(n, m, lo=0, hi=NB):
+            if n == 1:
+                nc.sync.dma_start(out=out[m * P : (m + 1) * P, : 2 * NB], in_=res["pair", m])
+            else:
+                nc.sync.dma_start(out=out[m * P : (m + 1) * P, n * NB + lo : n * NB + hi], in_=res[n, m][:, lo:hi])
 
-        vec = {}
 
-        def turn_vectors():
-            vec["rows"] = bank_tile(7, (P, P), BF16)
-            nc.tensor.transpose(vec["rows"][:], rows[:], ident_bf[:])
+        RES_BUFS = 8
+        EARLY, LATE = range(0, 4), range(4, 8)
+        FIRST = range(6)
 
-        def copy_vectors():
-            nc.vector.tensor_copy(out=cols[:], in_=vec["rows"][:, 0:24])
-            nc.vector.tensor_copy(out=gain_col[:], in_=vec["rows"][:, 16:24])
+        def acc_bank(n, m):
+            return m
 
-        def turn_prior(h):
-            vec[h] = bank_tile(4 + h, (P, M), BF16)
-            for i in range(8):
-                nc.tensor.transpose(
-                    vec[h][:, i * P : (i + 1) * P], cols[:, 8 * h + i : 8 * h + i + 1].to_broadcast([P, P]), ident_bf[:]
-                )
+        def turn_pair(x, a, b, engines):
+            for g in range(2):
+                turn(x, a, g, b + g)
+                drain(x, a, g, engines[g])
 
-        def copy_prior(h, engine):
-            copy_words(engine, prior_bc[:, 2 * h : 2 * h + 2, :].rearrange("p n w -> p (n w)"), vec[h][:])
+        def quant_both(x, a):
+            for g in range(2):
+                quant_pair(x, a, g)
 
-        def keep_busy(passes):
-            spare = bank_tile(5)
-            for i in range(passes):
-                nc.tensor.matmul_mx(
-                    out=spare[:],
-                    lhsT=q_codes[:, 0, 0, :].bitcast(E4M3X4),
-                    lhsT_scale=q_scales[:, 0, 0, :],
-                    rhs=q_codes[:, 0:2, :, :].rearrange("p m g r -> p (m g r)").bitcast(E4M3X4),
-                    rhs_scale=q_scales[:, 0:2, :, :].rearrange("p m g r -> p (m g r)"),
-                    start=True,
-                    stop=True,
-                )
+        def turn_c(n, g):
+            for h in range(2):
+                turn("c", 2 * n + h, g, 2 * g + h)
+                drain("c", 2 * n + h, g, S)
 
-        def finish(n, m, pieces=1):
-            res = stage.tile([P, NB], F32, name="res_t", bufs=12)
-            w = NB // pieces
-            for i in range(pieces):
-                cs = slice(i * w, (i + 1) * w)
-                oc = slice(n * NB + i * w, n * NB + (i + 1) * w)
-                nc.vector.scalar_tensor_tensor(
-                    out=res[:, cs],
-                    in0=acc[n, m][:, cs],
-                    scalar=gain_col[:, m : m + 1],
-                    in1=prior_bc[:, n, cs],
-                    op0=MULT,
-                    op1=ADD,
-                )
-                nc.sync.dma_start(out=out[m * P : (m + 1) * P, oc], in_=res[:, cs])
+        def quant_c(n, g):
+            for h in range(2):
+                quant_pair("c", 2 * n + h, g)
 
-        V, S = "V", "S"
-        halves = (range(0, 4), range(4, 8))
-
-        nc.vector.memset(rows[:], 0.0)
-        load_q(0, 1)
-        load_q(1, 2)
-        load_vectors()
-        load_q(2, 4)
-        load_r(0)
-        load_q(4, 6)
-        load_q(6, 8)
-        load_c(0)
-        load_r(1)
-        load_s(0, 0)
-        load_s(1, 0)
-        load_r(2)
-        load_s(2, 0)
-        load_c(1)
-        for c in range(3):
-            load_s(c, 1)
-
+        head_pairs = (("q", 0), ("c", 0), ("c", 1), ("q", 1), ("q", 2), ("q", 3))
+        nc.gpsimd.memset(rows[:], 0.0)
         make_identity(nc, ident[:])
-        nc.vector.tensor_copy(out=ident_bf[:], in_=ident[:])
+        make_identity(nc, ident_bf[:])
+        load_prior()
+        for x, a in head_pairs[:3]:
+            load_pair(x, a)
+        load_gain()
+        for x, a in head_pairs[3:5]:
+            load_pair(x, a)
+        load_k("r", 0, 0, 2)
+        load_pair("q", 3)
+        for c in range(2):
+            load_k("s", c, 0)
+        load_k("r", 1, 0, 2)
+        load_k("s", 2, 0)
+        load_k("r", 2, 0)
+        load_k("r", 2, 1)
+        load_k("s", 0, 1)
 
-        for m in (0, 1):
-            turn_q(m, m)
-            copy_q(m, S)
-        turn_vectors()
-        copy_vectors()
-        quant_q(0)
-        quant_q(1)
-        for m in (2, 3):
-            turn_q(m, m)
-            copy_q(m, (S, V)[m % 2])
-        for h in range(2):
-            turn_prior(h)
-            copy_prior(h, (V, S)[h])
-        copy_r(0, 0, V)
-        copy_r(0, 1, S)
-        quant_r(0, 0)
-        for m in range(4, 8):
-            turn_q(m, m)
-            copy_q(m, S)
-        quant_q(2)
-        quant_q(3)
-        quant_r(0, 1)
-        quant_q(4)
-        quant_q(5)
-        quant_q(6)
-        for t in range(4):
-            turn_c(0, t, 1 + t)
-            copy_c(0, t, (S, V)[t % 2])
-            if t == 2:
-                quant_q(7)
-                quant_c(0, 0, 0)
-        quant_c(0, 0, 1)
-        quant_c(0, 1, 0)
-        quant_c(0, 1, 1)
-        keep_busy(3)
+        spread_prior(0, 0, S)
+        spread_prior(1, 1, V)
+        for i, (x, a) in enumerate(head_pairs[:5]):
+            for g in range(2):
+                turn(x, a, g, 2 + (2 * i + g) % 6)
+                drain(x, a, g, V if g == 1 and i < 3 else S)
+            if i == 2:
+                spread_gain(0)
+            if i > 0:
+                quant_both(*head_pairs[i - 1])
+        quant_both("q", 2)
         for g in range(2):
-            for m in range(8):
-                pass_qc(0, m, g, m)
-        copy_r(1, 0, S)
-        copy_r(1, 1, V)
-        copy_s(0, 0, V)
-        quant_r(1, 1)
-        quant_s(0, 0)
-        quant_r(1, 0)
-        copy_s(1, 0, S)
-        for m in range(8):
-            pass_rs(0, m, 0)
-        copy_r(2, 0, V)
-        copy_r(2, 1, S)
-        quant_s(1, 0)
-        copy_s(2, 0, V + S)
-        quant_r(2, 0)
-        for m in range(8):
-            pass_rs(0, m, 1)
-        quant_s(2, 0)
-        quant_r(2, 1)
-        load_c(2)
-        for c in range(3):
-            load_s_wide(c)
-        for m in range(0, 4):
-            pass_rs(0, m, 2)
-        sort_c(1, 0, S)
-        sort_c(1, 1, S)
-        sort_c(1, 2)
-        sort_c(1, 3)
+            qc(0, EARLY, g)
+        weave2("r", 0, 0, 272)
+        weave2("r", 0, 1, 272)
+        quant_k("r", 0, 0)
+        weave2("s", 0, 0, 128)
+        quant_k("r", 0, 1)
+        turn_pair("q", 3, 6, (S, S))
+        for g in range(2):
+            qc(0, (4, 5), g)
+        weave("s", 1, 0, V, 272, NB)
+        quant_k("s", 0, 0)
+        quant_both("q", 3)
+        weave("s", 1, 0, S, 0, 272)
+        rs(0, range(6), 0)
+        for g in range(2):
+            qc(0, (6, 7), g)
+        rs(0, (6, 7), 0)
+        quant_k("s", 1, 0)
+        weave2("r", 1, 0, 256)
+        weave2("r", 1, 1, 256)
+        quant_k("r", 1, 0)
+        rs(0, EARLY, 1)
+        weave2("s", 2, 0, 256)
+        quant_k("r", 1, 1)
+        rs(0, LATE, 1)
+        weave2("r", 2, 0, 192)
+        quant_k("s", 2, 0)
+        quant_k("r", 2, 0)
+        weave2("r", 2, 1, 272)
+        rs(0, EARLY, 2)
+        quant_k("r", 2, 1)
+        rs(0, (4, 5), 2)
+        load_pair("c", 2)
+        load_pair("c", 3)
+        load_k("s", 1, 1)
+        load_k("s", 2, 1)
+        load_k("s", 0, 2, 2)
+        load_pair("c", 4)
+        load_pair("c", 5)
+        load_k("s", 1, 2, 2)
+        load_k("s", 2, 2, 2)
+        load_pair("c", 6)
+        load_pair("c", 7)
+
+        weave("s", 0, 1, S)
         finish(0, 0)
         finish(0, 1)
+        turn_pair("c", 2, 0, (S, S))
+        rs(0, (6, 7), 2)
         finish(0, 2)
         finish(0, 3)
-        load_c(3)
-        copy_s(0, 1, S)
+        turn_pair("c", 3, 2, (S, S))
+        quant_k("s", 0, 1)
+        weave("s", 1, 1, S)
+        for m in LATE:
+            finish(0, m)
+        rs(1, range(8), 0)
+        quant_c(1, 0)
+        quant_c(1, 1)
+        weave("s", 2, 1, S)
+        qc(1, range(8), 0)
+        quant_k("s", 1, 1)
+        qc(1, EARLY, 1)
+        weave("s", 0, 2, S)
         for h in range(2):
-            for t in (2 * h, 2 * h + 1):
-                turn_c(1, t, t)
-                copy_c(1, t, S)
-            for m in (4 + 2 * h, 5 + 2 * h):
-                pass_rs(0, m, 2)
-        finish(0, 4)
-        for g in range(2):
-            quant_c(1, g, 0)
-        finish(0, 5)
-        for g in range(2):
-            quant_c(1, g, 1)
-        finish(0, 6)
-        finish(0, 7)
-        quant_s(0, 1)
-        copy_s(1, 1, V + S)
-        copy_s(2, 1, V + S)
-        quant_s(1, 1)
+            sort("c", 4 + h, V)
+        rs(1, EARLY, 1)
+        quant_k("s", 2, 1)
+        rs(1, EARLY, 2)
+        weave("s", 1, 2, S)
+        quant_k("s", 0, 2)
+
+        def rest_of_strip_1(m):
+            qc(1, [m], 1)
+            rs(1, [m], 1)
+            rs(1, [m], 2)
 
         for n in range(1, N_BLOCKS):
             more = n + 1 < N_BLOCKS
-            if n == 1:
+            late = rest_of_strip_1 if n == 1 else (lambda m: whole(n, m))
+            if n > 1:
+                for m in LATE:
+                    store(n - 1, m)
+            for m in EARLY:
+                finish(n, m)
+                store(n, m)
+            late(4)
+            late(5)
+            if more:
+                quant_k("s", 1, n + 1)
                 for g in range(2):
-                    for m in range(6):
-                        pass_qc(n, m, g, m)
-                quant_s(2, 1)
-                for t in range(4):
-                    sort_c(2, t)
-                copy_s(0, 2, S)
+                    turn_c(n + 1, g)
+                weave("s", 2, n + 1, S)
+            finish(n, 4)
+            late(6)
+            finish(n, 5)
+            if more:
+                quant_c(n + 1, 0)
+            late(7)
+            finish(n, 6)
+            if more:
+                quant_c(n + 1, 1)
+                finish(n, 7)
                 for c in range(2):
-                    for m in range(4):
-                        pass_rs(n, m, c)
-                for h in range(2):
-                    for t in (2 * h, 2 * h + 1):
-                        turn_c(2, t, 6 + t % 2)
-                        copy_c(2, t, S)
-                    for m in (2 * h, 2 * h + 1):
-                        pass_rs(n, m, 2)
-                        finish(n, m)
-                    for g in range(2):
-                        quant_c(2, g, h)
-            for m in range(M_TILES):
-                if n > 1 or m > 5:
-                    for g in range(2):
-                        pass_qc(n, m, g, m)
-                if n > 1 or m > 3:
-                    for c in range(3):
-                        pass_rs(n, m, c)
-                if more:
-                    if m == 0 and n == 2:
-                        copy_s(0, n + 1, S)
-                    if m == 2:
-                        copy_s(1, n + 1, S)
-                    if m == 3:
-                        quant_s(0, n + 1)
-                    if m < 4 and n == 2:
-                        sort_c(n + 1, m)
-                    if m == 3 and n == 2:
-                        for t in range(4):
-                            turn_c(n + 1, t, t if t < 3 else 7)
-                            copy_c(n + 1, t, S)
-                if n > 1 or m > 3:
-                    finish(n, m, 2 if m == 7 and not more else 1)
-                if more:
-                    if m == 4:
-                        copy_s(2, n + 1, V + S)
-                        if n == 2:
-                            for h in range(2):
-                                for g in range(2):
-                                    quant_c(n + 1, g, h)
-                    if m == 5:
-                        quant_s(1, n + 1)
-                        quant_s(2, n + 1)
+                    rs(n + 1, EARLY, c)
+                if n + 2 < N_BLOCKS:
+                    weave("s", 0, n + 2, S)
+                    weave("s", 1, n + 2, S)
+                quant_k("s", 2, n + 1)
+                for g in range(2):
+                    qc(n + 1, EARLY, g)
+                if n + 2 < N_BLOCKS:
+                    for h in range(2):
+                        sort("c", 2 * n + 4 + h, V)
+                    quant_k("s", 0, n + 2)
+                rs(n + 1, EARLY, 2)
+        n = N_BLOCKS - 1
+        for m in (4, 5, 6):
+            store(n, m)
+        for lo in (0, 256):
+            finish(n, 7, lo, lo + 256)
+            store(n, 7, lo, lo + 256)

@@ -24,6 +24,10 @@ N_BLOCKS = N // NB
 PAIR = 2 * P
 WORDS = E // 2
 AL = 256
+LHS_CODE_SKIP = 64
+LHS_SCALE_SKIP = 192
+RHS_CODE_SKIP = 0
+RHS_SCALE_SKIP = 128
 
 
 def tile_rocchio_feedback_rescore_s2_kernel(tc, queries, corpus, relevance, sim, gain, prior, out):
@@ -43,10 +47,15 @@ def tile_rocchio_feedback_rescore_s2_kernel(tc, queries, corpus, relevance, sim,
         prior_raw = keep.tile([P, 16], BF16, name="prior_raw")
         prior_words = keep.tile([P, P, 8], F32, name="prior_words")
 
-        q_codes = keep.tile([P, 4, E_PASSES, PAIR], U32, name="q_codes", align_bytes=AL)
-        q_scales = keep.tile([P, 4, E_PASSES, PAIR], U8, name="q_scales", align_bytes=AL)
-        r_codes = keep.tile([P, J_PASSES, M], U32, name="r_codes", align_bytes=AL)
-        r_scales = keep.tile([P, J_PASSES, M], U8, name="r_scales", align_bytes=AL)
+        def shifted(pool, width, dtype, skip, name, bufs=1):
+            lead = skip // 4 if dtype == U32 else skip
+            whole_tile = pool.tile([P, lead + width], dtype, name=name, bufs=bufs, align_bytes=AL)
+            return whole_tile[:, lead:]
+
+        q_codes = shifted(keep, E_PASSES * M, U32, LHS_CODE_SKIP, "q_codes").rearrange("p (a g r) -> p a g r", a=4, g=2)
+        q_scales = shifted(keep, E_PASSES * M, U8, LHS_SCALE_SKIP, "q_scales").rearrange("p (a g r) -> p a g r", a=4, g=2)
+        r_codes = shifted(keep, J_PASSES * M, U32, LHS_CODE_SKIP, "r_codes").rearrange("p (c m) -> p c m", c=J_PASSES)
+        r_scales = shifted(keep, J_PASSES * M, U8, LHS_SCALE_SKIP, "r_scales").rearrange("p (c m) -> p c m", c=J_PASSES)
 
         pair_view = {
             "q": queries.rearrange("(a p t) e -> a p t e", p=P, t=2),
@@ -123,8 +132,8 @@ def tile_rocchio_feedback_rescore_s2_kernel(tc, queries, corpus, relevance, sim,
             else:
                 n, h = divmod(a, 2)
                 if h == 0:
-                    c_codes[n, g] = stage.tile([P, NB], U32, name="c_codes_t", bufs=4, align_bytes=AL)
-                    c_scales[n, g] = stage.tile([P, NB], U8, name="c_scales_t", bufs=4, align_bytes=AL)
+                    c_codes[n, g] = shifted(stage, NB, U32, RHS_CODE_SKIP, "c_codes_t", 4)
+                    c_scales[n, g] = shifted(stage, NB, U8, RHS_SCALE_SKIP, "c_scales_t", 4)
                 cs = slice(h * PAIR, (h + 1) * PAIR)
                 codes, scales = c_codes[n, g][:, cs], c_scales[n, g][:, cs]
             nc.vector.quantize_mx(out=codes.bitcast(E4M3X4), scales=scales, in_=grouped[x, a, g][:])
@@ -149,8 +158,8 @@ def tile_rocchio_feedback_rescore_s2_kernel(tc, queries, corpus, relevance, sim,
                 cs = slice(b * NB, (b + 1) * NB)
                 codes, scales = r_codes[:, c, cs].bitcast(E5M2X4), r_scales[:, c, cs]
             else:
-                s_codes[c, b] = stage.tile([P, NB], U32, name="s_codes_t", bufs=7, align_bytes=AL)
-                s_scales[c, b] = stage.tile([P, NB], U8, name="s_scales_t", bufs=7, align_bytes=AL)
+                s_codes[c, b] = shifted(stage, NB, U32, RHS_CODE_SKIP, "s_codes_t", 7)
+                s_scales[c, b] = shifted(stage, NB, U8, RHS_SCALE_SKIP, "s_scales_t", 7)
                 codes, scales = s_codes[c, b][:].bitcast(E4M3X4), s_scales[c, b][:]
             nc.vector.quantize_mx(out=codes, scales=scales, in_=woven[x, c, b][:].rearrange("p w j -> p (w j)"))
 
@@ -258,72 +267,67 @@ def tile_rocchio_feedback_rescore_s2_kernel(tc, queries, corpus, relevance, sim,
             for h in range(2):
                 quant_pair("c", 2 * n + h, g)
 
-        head_pairs = (("q", 0), ("c", 0), ("c", 1), ("q", 1), ("q", 2), ("q", 3))
+        first_pairs = (("q", 0), ("c", 0), ("c", 1), ("q", 1), ("q", 2), ("q", 3))
         nc.gpsimd.memset(rows[:], 0.0)
         make_identity(nc, ident[:])
         make_identity(nc, ident_bf[:])
         load_prior()
-        for x, a in head_pairs[:3]:
+        for x, a in first_pairs[:3]:
             load_pair(x, a)
         load_gain()
-        for x, a in head_pairs[3:5]:
+        for x, a in first_pairs[3:]:
             load_pair(x, a)
         load_k("r", 0, 0, 2)
-        load_pair("q", 3)
-        for c in range(2):
-            load_k("s", c, 0)
+        load_pair("c", 2)
+        load_pair("c", 3)
+        load_k("s", 0, 0)
+        load_k("s", 1, 0)
         load_k("r", 1, 0, 2)
         load_k("s", 2, 0)
         load_k("r", 2, 0)
         load_k("r", 2, 1)
         load_k("s", 0, 1)
 
-        spread_prior(0, 0, S)
+        spread_prior(0, 0, V)
         spread_prior(1, 1, V)
-        for i, (x, a) in enumerate(head_pairs[:5]):
-            for g in range(2):
-                turn(x, a, g, 2 + (2 * i + g) % 6)
-                drain(x, a, g, V if g == 1 and i < 3 else S)
+        for i, (x, a) in enumerate(first_pairs):
+            turn_pair(x, a, 2 + 2 * i % 6, (S, S))
             if i == 2:
                 spread_gain(0)
             if i > 0:
-                quant_both(*head_pairs[i - 1])
-        quant_both("q", 2)
+                quant_both(*first_pairs[i - 1])
+        quant_both("q", 3)
         for g in range(2):
             qc(0, EARLY, g)
-        weave2("r", 0, 0, 272)
-        weave2("r", 0, 1, 272)
+        weave2("r", 0, 0, 256)
+        weave2("r", 0, 1, 256)
         quant_k("r", 0, 0)
-        weave2("s", 0, 0, 128)
+        turn_pair("c", 2, 4, (S, S))
         quant_k("r", 0, 1)
-        turn_pair("q", 3, 6, (S, S))
-        for g in range(2):
-            qc(0, (4, 5), g)
-        weave("s", 1, 0, V, 272, NB)
+        turn_pair("c", 3, 6, (S, S))
+        weave("s", 0, 0, V)
+        quant_both("c", 2)
         quant_k("s", 0, 0)
-        quant_both("q", 3)
-        weave("s", 1, 0, S, 0, 272)
-        rs(0, range(6), 0)
         for g in range(2):
-            qc(0, (6, 7), g)
-        rs(0, (6, 7), 0)
+            qc(0, LATE, g)
+        rs(0, range(8), 0)
+        weave2("s", 1, 0, 320)
+        quant_both("c", 3)
         quant_k("s", 1, 0)
-        weave2("r", 1, 0, 256)
-        weave2("r", 1, 1, 256)
-        quant_k("r", 1, 0)
-        rs(0, EARLY, 1)
-        weave2("s", 2, 0, 256)
-        quant_k("r", 1, 1)
-        rs(0, LATE, 1)
-        weave2("r", 2, 0, 192)
-        quant_k("s", 2, 0)
+        units = (("r", 1, 0), ("r", 1, 1), ("s", 2, 0), ("r", 2, 0))
+        for i, unit in enumerate(units):
+            weave2(*unit, 240)
+            if i > 0:
+                quant_k(*units[i - 1])
+            if i == 1:
+                rs(0, EARLY, 1)
+            if i == 2:
+                rs(0, LATE, 1)
         quant_k("r", 2, 0)
-        weave2("r", 2, 1, 272)
+        weave2("r", 2, 1, 320)
         rs(0, EARLY, 2)
         quant_k("r", 2, 1)
-        rs(0, (4, 5), 2)
-        load_pair("c", 2)
-        load_pair("c", 3)
+        rs(0, LATE, 2)
         load_k("s", 1, 1)
         load_k("s", 2, 1)
         load_k("s", 0, 2, 2)
@@ -335,27 +339,18 @@ def tile_rocchio_feedback_rescore_s2_kernel(tc, queries, corpus, relevance, sim,
         load_pair("c", 7)
 
         weave("s", 0, 1, S)
-        finish(0, 0)
-        finish(0, 1)
-        turn_pair("c", 2, 0, (S, S))
-        rs(0, (6, 7), 2)
-        finish(0, 2)
-        finish(0, 3)
-        turn_pair("c", 3, 2, (S, S))
-        quant_k("s", 0, 1)
         weave("s", 1, 1, S)
-        for m in LATE:
+        for m in range(M_TILES):
             finish(0, m)
-        rs(1, range(8), 0)
-        quant_c(1, 0)
-        quant_c(1, 1)
+            for g in range(2):
+                qc(1, [m], g)
         weave("s", 2, 1, S)
-        qc(1, range(8), 0)
+        quant_k("s", 0, 1)
+        rs(1, range(8), 0)
         quant_k("s", 1, 1)
-        qc(1, EARLY, 1)
-        weave("s", 0, 2, S)
         for h in range(2):
             sort("c", 4 + h, V)
+        weave("s", 0, 2, S)
         rs(1, EARLY, 1)
         quant_k("s", 2, 1)
         rs(1, EARLY, 2)
@@ -363,7 +358,6 @@ def tile_rocchio_feedback_rescore_s2_kernel(tc, queries, corpus, relevance, sim,
         quant_k("s", 0, 2)
 
         def rest_of_strip_1(m):
-            qc(1, [m], 1)
             rs(1, [m], 1)
             rs(1, [m], 2)
 

@@ -153,15 +153,15 @@ def tile_rocchio_feedback_rescore_s2_kernel(tc, queries, corpus, relevance, sim,
             weave(x, c, b, S, 0, cut)
             weave(x, c, b, V, cut, NB)
 
-        def quant_k(x, c, b):
+        def quant_k(x, c, b, lo=0, hi=NB):
             if x == "r":
-                cs = slice(b * NB, (b + 1) * NB)
+                cs = slice(b * NB + lo, b * NB + hi)
                 codes, scales = r_codes[:, c, cs].bitcast(E5M2X4), r_scales[:, c, cs]
             else:
                 s_codes[c, b] = shifted(stage, NB, U32, RHS_CODE_SKIP, "s_codes_t", 7)
                 s_scales[c, b] = shifted(stage, NB, U8, RHS_SCALE_SKIP, "s_scales_t", 7)
                 codes, scales = s_codes[c, b][:].bitcast(E4M3X4), s_scales[c, b][:]
-            nc.vector.quantize_mx(out=codes, scales=scales, in_=woven[x, c, b][:].rearrange("p w j -> p (w j)"))
+            nc.vector.quantize_mx(out=codes, scales=scales, in_=woven[x, c, b][:, lo:hi, :].rearrange("p w j -> p (w j)"))
 
         acc, done = {}, {}
 
@@ -298,21 +298,22 @@ def tile_rocchio_feedback_rescore_s2_kernel(tc, queries, corpus, relevance, sim,
                 quant_both(*first_pairs[i - 1])
         quant_both("q", 3)
         for g in range(2):
-            qc(0, EARLY, g)
-        weave2("r", 0, 0, 256)
-        weave2("r", 0, 1, 256)
-        quant_k("r", 0, 0)
+            qc(0, (0, 1), g)
+        weave("r", 0, 0, S, 0, 384)
+        weave("r", 0, 1, V)
+        weave("r", 0, 0, V, 384, NB)
         turn_pair("c", 2, 4, (S, S))
         quant_k("r", 0, 1)
+        quant_k("r", 0, 0)
         turn_pair("c", 3, 6, (S, S))
-        weave("s", 0, 0, V)
         quant_both("c", 2)
+        weave2("s", 0, 0, 192)
+        quant_both("c", 3)
+        weave2("s", 1, 0, 256)
         quant_k("s", 0, 0)
         for g in range(2):
-            qc(0, LATE, g)
+            qc(0, range(2, 8), g)
         rs(0, range(8), 0)
-        weave2("s", 1, 0, 320)
-        quant_both("c", 3)
         quant_k("s", 1, 0)
         units = (("r", 1, 0), ("r", 1, 1), ("s", 2, 0), ("r", 2, 0))
         for i, unit in enumerate(units):
@@ -324,9 +325,10 @@ def tile_rocchio_feedback_rescore_s2_kernel(tc, queries, corpus, relevance, sim,
             if i == 2:
                 rs(0, LATE, 1)
         quant_k("r", 2, 0)
-        weave2("r", 2, 1, 320)
+        weave2("r", 2, 1, PAIR)
         rs(0, EARLY, 2)
-        quant_k("r", 2, 1)
+        quant_k("r", 2, 1, 0, PAIR)
+        quant_k("r", 2, 1, PAIR, NB)
         rs(0, LATE, 2)
         load_k("s", 1, 1)
         load_k("s", 2, 1)

@@ -291,7 +291,7 @@ def tile_rocchio_feedback_rescore_s2_kernel(tc, queries, corpus, relevance, sim,
         spread_prior(0, 0, V)
         spread_prior(1, 1, V)
         for i, (x, a) in enumerate(first_pairs):
-            turn_pair(x, a, 2 + 2 * i % 6, (S, S))
+            turn_pair(x, a, 2 + 2 * i % 6, (S, V) if i < 3 else (S, S))
             if i == 2:
                 spread_gain(0)
             if i > 0:
@@ -350,13 +350,12 @@ def tile_rocchio_feedback_rescore_s2_kernel(tc, queries, corpus, relevance, sim,
         quant_k("s", 0, 1)
         rs(1, range(8), 0)
         quant_k("s", 1, 1)
-        for h in range(2):
-            sort("c", 4 + h, V)
         weave("s", 0, 2, S)
         rs(1, EARLY, 1)
         quant_k("s", 2, 1)
+        for h in range(2):
+            sort("c", 4 + h, V)
         rs(1, EARLY, 2)
-        weave("s", 1, 2, S)
         quant_k("s", 0, 2)
 
         def rest_of_strip_1(m):
@@ -375,28 +374,29 @@ def tile_rocchio_feedback_rescore_s2_kernel(tc, queries, corpus, relevance, sim,
             late(4)
             late(5)
             if more:
-                quant_k("s", 1, n + 1)
+                weave("s", 1, n + 1, V)
                 for g in range(2):
                     turn_c(n + 1, g)
                 weave("s", 2, n + 1, S)
+                quant_c(n + 1, 0)
             finish(n, 4)
             late(6)
-            finish(n, 5)
-            if more:
-                quant_c(n + 1, 0)
-            late(7)
-            finish(n, 6)
             if more:
                 quant_c(n + 1, 1)
+            finish(n, 5)
+            late(7)
+            if more:
+                quant_k("s", 1, n + 1)
+            finish(n, 6)
+            if more:
                 finish(n, 7)
-                for c in range(2):
-                    rs(n + 1, EARLY, c)
+                rs(n + 1, EARLY, 0)
                 if n + 2 < N_BLOCKS:
                     weave("s", 0, n + 2, S)
-                    weave("s", 1, n + 2, S)
                 quant_k("s", 2, n + 1)
                 for g in range(2):
                     qc(n + 1, EARLY, g)
+                rs(n + 1, EARLY, 1)
                 if n + 2 < N_BLOCKS:
                     for h in range(2):
                         sort("c", 2 * n + 4 + h, V)

@@ -16,18 +16,20 @@ M, N, E, J = 1024, 2048, 1024, 1536
 FLOPS = 2 * M * N * (E + J)
 
 P = 128
-E_PASSES = 2
-J_PASSES = 3
+E_PASSES = E // 512
+J_PASSES = J // 512
 NB = 512
-M_TILES = M // P
-N_BLOCKS = N // NB
+TILES = range(M // P)
+EARLY, LATE = range(0, 4), range(4, 8)
+STRIPS = N // NB
 PAIR = 2 * P
-WORDS = E // 2
-AL = 256
-LHS_CODE_SKIP = 64
-LHS_SCALE_SKIP = 192
-RHS_CODE_SKIP = 0
-RHS_SCALE_SKIP = 128
+PASS_WORDS = 256
+ALIGN = 256
+
+SHARE_R0 = 384
+SHARE_S0 = 192
+SHARE_S1 = 256
+SHARE_STREAM = 240
 
 
 def tile_rocchio_feedback_rescore_s2_kernel(tc, queries, corpus, relevance, sim, gain, prior, out):
@@ -38,56 +40,53 @@ def tile_rocchio_feedback_rescore_s2_kernel(tc, queries, corpus, relevance, sim,
         stage = ctx.enter_context(tc.tile_pool(name="stage", bufs=1))
         psum = ctx.enter_context(tc.psum_pool(name="psum", bufs=1))
         ctx.enter_context(tc.manual_schedule())
-        V, S = "V", "S"
+        V, S = "vector", "scalar"
 
         ident = keep.tile([P, P], F32, name="ident")
         ident_bf = keep.tile([P, P], BF16, name="ident_bf")
-        rows = keep.tile([P, P], BF16, name="rows")
-        gain_col = keep.tile([P, M_TILES], F32, name="gain_col")
-        prior_raw = keep.tile([P, 16], BF16, name="prior_raw")
-        prior_words = keep.tile([P, P, 8], F32, name="prior_words")
+        gain_rows = keep.tile([P, P], BF16, name="gain_rows")
+        gain_col = keep.tile([P, len(TILES)], F32, name="gain_col")
+        prior_raw = keep.tile([P, N // P], BF16, name="prior_raw")
+        prior_words = keep.tile([P, P, N // PAIR], F32, name="prior_words")
 
-        def shifted(pool, width, dtype, skip, name, bufs=1):
-            lead = skip // 4 if dtype == U32 else skip
-            whole_tile = pool.tile([P, lead + width], dtype, name=name, bufs=bufs, align_bytes=AL)
-            return whole_tile[:, lead:]
+        def operand_tile(pool, width, dtype, name, bufs=1):
+            flat = pool.tile([P, width], dtype, name=name, bufs=bufs, align_bytes=ALIGN)
+            return flat[:]
 
-        q_codes = shifted(keep, E_PASSES * M, U32, LHS_CODE_SKIP, "q_codes").rearrange("p (a g r) -> p a g r", a=4, g=2)
-        q_scales = shifted(keep, E_PASSES * M, U8, LHS_SCALE_SKIP, "q_scales").rearrange("p (a g r) -> p a g r", a=4, g=2)
-        r_codes = shifted(keep, J_PASSES * M, U32, LHS_CODE_SKIP, "r_codes").rearrange("p (c m) -> p c m", c=J_PASSES)
-        r_scales = shifted(keep, J_PASSES * M, U8, LHS_SCALE_SKIP, "r_scales").rearrange("p (c m) -> p c m", c=J_PASSES)
+        by_pair = "p (a g r) -> p a g r"
+        by_pass = "p (c m) -> p c m"
+        q_codes = operand_tile(keep, E_PASSES * M, U32, "q_codes").rearrange(by_pair, g=E_PASSES, r=PAIR)
+        q_scales = operand_tile(keep, E_PASSES * M, U8, "q_scales").rearrange(by_pair, g=E_PASSES, r=PAIR)
+        r_codes = operand_tile(keep, J_PASSES * M, U32, "r_codes").rearrange(by_pass, c=J_PASSES)
+        r_scales = operand_tile(keep, J_PASSES * M, U8, "r_scales").rearrange(by_pass, c=J_PASSES)
 
         pair_view = {
             "q": queries.rearrange("(a p t) e -> a p t e", p=P, t=2),
             "c": corpus.rearrange("(a p t) e -> a p t e", p=P, t=2),
         }
-        r_view = relevance.rearrange("(c p j) m -> c p j m", p=P, j=4)
-        s_view = sim.rearrange("(c p j) n -> c p j n", p=P, j=4)
-
-        pair_raw, k_raw = {}, {}
+        piece_view = {
+            "r": relevance.rearrange("(c p i) m -> c p i m", p=P, i=4),
+            "s": sim.rearrange("(c p i) n -> c p i n", p=P, i=4),
+        }
+        pair_raw, piece_raw = {}, {}
 
         def load_pair(x, a):
-            pair_raw[x, a] = raw.tile([P, 2, E], BF16, name="pair_raw_t", bufs=8, align_bytes=AL)
+            pair_raw[x, a] = raw.tile([P, 2, E], BF16, name="pair_raw_t", bufs=8, align_bytes=ALIGN)
             nc.sync.dma_start(out=pair_raw[x, a][:], in_=pair_view[x][a])
 
-        def load_k(x, c, b, blocks=1):
-            view = r_view if x == "r" else s_view
-            if blocks == 1:
-                rows4 = raw.tile([P, 4, NB], BF16, name="narrow_raw_t", bufs=6, align_bytes=AL)
-            else:
-                rows4 = raw.tile([P, 4, 2 * NB], BF16, name="wide_raw_t", bufs=3, align_bytes=AL)
-            nc.sync.dma_start(out=rows4[:], in_=view[c, :, :, b * NB : (b + blocks) * NB])
-            for i in range(blocks):
-                k_raw[x, c, b + i] = rows4[:, :, i * NB : (i + 1) * NB]
+        def load_piece(x, c, b):
+            piece = raw.tile([P, 4, NB], BF16, name="piece_raw_t", bufs=6, align_bytes=ALIGN)
+            nc.sync.dma_start(out=piece[:], in_=piece_view[x][c, :, :, b * NB : (b + 1) * NB])
+            piece_raw[x, c, b] = piece[:]
 
-        def load_prior():
-            nc.sync.dma_start(out=prior_raw[:], in_=prior.rearrange("(p i) -> p i", p=P))
+        def load_two_pieces(x, c, b):
+            both = raw.tile([P, 4, 2 * NB], BF16, name="two_pieces_raw_t", bufs=3, align_bytes=ALIGN)
+            nc.sync.dma_start(out=both[:], in_=piece_view[x][c, :, :, b * NB : (b + 2) * NB])
+            for h in range(2):
+                piece_raw[x, c, b + h] = both[:, :, h * NB : (h + 1) * NB]
 
-        def load_gain():
-            nc.sync.dma_start(out=rows[0:M_TILES, :], in_=gain.rearrange("(a b) -> a b", b=P))
-
-        def bank_tile(b, shape=(P, NB), dtype=F32):
-            return psum.tile(list(shape), dtype, name="bank_t", tag=f"bank{b}")
+        def bank_tile(bank, shape=(P, NB), dtype=F32):
+            return psum.tile(list(shape), dtype, name="bank_t", tag=f"bank{bank}")
 
         def copy(engine, dst, src):
             if engine == S:
@@ -95,316 +94,295 @@ def tile_rocchio_feedback_rescore_s2_kernel(tc, queries, corpus, relevance, sim,
             else:
                 nc.vector.tensor_copy(out=dst, in_=src)
 
-        pair_sorted, turned, grouped = {}, {}, {}
+        pair_sorted, turned, drained = {}, {}, {}
 
-        def sort(x, a, engine):
-            pair_sorted[x, a] = raw.tile([P, 4, 2, P], F32, name="sorted_t", bufs=2, align_bytes=AL)
-            copy(
-                engine,
-                pair_sorted[x, a][:],
-                pair_raw[x, a][:].rearrange("p t e -> p (t e)").bitcast(F32).rearrange("p (s w u) -> p s u w", s=4, u=2),
-            )
+        def sort(a):
+            pair_sorted["c", a] = raw.tile([P, 4, 2, P], F32, name="sorted_t", bufs=2, align_bytes=ALIGN)
+            words = pair_raw["c", a][:].rearrange("p t e -> p (t e)").bitcast(F32)
+            nc.vector.tensor_copy(out=pair_sorted["c", a][:], in_=words.rearrange("p (s w u) -> p s u w", s=4, u=2))
 
-        def turn(x, a, g, b):
-            turned[x, a, g] = bank_tile(b)
+        def turn(x, a, g, bank, engine):
+            turned[x, a, g] = bank_tile(bank)
             for t in range(2):
                 for u in range(2):
                     if (x, a) in pair_sorted:
-                        src = pair_sorted[x, a][:, 2 * t + g, u, :]
+                        words = pair_sorted[x, a][:, E_PASSES * t + g, u, :]
                     else:
-                        src = pair_raw[x, a][:, t, :].bitcast(F32)[:, 256 * g + u : 256 * (g + 1) : 2]
-                    s = 2 * t + u
-                    nc.tensor.transpose(turned[x, a, g][:, s * P : (s + 1) * P], src, ident[:])
-
-        def drain(x, a, g, engine):
-            grouped[x, a, g] = stage.tile([P, PAIR * 4], BF16, name="turned_grp_t", bufs=6, align_bytes=AL)
+                        words = pair_raw[x, a][:, t, :].bitcast(F32)[:, PASS_WORDS * g + u : PASS_WORDS * (g + 1) : 2]
+                    slot = 2 * t + u
+                    nc.tensor.transpose(turned[x, a, g][:, slot * P : (slot + 1) * P], words, ident[:])
+            drained[x, a, g] = stage.tile([P, PAIR * 4], BF16, name="drained_t", bufs=6, align_bytes=ALIGN)
             copy(
                 engine,
-                grouped[x, a, g][:].bitcast(F32).rearrange("p (r s) -> p r s", s=4),
+                drained[x, a, g][:].bitcast(F32).rearrange("p (r s) -> p r s", s=4),
                 turned[x, a, g][:].rearrange("p (s r) -> p r s", s=4),
             )
 
+        def turn_pair(x, a, bank, engines=(S, S)):
+            for g in range(E_PASSES):
+                turn(x, a, g, bank + g, engines[g])
+
         c_codes, c_scales, s_codes, s_scales = {}, {}, {}, {}
 
-        def quant_pair(x, a, g):
+        def quant_turned(x, a, g):
             if x == "q":
                 codes, scales = q_codes[:, a, g, :], q_scales[:, a, g, :]
             else:
                 n, h = divmod(a, 2)
                 if h == 0:
-                    c_codes[n, g] = shifted(stage, NB, U32, RHS_CODE_SKIP, "c_codes_t", 4)
-                    c_scales[n, g] = shifted(stage, NB, U8, RHS_SCALE_SKIP, "c_scales_t", 4)
-                cs = slice(h * PAIR, (h + 1) * PAIR)
-                codes, scales = c_codes[n, g][:, cs], c_scales[n, g][:, cs]
-            nc.vector.quantize_mx(out=codes.bitcast(E4M3X4), scales=scales, in_=grouped[x, a, g][:])
+                    c_codes[n, g] = operand_tile(stage, NB, U32, "c_codes_t", 4)
+                    c_scales[n, g] = operand_tile(stage, NB, U8, "c_scales_t", 4)
+                cols = slice(h * PAIR, (h + 1) * PAIR)
+                codes, scales = c_codes[n, g][:, cols], c_scales[n, g][:, cols]
+            nc.vector.quantize_mx(out=codes.bitcast(E4M3X4), scales=scales, in_=drained[x, a, g][:])
+
+        def quant_pair(x, a):
+            for g in range(E_PASSES):
+                quant_turned(x, a, g)
+
+        def quant_corpus(n, g):
+            for h in range(2):
+                quant_turned("c", 2 * n + h, g)
 
         woven = {}
 
         def weave(x, c, b, engine, lo=0, hi=NB):
             if (x, c, b) not in woven:
-                woven[x, c, b] = stage.tile([P, NB, 4], BF16, name="woven_t", bufs=5, align_bytes=AL)
+                woven[x, c, b] = stage.tile([P, NB, 4], BF16, name="woven_t", bufs=5, align_bytes=ALIGN)
             copy(
                 engine,
-                woven[x, c, b][:, lo:hi, :].rearrange("p (w i) j -> p w j i", i=4),
-                k_raw[x, c, b][:, :, lo:hi].rearrange("p j (w i) -> p w j i", i=4),
+                woven[x, c, b][:, lo:hi, :].rearrange("p (w j) i -> p w i j", j=4),
+                piece_raw[x, c, b][:, :, lo:hi].rearrange("p i (w j) -> p w i j", j=4),
             )
 
-        def weave2(x, c, b, cut):
-            weave(x, c, b, S, 0, cut)
-            weave(x, c, b, V, cut, NB)
+        def weave_shared(x, c, b, share):
+            weave(x, c, b, S, 0, share)
+            weave(x, c, b, V, share, NB)
 
-        def quant_k(x, c, b, lo=0, hi=NB):
+        def quant_piece(x, c, b, lo=0, hi=NB):
             if x == "r":
-                cs = slice(b * NB + lo, b * NB + hi)
-                codes, scales = r_codes[:, c, cs].bitcast(E5M2X4), r_scales[:, c, cs]
+                cols = slice(b * NB + lo, b * NB + hi)
+                codes, scales = r_codes[:, c, cols].bitcast(E5M2X4), r_scales[:, c, cols]
             else:
-                s_codes[c, b] = shifted(stage, NB, U32, RHS_CODE_SKIP, "s_codes_t", 7)
-                s_scales[c, b] = shifted(stage, NB, U8, RHS_SCALE_SKIP, "s_scales_t", 7)
-                codes, scales = s_codes[c, b][:].bitcast(E4M3X4), s_scales[c, b][:]
-            nc.vector.quantize_mx(out=codes, scales=scales, in_=woven[x, c, b][:, lo:hi, :].rearrange("p w j -> p (w j)"))
+                s_codes[c, b] = operand_tile(stage, NB, U32, "s_codes_t", 7)
+                s_scales[c, b] = operand_tile(stage, NB, U8, "s_scales_t", 7)
+                codes, scales = s_codes[c, b].bitcast(E4M3X4), s_scales[c, b]
+            nc.vector.quantize_mx(out=codes, scales=scales, in_=woven[x, c, b][:, lo:hi, :].rearrange("p w i -> p (w i)"))
 
-        acc, done = {}, {}
+        acc, passes_done = {}, {}
 
         def mx_pass(n, m, lhsT, lhsT_scale, rhs, rhs_scale):
             if (n, m) not in acc:
-                acc[n, m] = bank_tile(acc_bank(n, m))
-                done[n, m] = 0
-            done[n, m] = done[n, m] + 1
+                acc[n, m] = bank_tile(m)
+                passes_done[n, m] = 0
+            passes_done[n, m] = passes_done[n, m] + 1
             nc.tensor.matmul_mx(
                 out=acc[n, m][:],
                 lhsT=lhsT,
                 lhsT_scale=lhsT_scale,
                 rhs=rhs,
                 rhs_scale=rhs_scale,
-                start=(done[n, m] == 1),
-                stop=(done[n, m] == E_PASSES + J_PASSES),
+                start=(passes_done[n, m] == 1),
+                stop=(passes_done[n, m] == E_PASSES + J_PASSES),
             )
 
-        def qc(n, tiles, g):
+        def qc_pass(n, tiles, g):
             for m in tiles:
-                cs = slice((m % 2) * P, (m % 2 + 1) * P)
+                a, h = divmod(m, 2)
+                cols = slice(h * P, (h + 1) * P)
                 mx_pass(
-                    n, m, q_codes[:, m // 2, g, cs].bitcast(E4M3X4), q_scales[:, m // 2, g, cs],
-                    c_codes[n, g][:].bitcast(E4M3X4), c_scales[n, g][:],
+                    n, m, q_codes[:, a, g, cols].bitcast(E4M3X4), q_scales[:, a, g, cols],
+                    c_codes[n, g].bitcast(E4M3X4), c_scales[n, g],
                 )
 
-        def rs(n, tiles, c):
-            for m in tiles:
-                cs = slice(m * P, (m + 1) * P)
-                mx_pass(
-                    n, m, r_codes[:, c, cs].bitcast(E5M2X4), r_scales[:, c, cs],
-                    s_codes[c, n][:].bitcast(E4M3X4), s_scales[c, n][:],
-                )
-
-        def whole(n, m):
+        def qc_passes(n, tiles):
             for g in range(E_PASSES):
-                qc(n, [m], g)
-            for c in range(J_PASSES):
-                rs(n, [m], c)
+                qc_pass(n, tiles, g)
 
-        def spread_gain(b):
-            bank = bank_tile(b, (P, P), BF16)
-            nc.tensor.transpose(bank[:], rows[:], ident_bf[:])
-            nc.vector.tensor_copy(out=gain_col[:], in_=bank[:, 0:M_TILES])
+        def rs_pass(n, tiles, c):
+            for m in tiles:
+                cols = slice(m * P, (m + 1) * P)
+                mx_pass(
+                    n, m, r_codes[:, c, cols].bitcast(E5M2X4), r_scales[:, c, cols],
+                    s_codes[c, n].bitcast(E4M3X4), s_scales[c, n],
+                )
 
-        def spread_prior(h, b, engine):
-            bank = bank_tile(b)
+        def close_late_tile(n, m):
+            if n > 1:
+                qc_passes(n, [m])
+            for c in range(0 if n > 1 else 1, J_PASSES):
+                rs_pass(n, [m], c)
+
+        def spread_gain(bank):
+            columns = bank_tile(bank, (P, P), BF16)
+            nc.tensor.transpose(columns[:], gain_rows[:], ident_bf[:])
+            nc.vector.tensor_copy(out=gain_col[:], in_=columns[:, 0 : len(TILES)])
+
+        def spread_prior(h, bank):
+            spread = bank_tile(bank)
             words = prior_raw[:].bitcast(F32)
             for i in range(4):
-                col = words[:, 4 * h + i : 4 * h + i + 1]
-                nc.tensor.transpose(bank[:, i * P : (i + 1) * P], col.to_broadcast([P, P]), ident[:])
-            copy(engine, prior_words[:, :, 4 * h : 4 * h + 4], bank[:].rearrange("p (i w) -> p w i", i=4))
+                column = words[:, 4 * h + i : 4 * h + i + 1]
+                nc.tensor.transpose(spread[:, i * P : (i + 1) * P], column.to_broadcast([P, P]), ident[:])
+            nc.vector.tensor_copy(out=prior_words[:, :, 4 * h : 4 * h + 4], in_=spread[:].rearrange("p (i w) -> p w i", i=4))
 
-        prior_bc = prior_words[:].rearrange("p w i -> p (w i)").bitcast(BF16)
+        prior_all = prior_words[:].rearrange("p w i -> p (w i)").bitcast(BF16)
 
-        res = {}
+        result, result_01 = {}, {}
 
         def finish(n, m, lo=0, hi=NB):
             if n == 0:
-                both = stage.tile([P, 2 * NB], F32, name="res_pair_t", bufs=M_TILES)
-                res[0, m], res[1, m], res["pair", m] = both[:, :NB], both[:, NB:], both[:]
+                result_01[m] = stage.tile([P, 2 * NB], F32, name="result_01_t", bufs=len(TILES))
+                result[0, m], result[1, m] = result_01[m][:, :NB], result_01[m][:, NB:]
             elif n > 1 and lo == 0:
-                one = stage.tile([P, NB], F32, name="res_t", bufs=RES_BUFS)
-                res[n, m] = one[:]
+                single = stage.tile([P, NB], F32, name="result_t", bufs=len(TILES))
+                result[n, m] = single[:]
             nc.vector.scalar_tensor_tensor(
-                out=res[n, m][:, lo:hi],
+                out=result[n, m][:, lo:hi],
                 in0=acc[n, m][:, lo:hi],
                 scalar=gain_col[:, m : m + 1],
-                in1=prior_bc[:, n * NB + lo : n * NB + hi],
+                in1=prior_all[:, n * NB + lo : n * NB + hi],
                 op0=MULT,
                 op1=ADD,
             )
 
         def store(n, m, lo=0, hi=NB):
+            rows = slice(m * P, (m + 1) * P)
             if n == 1:
-                nc.sync.dma_start(out=out[m * P : (m + 1) * P, : 2 * NB], in_=res["pair", m])
+                nc.sync.dma_start(out=out[rows, : 2 * NB], in_=result_01[m][:])
             else:
-                nc.sync.dma_start(out=out[m * P : (m + 1) * P, n * NB + lo : n * NB + hi], in_=res[n, m][:, lo:hi])
-
-
-        RES_BUFS = 8
-        EARLY, LATE = range(0, 4), range(4, 8)
-        FIRST = range(6)
-
-        def acc_bank(n, m):
-            return m
-
-        def turn_pair(x, a, b, engines):
-            for g in range(2):
-                turn(x, a, g, b + g)
-                drain(x, a, g, engines[g])
-
-        def quant_both(x, a):
-            for g in range(2):
-                quant_pair(x, a, g)
-
-        def turn_c(n, g):
-            for h in range(2):
-                turn("c", 2 * n + h, g, 2 * g + h)
-                drain("c", 2 * n + h, g, S)
-
-        def quant_c(n, g):
-            for h in range(2):
-                quant_pair("c", 2 * n + h, g)
+                nc.sync.dma_start(out=out[rows, n * NB + lo : n * NB + hi], in_=result[n, m][:, lo:hi])
 
         first_pairs = (("q", 0), ("c", 0), ("c", 1), ("q", 1), ("q", 2), ("q", 3))
-        nc.gpsimd.memset(rows[:], 0.0)
+        nc.gpsimd.memset(gain_rows[:], 0.0)
         make_identity(nc, ident[:])
         make_identity(nc, ident_bf[:])
-        load_prior()
+        nc.sync.dma_start(out=prior_raw[:], in_=prior.rearrange("(p i) -> p i", p=P))
         for x, a in first_pairs[:3]:
             load_pair(x, a)
-        load_gain()
+        nc.sync.dma_start(out=gain_rows[0 : len(TILES), :], in_=gain.rearrange("(m p) -> m p", p=P))
         for x, a in first_pairs[3:]:
             load_pair(x, a)
-        load_k("r", 0, 0, 2)
+        load_two_pieces("r", 0, 0)
         load_pair("c", 2)
         load_pair("c", 3)
-        load_k("s", 0, 0)
-        load_k("s", 1, 0)
-        load_k("r", 1, 0, 2)
-        load_k("s", 2, 0)
-        load_k("r", 2, 0)
-        load_k("r", 2, 1)
-        load_k("s", 0, 1)
+        load_piece("s", 0, 0)
+        load_piece("s", 1, 0)
+        load_two_pieces("r", 1, 0)
+        load_piece("s", 2, 0)
+        load_piece("r", 2, 0)
+        load_piece("r", 2, 1)
+        load_piece("s", 0, 1)
 
-        spread_prior(0, 0, V)
-        spread_prior(1, 1, V)
+        for h in range(2):
+            spread_prior(h, h)
         for i, (x, a) in enumerate(first_pairs):
-            turn_pair(x, a, 2 + 2 * i % 6, (S, V) if i < 3 else (S, S))
+            turn_pair(x, a, 2 + 2 * (i % 3), (S, V) if i < 3 else (S, S))
             if i == 2:
                 spread_gain(0)
             if i > 0:
-                quant_both(*first_pairs[i - 1])
-        quant_both("q", 3)
-        for g in range(2):
-            qc(0, (0, 1), g)
-        weave("r", 0, 0, S, 0, 384)
+                quant_pair(*first_pairs[i - 1])
+        quant_pair(*first_pairs[-1])
+        qc_passes(0, TILES[:2])
+        weave("r", 0, 0, S, 0, SHARE_R0)
         weave("r", 0, 1, V)
-        weave("r", 0, 0, V, 384, NB)
-        turn_pair("c", 2, 4, (S, S))
-        quant_k("r", 0, 1)
-        quant_k("r", 0, 0)
-        turn_pair("c", 3, 6, (S, S))
-        quant_both("c", 2)
-        weave2("s", 0, 0, 192)
-        quant_both("c", 3)
-        weave2("s", 1, 0, 256)
-        quant_k("s", 0, 0)
-        for g in range(2):
-            qc(0, range(2, 8), g)
-        rs(0, range(8), 0)
-        quant_k("s", 1, 0)
-        units = (("r", 1, 0), ("r", 1, 1), ("s", 2, 0), ("r", 2, 0))
-        for i, unit in enumerate(units):
-            weave2(*unit, 240)
-            if i > 0:
-                quant_k(*units[i - 1])
-            if i == 1:
-                rs(0, EARLY, 1)
-            if i == 2:
-                rs(0, LATE, 1)
-        quant_k("r", 2, 0)
-        weave2("r", 2, 1, PAIR)
-        rs(0, EARLY, 2)
-        quant_k("r", 2, 1, 0, PAIR)
-        quant_k("r", 2, 1, PAIR, NB)
-        rs(0, LATE, 2)
-        load_k("s", 1, 1)
-        load_k("s", 2, 1)
-        load_k("s", 0, 2, 2)
+        weave("r", 0, 0, V, SHARE_R0, NB)
+        turn_pair("c", 2, LATE[0])
+        quant_piece("r", 0, 1)
+        quant_piece("r", 0, 0)
+        turn_pair("c", 3, LATE[2])
+        quant_pair("c", 2)
+        weave_shared("s", 0, 0, SHARE_S0)
+        quant_pair("c", 3)
+        weave_shared("s", 1, 0, SHARE_S1)
+        quant_piece("s", 0, 0)
+        qc_passes(0, TILES[2:])
+        rs_pass(0, TILES, 0)
+        quant_piece("s", 1, 0)
+        weave_shared("r", 1, 0, SHARE_STREAM)
+        weave_shared("r", 1, 1, SHARE_STREAM)
+        quant_piece("r", 1, 0)
+        rs_pass(0, EARLY, 1)
+        weave_shared("s", 2, 0, SHARE_STREAM)
+        quant_piece("r", 1, 1)
+        rs_pass(0, LATE, 1)
+        weave_shared("r", 2, 0, SHARE_STREAM)
+        quant_piece("s", 2, 0)
+        quant_piece("r", 2, 0)
+        weave_shared("r", 2, 1, PAIR)
+        rs_pass(0, EARLY, 2)
+        quant_piece("r", 2, 1, 0, PAIR)
+        quant_piece("r", 2, 1, PAIR, NB)
+        rs_pass(0, LATE, 2)
+
+        load_piece("s", 1, 1)
+        load_piece("s", 2, 1)
+        load_two_pieces("s", 0, 2)
         load_pair("c", 4)
         load_pair("c", 5)
-        load_k("s", 1, 2, 2)
-        load_k("s", 2, 2, 2)
+        load_two_pieces("s", 1, 2)
+        load_two_pieces("s", 2, 2)
         load_pair("c", 6)
         load_pair("c", 7)
 
         weave("s", 0, 1, S)
         weave("s", 1, 1, S)
-        for m in range(M_TILES):
+        for m in TILES:
             finish(0, m)
-            for g in range(2):
-                qc(1, [m], g)
+            qc_passes(1, [m])
         weave("s", 2, 1, S)
-        quant_k("s", 0, 1)
-        rs(1, range(8), 0)
-        quant_k("s", 1, 1)
+        quant_piece("s", 0, 1)
+        rs_pass(1, TILES, 0)
+        quant_piece("s", 1, 1)
         weave("s", 0, 2, S)
-        rs(1, EARLY, 1)
-        quant_k("s", 2, 1)
+        rs_pass(1, EARLY, 1)
+        quant_piece("s", 2, 1)
         for h in range(2):
-            sort("c", 4 + h, V)
-        rs(1, EARLY, 2)
-        quant_k("s", 0, 2)
+            sort(4 + h)
+        rs_pass(1, EARLY, 2)
+        quant_piece("s", 0, 2)
 
-        def rest_of_strip_1(m):
-            rs(1, [m], 1)
-            rs(1, [m], 2)
-
-        for n in range(1, N_BLOCKS):
-            more = n + 1 < N_BLOCKS
-            late = rest_of_strip_1 if n == 1 else (lambda m: whole(n, m))
+        last = STRIPS - 1
+        for n in range(1, STRIPS):
             if n > 1:
                 for m in LATE:
                     store(n - 1, m)
             for m in EARLY:
                 finish(n, m)
                 store(n, m)
-            late(4)
-            late(5)
-            if more:
+            close_late_tile(n, LATE[0])
+            close_late_tile(n, LATE[1])
+            if n < last:
                 weave("s", 1, n + 1, V)
-                for g in range(2):
-                    turn_c(n + 1, g)
-                weave("s", 2, n + 1, S)
-                quant_c(n + 1, 0)
-            finish(n, 4)
-            late(6)
-            if more:
-                quant_c(n + 1, 1)
-            finish(n, 5)
-            late(7)
-            if more:
-                quant_k("s", 1, n + 1)
-            finish(n, 6)
-            if more:
-                finish(n, 7)
-                rs(n + 1, EARLY, 0)
-                if n + 2 < N_BLOCKS:
-                    weave("s", 0, n + 2, S)
-                quant_k("s", 2, n + 1)
-                for g in range(2):
-                    qc(n + 1, EARLY, g)
-                rs(n + 1, EARLY, 1)
-                if n + 2 < N_BLOCKS:
+                for g in range(E_PASSES):
                     for h in range(2):
-                        sort("c", 2 * n + 4 + h, V)
-                    quant_k("s", 0, n + 2)
-                rs(n + 1, EARLY, 2)
-        n = N_BLOCKS - 1
-        for m in (4, 5, 6):
-            store(n, m)
-        for lo in (0, 256):
-            finish(n, 7, lo, lo + 256)
-            store(n, 7, lo, lo + 256)
+                        turn("c", 2 * (n + 1) + h, g, EARLY[2 * g + h], S)
+                weave("s", 2, n + 1, S)
+                quant_corpus(n + 1, 0)
+            finish(n, LATE[0])
+            close_late_tile(n, LATE[2])
+            if n < last:
+                quant_corpus(n + 1, 1)
+            finish(n, LATE[1])
+            close_late_tile(n, LATE[3])
+            if n < last:
+                quant_piece("s", 1, n + 1)
+            finish(n, LATE[2])
+            if n < last:
+                finish(n, LATE[3])
+                rs_pass(n + 1, EARLY, 0)
+                if n + 1 < last:
+                    weave("s", 0, n + 2, S)
+                quant_piece("s", 2, n + 1)
+                qc_passes(n + 1, EARLY)
+                rs_pass(n + 1, EARLY, 1)
+                if n + 1 < last:
+                    for h in range(2):
+                        sort(2 * (n + 2) + h)
+                    quant_piece("s", 0, n + 2)
+                rs_pass(n + 1, EARLY, 2)
+        for m in LATE[:3]:
+            store(last, m)
+        for lo in (0, PAIR):
+            finish(last, LATE[3], lo, lo + PAIR)
+            store(last, LATE[3], lo, lo + PAIR)

@@ -11,6 +11,7 @@ E4M3X4 = mybir.dt.float8_e4m3fn_x4
 E5M2X4 = mybir.dt.float8_e5m2_x4
 MULT = mybir.AluOpType.mult
 ADD = mybir.AluOpType.add
+COPY = mybir.ActivationFunctionType.Copy
 
 M, N, E, J = 1024, 2048, 1024, 1536
 FLOPS = 2 * M * N * (E + J)
@@ -237,6 +238,9 @@ def tile_rocchio_feedback_rescore_s2_kernel(tc, queries, corpus, relevance, sim,
             elif n > 1 and lo == 0:
                 single = stage.tile([P, NB], F32, name="result_t", bufs=len(TILES))
                 result[n, m] = single[:]
+            if n == 0 and m % 2 == 1:
+                nc.scalar.activation(out=result[n, m], in_=acc[n, m][:], func=COPY, scale=gain_col[:, m : m + 1])
+                return
             nc.vector.scalar_tensor_tensor(
                 out=result[n, m][:, lo:hi],
                 in0=acc[n, m][:, lo:hi],
@@ -245,6 +249,9 @@ def tile_rocchio_feedback_rescore_s2_kernel(tc, queries, corpus, relevance, sim,
                 op0=MULT,
                 op1=ADD,
             )
+
+        def add_prior(m):
+            nc.vector.tensor_tensor(out=result[0, m], in0=result[0, m], in1=prior_all[:, :NB], op=ADD)
 
         def store(n, m, lo=0, hi=NB):
             rows = slice(m * P, (m + 1) * P)
@@ -325,18 +332,23 @@ def tile_rocchio_feedback_rescore_s2_kernel(tc, queries, corpus, relevance, sim,
         load_pair("c", 6)
         load_pair("c", 7)
 
-        weave("s", 0, 1, S)
-        weave("s", 1, 1, S)
         for m in TILES:
+            if m % 2 == 1:
+                weave("s", 0, 1, S, (m // 2) * P, (m // 2 + 1) * P)
             finish(0, m)
             qc_passes(1, [m])
-        weave("s", 2, 1, S)
+        weave("s", 1, 1, S)
+        weave("s", 2, 1, V)
         quant_piece("s", 0, 1)
         rs_pass(1, TILES, 0)
-        quant_piece("s", 1, 1)
-        weave("s", 0, 2, S)
-        rs_pass(1, EARLY, 1)
         quant_piece("s", 2, 1)
+        weave("s", 0, 2, S)
+        for m in EARLY[1::2]:
+            add_prior(m)
+        quant_piece("s", 1, 1)
+        for m in LATE[1::2]:
+            add_prior(m)
+        rs_pass(1, EARLY, 1)
         for h in range(2):
             sort(4 + h)
         rs_pass(1, EARLY, 2)

@@ -97,10 +97,10 @@ def tile_rocchio_feedback_rescore_s2_kernel(tc, queries, corpus, relevance, sim,
 
         pair_sorted, turned, drained = {}, {}, {}
 
-        def sort(a):
-            pair_sorted["c", a] = raw.tile([P, 4, 2, P], F32, name="sorted_t", bufs=2, align_bytes=ALIGN)
-            words = pair_raw["c", a][:].rearrange("p t e -> p (t e)").bitcast(F32)
-            nc.vector.tensor_copy(out=pair_sorted["c", a][:], in_=words.rearrange("p (s w u) -> p s u w", s=4, u=2))
+        def sort(x, a, engine=V):
+            pair_sorted[x, a] = raw.tile([P, 4, 2, P], F32, name="sorted_t", bufs=2, align_bytes=ALIGN)
+            words = pair_raw[x, a][:].rearrange("p t e -> p (t e)").bitcast(F32)
+            copy(engine, pair_sorted[x, a][:], words.rearrange("p (s w u) -> p s u w", s=4, u=2))
 
         def turn(x, a, g, bank, engine):
             turned[x, a, g] = bank_tile(bank)
@@ -260,67 +260,91 @@ def tile_rocchio_feedback_rescore_s2_kernel(tc, queries, corpus, relevance, sim,
             else:
                 nc.sync.dma_start(out=out[rows, n * NB + lo : n * NB + hi], in_=result[n, m][:, lo:hi])
 
-        first_pairs = (("q", 0), ("c", 0), ("c", 1), ("q", 1), ("q", 2), ("q", 3))
-        nc.gpsimd.memset(gain_rows[:], 0.0)
         make_identity(nc, ident[:])
+        nc.gpsimd.memset(gain_rows[:], 0.0)
         make_identity(nc, ident_bf[:])
         nc.sync.dma_start(out=prior_raw[:], in_=prior.rearrange("(p i) -> p i", p=P))
-        for x, a in first_pairs[:3]:
-            load_pair(x, a)
+        load_pair("c", 0)
+        load_pair("c", 1)
+        load_pair("q", 0)
         nc.sync.dma_start(out=gain_rows[0 : len(TILES), :], in_=gain.rearrange("(m p) -> m p", p=P))
-        for x, a in first_pairs[3:]:
-            load_pair(x, a)
-        load_two_pieces("r", 0, 0)
-        load_pair("c", 2)
-        load_pair("c", 3)
+        load_pair("q", 1)
         load_piece("s", 0, 0)
+        load_pair("q", 2)
+        load_piece("r", 0, 0)
+        load_pair("q", 3)
+        load_piece("r", 0, 1)
+        load_pair("c", 2)
         load_piece("s", 1, 0)
-        load_two_pieces("r", 1, 0)
-        load_piece("s", 2, 0)
-        load_piece("r", 2, 0)
-        load_piece("r", 2, 1)
-        load_piece("s", 0, 1)
-
+        load_pair("c", 3)
+        load_piece("r", 1, 0)
+        load_piece("r", 1, 1)
         for h in range(2):
             spread_prior(h, h)
-        for i, (x, a) in enumerate(first_pairs):
-            turn_pair(x, a, 2 + 2 * (i % 3), (S, V) if i < 3 else (S, S))
-            if i == 2:
-                spread_gain(0)
-            if i > 0:
-                quant_pair(*first_pairs[i - 1])
-        quant_pair(*first_pairs[-1])
-        qc_passes(0, TILES[:2])
-        weave("r", 0, 0, S, 0, SHARE_R0)
-        weave("r", 0, 1, V)
-        weave("r", 0, 0, V, SHARE_R0, NB)
-        turn_pair("c", 2, LATE[0])
-        quant_piece("r", 0, 1)
-        quant_piece("r", 0, 0)
-        turn_pair("c", 3, LATE[2])
-        quant_pair("c", 2)
-        weave_shared("s", 0, 0, SHARE_S0)
-        quant_pair("c", 3)
-        weave_shared("s", 1, 0, SHARE_S1)
+        turn_pair("c", 0, 2, (S, V))
+        turn_pair("c", 1, 4, (S, S))
+        quant_pair("c", 0)
+        turn_pair("q", 0, 6, (S, S))
+        quant_pair("c", 1)
+        spread_gain(0)
+        turn_pair("q", 1, 2)
+        quant_pair("q", 0)
+        qc_passes(0, TILES[0:2])
+        weave("s", 0, 0, V, 192, NB)
+        quant_pair("q", 1)
+        weave("s", 0, 0, S, 0, 192)
+        sort("q", 2)
+        qc_passes(0, TILES[2:4])
         quant_piece("s", 0, 0)
-        qc_passes(0, TILES[2:])
-        rs_pass(0, TILES, 0)
+        load_piece("s", 2, 0)
+        weave("r", 0, 0, S, 0, 224)
+        weave("r", 0, 0, V, 224, NB)
+        sort("q", 3)
+        turn_pair("q", 2, 4)
+        turn_pair("q", 3, 6)
+        quant_piece("r", 0, 0)
+        load_piece("r", 2, 0)
+        rs_pass(0, EARLY, 0)
+        weave("r", 0, 1, V, 128, NB)
+        quant_pair("q", 2)
+        weave("r", 0, 1, S, 0, 128)
+        turn_pair("c", 2, 6)
+        quant_pair("q", 3)
+        qc_passes(0, TILES[4:6])
+        weave("s", 1, 0, V, 128, NB)
+        quant_piece("r", 0, 1)
+        load_piece("r", 2, 1)
+        weave("s", 1, 0, S, 0, 128)
+        quant_pair("c", 2)
         quant_piece("s", 1, 0)
-        weave_shared("r", 1, 0, SHARE_STREAM)
-        weave_shared("r", 1, 1, SHARE_STREAM)
+        weave_shared("r", 1, 0, 96)
+        turn_pair("c", 3, 6)
+        load_piece("s", 0, 1)
+        rs_pass(0, TILES[4:6], 0)
+        weave_shared("r", 1, 1, 224)
         quant_piece("r", 1, 0)
+        qc_passes(0, TILES[6:8])
+        rs_pass(0, TILES[6:8], 0)
         rs_pass(0, EARLY, 1)
-        weave_shared("s", 2, 0, SHARE_STREAM)
+        weave_shared("s", 2, 0, 256)
         quant_piece("r", 1, 1)
         rs_pass(0, LATE, 1)
-        weave_shared("r", 2, 0, SHARE_STREAM)
+        weave("r", 2, 0, S, 0, PAIR)
+
+        weave("r", 2, 0, V, PAIR, NB)
         quant_piece("s", 2, 0)
-        quant_piece("r", 2, 0)
-        weave_shared("r", 2, 1, PAIR)
-        rs_pass(0, EARLY, 2)
-        quant_piece("r", 2, 1, 0, PAIR)
+        weave("r", 2, 1, S, 0, PAIR)
+        quant_piece("r", 2, 0, PAIR, NB)
+        rs_pass(0, TILES[2:4], 2)
+        quant_piece("r", 2, 0, 0, PAIR)
+        rs_pass(0, TILES[0:2], 2)
+        weave("r", 2, 1, V, PAIR, NB)
+        quant_turned("c", 3, 0)
         quant_piece("r", 2, 1, PAIR, NB)
-        rs_pass(0, LATE, 2)
+        rs_pass(0, TILES[6:8], 2)
+        quant_piece("r", 2, 1, 0, PAIR)
+        rs_pass(0, TILES[4:6], 2)
+        quant_turned("c", 3, 1)
 
         load_piece("s", 1, 1)
         load_piece("s", 2, 1)
@@ -350,9 +374,8 @@ def tile_rocchio_feedback_rescore_s2_kernel(tc, queries, corpus, relevance, sim,
             add_prior(m)
         rs_pass(1, EARLY, 1)
         for h in range(2):
-            sort(4 + h)
+            sort("c", 4 + h)
         rs_pass(1, EARLY, 2)
-        quant_piece("s", 0, 2)
 
         last = STRIPS - 1
         for n in range(1, STRIPS):
@@ -365,7 +388,8 @@ def tile_rocchio_feedback_rescore_s2_kernel(tc, queries, corpus, relevance, sim,
             close_late_tile(n, LATE[0])
             close_late_tile(n, LATE[1])
             if n < last:
-                weave("s", 1, n + 1, V)
+                weave("s", 1, n + 1, S)
+                quant_piece("s", 0, n + 1)
                 for g in range(E_PASSES):
                     for h in range(2):
                         turn("c", 2 * (n + 1) + h, g, EARLY[2 * g + h], S)
@@ -390,8 +414,7 @@ def tile_rocchio_feedback_rescore_s2_kernel(tc, queries, corpus, relevance, sim,
                 rs_pass(n + 1, EARLY, 1)
                 if n + 1 < last:
                     for h in range(2):
-                        sort(2 * (n + 2) + h)
-                    quant_piece("s", 0, n + 2)
+                        sort("c", 2 * (n + 2) + h)
                 rs_pass(n + 1, EARLY, 2)
         for m in LATE[:3]:
             store(last, m)

@@ -25,6 +25,7 @@ EARLY, LATE = range(0, 4), range(4, 8)
 STRIPS = N // NB
 PAIR = 2 * P
 PASS_WORDS = 256
+QUAD = 32
 ALIGN = 256
 
 SHARE_R0 = 384
@@ -47,8 +48,10 @@ def tile_rocchio_feedback_rescore_s2_kernel(tc, queries, corpus, relevance, sim,
         ident_bf = keep.tile([P, P], BF16, name="ident_bf")
         gain_rows = keep.tile([P, P], BF16, name="gain_rows")
         gain_col = keep.tile([P, len(TILES)], F32, name="gain_col")
-        prior_raw = keep.tile([P, N // P], BF16, name="prior_raw")
-        prior_words = keep.tile([P, P, N // PAIR], F32, name="prior_words")
+        prior_raw = keep.tile([P, 2 * QUAD], BF16, name="prior_raw", align_bytes=ALIGN)
+        prior_turned = keep.tile([P, QUAD], F32, name="prior_turned", align_bytes=ALIGN)
+        prior_repeated = keep.tile([P, QUAD, QUAD], F32, name="prior_repeated", align_bytes=ALIGN)
+        prior_words = keep.tile([P, QUAD, QUAD], F32, name="prior_words", align_bytes=ALIGN)
 
         def operand_tile(pool, width, dtype, name, bufs=1):
             flat = pool.tile([P, width], dtype, name=name, bufs=bufs, align_bytes=ALIGN)
@@ -74,6 +77,11 @@ def tile_rocchio_feedback_rescore_s2_kernel(tc, queries, corpus, relevance, sim,
         def load_pair(x, a):
             pair_raw[x, a] = raw.tile([P, 2, E], BF16, name="pair_raw_t", bufs=8, align_bytes=ALIGN)
             nc.sync.dma_start(out=pair_raw[x, a][:], in_=pair_view[x][a])
+
+        def load_pair_in_halves(x, a):
+            pair_raw[x, a] = raw.tile([P, 2, E], BF16, name="pair_raw_t", bufs=8, align_bytes=ALIGN)
+            for t in range(2):
+                nc.sync.dma_start(out=pair_raw[x, a][:, t, :], in_=pair_view[x][a, :, t, :])
 
         def load_piece(x, c, b):
             piece = raw.tile([P, 4, NB], BF16, name="piece_raw_t", bufs=6, align_bytes=ALIGN)
@@ -118,6 +126,23 @@ def tile_rocchio_feedback_rescore_s2_kernel(tc, queries, corpus, relevance, sim,
                 drained[x, a, g][:].bitcast(F32).rearrange("p (r s) -> p r s", s=4),
                 turned[x, a, g][:].rearrange("p (s r) -> p r s", s=4),
             )
+
+        def turn_by_rows(x, a, bank):
+            for g in range(E_PASSES):
+                turned[x, a, g] = bank_tile(bank + g)
+            for t in range(2):
+                for g in range(E_PASSES):
+                    for u in range(2):
+                        words = pair_raw[x, a][:, t, :].bitcast(F32)[:, PASS_WORDS * g + u : PASS_WORDS * (g + 1) : 2]
+                        slot = 2 * t + u
+                        nc.tensor.transpose(turned[x, a, g][:, slot * P : (slot + 1) * P], words, ident[:])
+            for g in range(E_PASSES):
+                drained[x, a, g] = stage.tile([P, PAIR * 4], BF16, name="drained_t", bufs=6, align_bytes=ALIGN)
+                copy(
+                    S,
+                    drained[x, a, g][:].bitcast(F32).rearrange("p (r s) -> p r s", s=4),
+                    turned[x, a, g][:].rearrange("p (s r) -> p r s", s=4),
+                )
 
         def turn_pair(x, a, bank, engines=(S, S)):
             for g in range(E_PASSES):
@@ -219,13 +244,12 @@ def tile_rocchio_feedback_rescore_s2_kernel(tc, queries, corpus, relevance, sim,
             nc.tensor.transpose(columns[:], gain_rows[:], ident_bf[:])
             nc.vector.tensor_copy(out=gain_col[:], in_=columns[:, 0 : len(TILES)])
 
-        def spread_prior(h, bank):
-            spread = bank_tile(bank)
-            words = prior_raw[:].bitcast(F32)
-            for i in range(4):
-                column = words[:, 4 * h + i : 4 * h + i + 1]
-                nc.tensor.transpose(spread[:, i * P : (i + 1) * P], column.to_broadcast([P, P]), ident[:])
-            nc.vector.tensor_copy(out=prior_words[:, :, 4 * h : 4 * h + 4], in_=spread[:].rearrange("p (i w) -> p w i", i=4))
+        def spread_prior():
+            nc.vector.transpose(out=prior_turned[:], in_=prior_raw[:].bitcast(F32))
+            nc.vector.tensor_copy(out=prior_repeated[:], in_=prior_turned[:].unsqueeze(2).to_broadcast([P, QUAD, QUAD]))
+            nc.vector.transpose(
+                out=prior_words[:].rearrange("p b i -> p (b i)"), in_=prior_repeated[:].rearrange("p b i -> p (b i)")
+            )
 
         prior_all = prior_words[:].rearrange("p w i -> p (w i)").bitcast(BF16)
 
@@ -263,10 +287,11 @@ def tile_rocchio_feedback_rescore_s2_kernel(tc, queries, corpus, relevance, sim,
         make_identity(nc, ident[:])
         nc.gpsimd.memset(gain_rows[:], 0.0)
         make_identity(nc, ident_bf[:])
-        nc.sync.dma_start(out=prior_raw[:], in_=prior.rearrange("(p i) -> p i", p=P))
-        load_pair("c", 0)
-        load_pair("c", 1)
-        load_pair("q", 0)
+        load_pair_in_halves("c", 0)
+        for quad in range(P // QUAD):
+            nc.scalar.dma_start(out=prior_raw[quad * QUAD : (quad + 1) * QUAD, :], in_=prior.rearrange("(p i) -> p i", p=QUAD))
+        load_pair_in_halves("c", 1)
+        load_pair_in_halves("q", 0)
         nc.sync.dma_start(out=gain_rows[0 : len(TILES), :], in_=gain.rearrange("(m p) -> m p", p=P))
         load_pair("q", 1)
         load_piece("s", 0, 0)
@@ -279,12 +304,11 @@ def tile_rocchio_feedback_rescore_s2_kernel(tc, queries, corpus, relevance, sim,
         load_pair("c", 3)
         load_piece("r", 1, 0)
         load_piece("r", 1, 1)
-        for h in range(2):
-            spread_prior(h, h)
-        turn_pair("c", 0, 2, (S, V))
-        turn_pair("c", 1, 4, (S, S))
+        spread_prior()
+        turn_by_rows("c", 0, 2)
+        turn_by_rows("c", 1, 4)
         quant_pair("c", 0)
-        turn_pair("q", 0, 6, (S, S))
+        turn_by_rows("q", 0, 6)
         quant_pair("c", 1)
         spread_gain(0)
         turn_pair("q", 1, 2)

@@ -28,11 +28,6 @@ PASS_WORDS = 256
 QUAD = 32
 ALIGN = 256
 
-SHARE_R0 = 384
-SHARE_S0 = 192
-SHARE_S1 = 256
-SHARE_STREAM = 240
-
 
 def tile_rocchio_feedback_rescore_s2_kernel(tc, queries, corpus, relevance, sim, gain, prior, out):
     nc = tc.nc
@@ -147,6 +142,46 @@ def tile_rocchio_feedback_rescore_s2_kernel(tc, queries, corpus, relevance, sim,
         def turn_pair(x, a, bank, engines=(S, S)):
             for g in range(E_PASSES):
                 turn(x, a, g, bank + g, engines[g])
+
+        quad_view = corpus.rearrange("(n a i) (g q e) -> n g q i a e", a=NB // QUAD, i=QUAD, g=E_PASSES, q=P // QUAD)
+        quad_raw, quad_sorted, quad_turned, quad_ready = {}, {}, {}, {}
+
+        def load_quads(n, g):
+            quad_raw[n, g] = raw.tile([P, 2, E], BF16, name="pair_raw_t", bufs=8, align_bytes=ALIGN)
+            rows = quad_raw[n, g][:].rearrange("p t e -> p (t e)").rearrange("p (a e) -> p a e", a=NB // QUAD)
+            for q in (0, 2, 1, 3):
+                nc.sync.dma_start(out=rows[q * QUAD : (q + 1) * QUAD], in_=quad_view[n, g, q])
+
+        def sort_quads(n, g, engine):
+            quad_sorted[n, g] = raw.tile([P, 4, 2, P], F32, name="sorted_t", bufs=2, align_bytes=ALIGN)
+            words = quad_raw[n, g][:].rearrange("p t e -> p (t e)").bitcast(F32)
+            copy(
+                engine,
+                quad_sorted[n, g][:].rearrange("p s u w -> p (s u w)").rearrange("p (a u j) -> p a u j", u=2, j=QUAD),
+                words.rearrange("p (a j u) -> p a u j", u=2, j=QUAD),
+            )
+
+        def turn_quads(n, g):
+            quad_turned[n, g] = raw.tile([P, 2, E], BF16, name="pair_raw_t", bufs=8, align_bytes=ALIGN)
+            nc.vector.transpose(
+                out=quad_turned[n, g][:].rearrange("p t e -> p (t e)").bitcast(F32),
+                in_=quad_sorted[n, g][:].rearrange("p s u w -> p (s u w)"),
+            )
+
+        def pair_quads(n, g, engine):
+            quad_ready[n, g] = stage.tile([P, NB, 4], BF16, name="woven_t", bufs=5, align_bytes=ALIGN)
+            copy(
+                engine,
+                quad_ready[n, g][:].rearrange("p w i -> p (w i)").bitcast(F32).rearrange("p (a i u) -> p a i u", i=QUAD, u=2),
+                quad_turned[n, g][:].rearrange("p t e -> p (t e)").bitcast(F32).rearrange("p (a u i) -> p a i u", i=QUAD, u=2),
+            )
+
+        def quant_quads(n, g):
+            c_codes[n, g] = operand_tile(stage, NB, U32, "c_codes_t", 4)
+            c_scales[n, g] = operand_tile(stage, NB, U8, "c_scales_t", 4)
+            nc.vector.quantize_mx(
+                out=c_codes[n, g].bitcast(E4M3X4), scales=c_scales[n, g], in_=quad_ready[n, g][:].rearrange("p w i -> p (w i)")
+            )
 
         c_codes, c_scales, s_codes, s_scales = {}, {}, {}, {}
 
@@ -377,8 +412,8 @@ def tile_rocchio_feedback_rescore_s2_kernel(tc, queries, corpus, relevance, sim,
         load_pair("c", 5)
         load_two_pieces("s", 1, 2)
         load_two_pieces("s", 2, 2)
-        load_pair("c", 6)
-        load_pair("c", 7)
+        load_quads(3, 0)
+        load_quads(3, 1)
 
         for m in TILES:
             if m % 2 == 1:
@@ -401,47 +436,72 @@ def tile_rocchio_feedback_rescore_s2_kernel(tc, queries, corpus, relevance, sim,
             sort("c", 4 + h)
         rs_pass(1, EARLY, 2)
 
-        last = STRIPS - 1
-        for n in range(1, STRIPS):
-            if n > 1:
-                for m in LATE:
-                    store(n - 1, m)
-            for m in EARLY:
-                finish(n, m)
-                store(n, m)
-            close_late_tile(n, LATE[0])
-            close_late_tile(n, LATE[1])
-            if n < last:
-                weave("s", 1, n + 1, S)
-                quant_piece("s", 0, n + 1)
-                for g in range(E_PASSES):
-                    for h in range(2):
-                        turn("c", 2 * (n + 1) + h, g, EARLY[2 * g + h], S)
-                weave("s", 2, n + 1, S)
-                quant_corpus(n + 1, 0)
-            finish(n, LATE[0])
-            close_late_tile(n, LATE[2])
-            if n < last:
-                quant_corpus(n + 1, 1)
-            finish(n, LATE[1])
-            close_late_tile(n, LATE[3])
-            if n < last:
-                quant_piece("s", 1, n + 1)
-            finish(n, LATE[2])
-            if n < last:
-                finish(n, LATE[3])
-                rs_pass(n + 1, EARLY, 0)
-                if n + 1 < last:
-                    weave("s", 0, n + 2, S)
-                quant_piece("s", 2, n + 1)
-                qc_passes(n + 1, EARLY)
-                rs_pass(n + 1, EARLY, 1)
-                if n + 1 < last:
-                    for h in range(2):
-                        sort("c", 2 * (n + 2) + h)
-                rs_pass(n + 1, EARLY, 2)
+        for m in EARLY:
+            finish(1, m)
+            store(1, m)
+        close_late_tile(1, LATE[0])
+        close_late_tile(1, LATE[1])
+        weave("s", 1, 2, S)
+        quant_piece("s", 0, 2)
+        for g in range(E_PASSES):
+            for h in range(2):
+                turn("c", 4 + h, g, EARLY[2 * g + h], S)
+        weave("s", 2, 2, S)
+        quant_corpus(2, 0)
+        finish(1, LATE[0])
+        close_late_tile(1, LATE[2])
+        quant_corpus(2, 1)
+        finish(1, LATE[1])
+        close_late_tile(1, LATE[3])
+        quant_piece("s", 1, 2)
+        finish(1, LATE[2])
+        finish(1, LATE[3])
+        rs_pass(2, EARLY, 0)
+        weave("s", 0, 3, S)
+        quant_piece("s", 2, 2)
+        qc_passes(2, EARLY)
+        rs_pass(2, EARLY, 1)
+        sort_quads(3, 0, V)
+        sort_quads(3, 1, V)
+        turn_quads(3, 0)
+        rs_pass(2, EARLY, 2)
+
+        for m in LATE:
+            store(1, m)
+        weave("s", 1, 3, S)
+        pair_quads(3, 0, S)
+        for m in EARLY:
+            finish(2, m)
+            store(2, m)
+        weave("s", 2, 3, S)
+        for m in LATE:
+            close_late_tile(2, m)
+        quant_piece("s", 0, 3)
+        turn_quads(3, 1)
+        pair_quads(3, 1, S)
+        quant_piece("s", 1, 3)
+        quant_quads(3, 0)
+        finish(2, LATE[0])
+        quant_piece("s", 2, 3)
+        finish(2, LATE[1])
+        quant_quads(3, 1)
+        finish(2, LATE[2])
+        finish(2, LATE[3])
+        rs_pass(3, EARLY, 0)
+        rs_pass(3, EARLY, 1)
+        qc_pass(3, EARLY, 0)
+        rs_pass(3, EARLY, 2)
+        qc_pass(3, EARLY, 1)
+        for m in LATE:
+            store(2, m)
+        for m in EARLY:
+            finish(3, m)
+            store(3, m)
         for m in LATE[:3]:
-            store(last, m)
+            close_late_tile(3, m)
+            finish(3, m)
+            store(3, m)
+        close_late_tile(3, LATE[3])
         for lo in (0, PAIR):
-            finish(last, LATE[3], lo, lo + PAIR)
-            store(last, LATE[3], lo, lo + PAIR)
+            finish(3, LATE[3], lo, lo + PAIR)
+            store(3, LATE[3], lo, lo + PAIR)

@@ -26,6 +26,7 @@ STRIPS = N // NB
 PAIR = 2 * P
 PASS_WORDS = 256
 QUAD = 32
+STRIP_ROWS = NB // (2 * QUAD)
 ALIGN = 256
 
 
@@ -37,7 +38,7 @@ def tile_rocchio_feedback_rescore_s2_kernel(tc, queries, corpus, relevance, sim,
         stage = ctx.enter_context(tc.tile_pool(name="stage", bufs=1))
         psum = ctx.enter_context(tc.psum_pool(name="psum", bufs=1))
         ctx.enter_context(tc.manual_schedule())
-        V, S = "vector", "scalar"
+        V, S, G = "vector", "scalar", "gpsimd"
 
         ident = keep.tile([P, P], F32, name="ident")
         ident_bf = keep.tile([P, P], BF16, name="ident_bf")
@@ -67,11 +68,20 @@ def tile_rocchio_feedback_rescore_s2_kernel(tc, queries, corpus, relevance, sim,
             "r": relevance.rearrange("(c p i) m -> c p i m", p=P, i=4),
             "s": sim.rearrange("(c p i) n -> c p i n", p=P, i=4),
         }
-        pair_raw, piece_raw = {}, {}
+        pair_raw, piece_raw, half_raw = {}, {}, {}
 
         def load_pair(x, a):
             pair_raw[x, a] = raw.tile([P, 2, E], BF16, name="pair_raw_t", bufs=8, align_bytes=ALIGN)
             nc.sync.dma_start(out=pair_raw[x, a][:], in_=pair_view[x][a])
+
+        def load_prior():
+            for quad in range(P // QUAD):
+                nc.scalar.dma_start(
+                    out=prior_raw[quad * QUAD : (quad + 1) * QUAD, :], in_=prior.rearrange("(p i) -> p i", p=QUAD)
+                )
+
+        def load_gain():
+            nc.sync.dma_start(out=gain_rows[0 : len(TILES), :], in_=gain.rearrange("(m p) -> m p", p=P))
 
         def load_pair_in_halves(x, a):
             pair_raw[x, a] = raw.tile([P, 2, E], BF16, name="pair_raw_t", bufs=8, align_bytes=ALIGN)
@@ -82,6 +92,12 @@ def tile_rocchio_feedback_rescore_s2_kernel(tc, queries, corpus, relevance, sim,
             piece = raw.tile([P, 4, NB], BF16, name="piece_raw_t", bufs=6, align_bytes=ALIGN)
             nc.sync.dma_start(out=piece[:], in_=piece_view[x][c, :, :, b * NB : (b + 1) * NB])
             piece_raw[x, c, b] = piece[:]
+
+        def load_piece_in_halves(x, c, b):
+            piece = raw.tile([P, 2, 4, PAIR], BF16, name="piece_raw_t", bufs=6, align_bytes=ALIGN)
+            for h in range(2):
+                nc.sync.dma_start(out=piece[:, h], in_=piece_view[x][c, :, :, b * NB + h * PAIR : b * NB + (h + 1) * PAIR])
+            half_raw[x, c, b] = piece
 
         def load_two_pieces(x, c, b):
             both = raw.tile([P, 4, 2 * NB], BF16, name="two_pieces_raw_t", bufs=3, align_bytes=ALIGN)
@@ -95,6 +111,8 @@ def tile_rocchio_feedback_rescore_s2_kernel(tc, queries, corpus, relevance, sim,
         def copy(engine, dst, src):
             if engine == S:
                 nc.scalar.copy(out=dst, in_=src)
+            elif engine == G:
+                nc.gpsimd.tensor_scalar(out=dst, in0=src, scalar1=1.0, scalar2=0.0, op0=MULT, op1=ADD)
             else:
                 nc.vector.tensor_copy(out=dst, in_=src)
 
@@ -105,7 +123,7 @@ def tile_rocchio_feedback_rescore_s2_kernel(tc, queries, corpus, relevance, sim,
             words = pair_raw[x, a][:].rearrange("p t e -> p (t e)").bitcast(F32)
             copy(engine, pair_sorted[x, a][:], words.rearrange("p (s w u) -> p s u w", s=4, u=2))
 
-        def turn(x, a, g, bank, engine):
+        def turn(x, a, g, bank):
             turned[x, a, g] = bank_tile(bank)
             for t in range(2):
                 for u in range(2):
@@ -115,33 +133,17 @@ def tile_rocchio_feedback_rescore_s2_kernel(tc, queries, corpus, relevance, sim,
                         words = pair_raw[x, a][:, t, :].bitcast(F32)[:, PASS_WORDS * g + u : PASS_WORDS * (g + 1) : 2]
                     slot = 2 * t + u
                     nc.tensor.transpose(turned[x, a, g][:, slot * P : (slot + 1) * P], words, ident[:])
-            drained[x, a, g] = stage.tile([P, PAIR * 4], BF16, name="drained_t", bufs=6, align_bytes=ALIGN)
+
+        def slot_tile(slot):
+            return stage.tile([P, PAIR * 4], BF16, name="slot_t", tag=f"slot{slot}", align_bytes=ALIGN)
+
+        def drain(x, a, g, engine, slot):
+            drained[x, a, g] = slot_tile(slot)
             copy(
                 engine,
                 drained[x, a, g][:].bitcast(F32).rearrange("p (r s) -> p r s", s=4),
                 turned[x, a, g][:].rearrange("p (s r) -> p r s", s=4),
             )
-
-        def turn_by_rows(x, a, bank):
-            for g in range(E_PASSES):
-                turned[x, a, g] = bank_tile(bank + g)
-            for t in range(2):
-                for g in range(E_PASSES):
-                    for u in range(2):
-                        words = pair_raw[x, a][:, t, :].bitcast(F32)[:, PASS_WORDS * g + u : PASS_WORDS * (g + 1) : 2]
-                        slot = 2 * t + u
-                        nc.tensor.transpose(turned[x, a, g][:, slot * P : (slot + 1) * P], words, ident[:])
-            for g in range(E_PASSES):
-                drained[x, a, g] = stage.tile([P, PAIR * 4], BF16, name="drained_t", bufs=6, align_bytes=ALIGN)
-                copy(
-                    S,
-                    drained[x, a, g][:].bitcast(F32).rearrange("p (r s) -> p r s", s=4),
-                    turned[x, a, g][:].rearrange("p (s r) -> p r s", s=4),
-                )
-
-        def turn_pair(x, a, bank, engines=(S, S)):
-            for g in range(E_PASSES):
-                turn(x, a, g, bank + g, engines[g])
 
         quad_view = corpus.rearrange("(n a i) (g q e) -> n g q i a e", a=NB // QUAD, i=QUAD, g=E_PASSES, q=P // QUAD)
         quad_raw, quad_sorted, quad_turned, quad_ready = {}, {}, {}, {}
@@ -169,7 +171,7 @@ def tile_rocchio_feedback_rescore_s2_kernel(tc, queries, corpus, relevance, sim,
             )
 
         def pair_quads(n, g, engine):
-            quad_ready[n, g] = stage.tile([P, NB, 4], BF16, name="woven_t", bufs=5, align_bytes=ALIGN)
+            quad_ready[n, g] = stage.tile([P, NB, 4], BF16, name="woven_t", bufs=4, align_bytes=ALIGN)
             copy(
                 engine,
                 quad_ready[n, g][:].rearrange("p w i -> p (w i)").bitcast(F32).rearrange("p (a i u) -> p a i u", i=QUAD, u=2),
@@ -209,12 +211,41 @@ def tile_rocchio_feedback_rescore_s2_kernel(tc, queries, corpus, relevance, sim,
 
         def weave(x, c, b, engine, lo=0, hi=NB):
             if (x, c, b) not in woven:
-                woven[x, c, b] = stage.tile([P, NB, 4], BF16, name="woven_t", bufs=5, align_bytes=ALIGN)
+                woven[x, c, b] = stage.tile([P, NB, 4], BF16, name="woven_t", bufs=4, align_bytes=ALIGN)
+            if (x, c, b) in half_raw:
+                h = lo // PAIR
+                rows = half_raw[x, c, b][:, h, :, lo - h * PAIR : hi - h * PAIR]
+            else:
+                rows = piece_raw[x, c, b][:, :, lo:hi]
             copy(
                 engine,
                 woven[x, c, b][:, lo:hi, :].rearrange("p (w j) i -> p w i j", j=4),
-                piece_raw[x, c, b][:, :, lo:hi].rearrange("p i (w j) -> p w i j", j=4),
+                rows.rearrange("p i (w j) -> p w i j", j=4),
             )
+
+        half_woven = {}
+
+        def weave_half(x, c, b, h, engine, lo, hi, slot):
+            if (x, c, b, h) not in half_woven:
+                half_woven[x, c, b, h] = slot_tile(slot)
+            dst = half_woven[x, c, b, h][:].rearrange("p (w i) -> p w i", i=4)
+            copy(
+                engine,
+                dst[:, lo:hi, :].rearrange("p (w j) i -> p w i j", j=4),
+                piece_raw[x, c, b][:, :, h * PAIR + lo : h * PAIR + hi].rearrange("p i (w j) -> p w i j", j=4),
+            )
+
+        def quant_half(x, c, b, h):
+            if x == "r":
+                cols = slice(b * NB + h * PAIR, b * NB + (h + 1) * PAIR)
+                codes, scales = r_codes[:, c, cols].bitcast(E5M2X4), r_scales[:, c, cols]
+            else:
+                if (c, b) not in s_codes:
+                    s_codes[c, b] = operand_tile(stage, NB, U32, "s_codes_t", 7)
+                    s_scales[c, b] = operand_tile(stage, NB, U8, "s_scales_t", 7)
+                cols = slice(h * PAIR, (h + 1) * PAIR)
+                codes, scales = s_codes[c, b][:, cols].bitcast(E4M3X4), s_scales[c, b][:, cols]
+            nc.vector.quantize_mx(out=codes, scales=scales, in_=half_woven[x, c, b, h][:])
 
         def weave_shared(x, c, b, share):
             weave(x, c, b, S, 0, share)
@@ -232,7 +263,26 @@ def tile_rocchio_feedback_rescore_s2_kernel(tc, queries, corpus, relevance, sim,
 
         acc, passes_done = {}, {}
 
+        parked = set()
+
+        def park_pass(m, g, bank, lo=0, hi=NB):
+            if m not in parked:
+                acc["park", m] = bank_tile(bank)
+                parked.add(m)
+            a, h = divmod(m, 2)
+            cols = slice(h * P, (h + 1) * P)
+            nc.tensor.matmul_mx(
+                out=acc["park", m][:, lo:hi],
+                lhsT=q_codes[:, a, g, cols].bitcast(E4M3X4),
+                lhsT_scale=q_scales[:, a, g, cols],
+                rhs=c_codes[1, g][:, lo:hi].bitcast(E4M3X4),
+                rhs_scale=c_scales[1, g][:, lo:hi],
+                start=(g == 0),
+                stop=(g == E_PASSES - 1),
+            )
+
         def mx_pass(n, m, lhsT, lhsT_scale, rhs, rhs_scale):
+            passes = J_PASSES if n == 1 and m in parked else E_PASSES + J_PASSES
             if (n, m) not in acc:
                 acc[n, m] = bank_tile(m)
                 passes_done[n, m] = 0
@@ -244,7 +294,7 @@ def tile_rocchio_feedback_rescore_s2_kernel(tc, queries, corpus, relevance, sim,
                 rhs=rhs,
                 rhs_scale=rhs_scale,
                 start=(passes_done[n, m] == 1),
-                stop=(passes_done[n, m] == E_PASSES + J_PASSES),
+                stop=(passes_done[n, m] == passes),
             )
 
         def qc_pass(n, tiles, g):
@@ -274,43 +324,73 @@ def tile_rocchio_feedback_rescore_s2_kernel(tc, queries, corpus, relevance, sim,
             for c in range(0 if n > 1 else 1, J_PASSES):
                 rs_pass(n, [m], c)
 
-        def spread_gain(bank):
-            columns = bank_tile(bank, (P, P), BF16)
-            nc.tensor.transpose(columns[:], gain_rows[:], ident_bf[:])
-            nc.vector.tensor_copy(out=gain_col[:], in_=columns[:, 0 : len(TILES)])
+        gain_turned = {}
 
-        def spread_prior():
+        def turn_gain(bank):
+            gain_turned[0] = bank_tile(bank, (P, P), BF16)
+            nc.tensor.transpose(gain_turned[0][:], gain_rows[:], ident_bf[:])
+
+        def drain_gain():
+            nc.vector.tensor_copy(out=gain_col[:], in_=gain_turned[0][:, 0 : len(TILES)])
+
+        def turn_prior():
             nc.vector.transpose(out=prior_turned[:], in_=prior_raw[:].bitcast(F32))
-            nc.vector.tensor_copy(out=prior_repeated[:], in_=prior_turned[:].unsqueeze(2).to_broadcast([P, QUAD, QUAD]))
+
+        def spread_prior(n):
+            rows = slice(n * STRIP_ROWS, (n + 1) * STRIP_ROWS)
+            nc.vector.tensor_copy(
+                out=prior_repeated[:, rows, :], in_=prior_turned[:, rows].unsqueeze(2).to_broadcast([P, STRIP_ROWS, QUAD])
+            )
+
+        def finish_prior(n):
+            rows = slice(n * STRIP_ROWS, (n + 1) * STRIP_ROWS)
             nc.vector.transpose(
-                out=prior_words[:].rearrange("p b i -> p (b i)"), in_=prior_repeated[:].rearrange("p b i -> p (b i)")
+                out=prior_words[:, rows, :].rearrange("p b i -> p (b i)"),
+                in_=prior_repeated[:, rows, :].rearrange("p b i -> p (b i)"),
             )
 
         prior_all = prior_words[:].rearrange("p w i -> p (w i)").bitcast(BF16)
 
         result, result_01 = {}, {}
 
-        def finish(n, m, lo=0, hi=NB):
-            if n == 0:
+        def result_pair(m):
+            if m not in result_01:
                 result_01[m] = stage.tile([P, 2 * NB], F32, name="result_01_t", bufs=len(TILES))
                 result[0, m], result[1, m] = result_01[m][:, :NB], result_01[m][:, NB:]
-            elif n > 1 and lo == 0:
+
+        def park(m):
+            result_pair(m)
+            nc.vector.scalar_tensor_tensor(
+                out=result[1, m], in0=acc["park", m][:], scalar=gain_col[:, m : m + 1], in1=prior_all[:, NB : 2 * NB],
+                op0=MULT, op1=ADD,
+            )
+
+        def park_scaled(m):
+            result_pair(m)
+            nc.scalar.activation(out=result[1, m], in_=acc["park", m][:], func=COPY, scale=gain_col[:, m : m + 1])
+
+        def finish(n, m, lo=0, hi=NB):
+            if n < 2:
+                result_pair(m)
+            elif lo == 0:
                 single = stage.tile([P, NB], F32, name="result_t", bufs=len(TILES))
                 result[n, m] = single[:]
-            if n == 0 and m % 2 == 1:
-                nc.scalar.activation(out=result[n, m], in_=acc[n, m][:], func=COPY, scale=gain_col[:, m : m + 1])
-                return
+            rest = result[n, m][:, lo:hi] if n == 1 and m in parked else prior_all[:, n * NB + lo : n * NB + hi]
             nc.vector.scalar_tensor_tensor(
                 out=result[n, m][:, lo:hi],
                 in0=acc[n, m][:, lo:hi],
                 scalar=gain_col[:, m : m + 1],
-                in1=prior_all[:, n * NB + lo : n * NB + hi],
+                in1=rest,
                 op0=MULT,
                 op1=ADD,
             )
 
-        def add_prior(m):
-            nc.vector.tensor_tensor(out=result[0, m], in0=result[0, m], in1=prior_all[:, :NB], op=ADD)
+        def scale_only(m):
+            result_pair(m)
+            nc.scalar.activation(out=result[0, m], in_=acc[0, m][:], func=COPY, scale=gain_col[:, m : m + 1])
+
+        def add_prior(n, m):
+            nc.vector.tensor_tensor(out=result[n, m], in0=result[n, m], in1=prior_all[:, n * NB : (n + 1) * NB], op=ADD)
 
         def store(n, m, lo=0, hi=NB):
             rows = slice(m * P, (m + 1) * P)
@@ -322,90 +402,150 @@ def tile_rocchio_feedback_rescore_s2_kernel(tc, queries, corpus, relevance, sim,
         make_identity(nc, ident[:])
         nc.gpsimd.memset(gain_rows[:], 0.0)
         make_identity(nc, ident_bf[:])
-        load_pair_in_halves("c", 0)
-        for quad in range(P // QUAD):
-            nc.scalar.dma_start(out=prior_raw[quad * QUAD : (quad + 1) * QUAD, :], in_=prior.rearrange("(p i) -> p i", p=QUAD))
-        load_pair_in_halves("c", 1)
+        load_pair_in_halves("c", 2)
+        load_prior()
+        load_pair_in_halves("c", 3)
         load_pair_in_halves("q", 0)
-        nc.sync.dma_start(out=gain_rows[0 : len(TILES), :], in_=gain.rearrange("(m p) -> m p", p=P))
+        load_gain()
         load_pair("q", 1)
         load_piece("s", 0, 0)
         load_pair("q", 2)
         load_piece("r", 0, 0)
         load_pair("q", 3)
-        load_piece("r", 0, 1)
-        load_pair("c", 2)
         load_piece("s", 1, 0)
-        load_pair("c", 3)
+        load_pair("c", 0)
         load_piece("r", 1, 0)
-        load_piece("r", 1, 1)
-        spread_prior()
-        turn_by_rows("c", 0, 2)
-        turn_by_rows("c", 1, 4)
-        quant_pair("c", 0)
-        turn_by_rows("q", 0, 6)
-        quant_pair("c", 1)
-        spread_gain(0)
-        turn_pair("q", 1, 2)
-        quant_pair("q", 0)
-        qc_passes(0, TILES[0:2])
-        weave("s", 0, 0, V, 192, NB)
-        quant_pair("q", 1)
-        weave("s", 0, 0, S, 0, 192)
-        sort("q", 2)
-        qc_passes(0, TILES[2:4])
-        quant_piece("s", 0, 0)
+        load_pair("c", 1)
+        load_piece("r", 0, 1)
         load_piece("s", 2, 0)
-        weave("r", 0, 0, S, 0, 224)
-        weave("r", 0, 0, V, 224, NB)
-        sort("q", 3)
-        turn_pair("q", 2, 4)
-        turn_pair("q", 3, 6)
-        quant_piece("r", 0, 0)
-        load_piece("r", 2, 0)
-        rs_pass(0, EARLY, 0)
-        weave("r", 0, 1, V, 128, NB)
-        quant_pair("q", 2)
-        weave("r", 0, 1, S, 0, 128)
-        turn_pair("c", 2, 6)
-        quant_pair("q", 3)
-        qc_passes(0, TILES[4:6])
-        weave("s", 1, 0, V, 128, NB)
-        quant_piece("r", 0, 1)
-        load_piece("r", 2, 1)
-        weave("s", 1, 0, S, 0, 128)
-        quant_pair("c", 2)
-        quant_piece("s", 1, 0)
-        weave_shared("r", 1, 0, 96)
-        turn_pair("c", 3, 6)
-        load_piece("s", 0, 1)
-        rs_pass(0, TILES[4:6], 0)
-        weave_shared("r", 1, 1, 224)
-        quant_piece("r", 1, 0)
-        qc_passes(0, TILES[6:8])
-        rs_pass(0, TILES[6:8], 0)
-        rs_pass(0, EARLY, 1)
-        weave_shared("s", 2, 0, 256)
-        quant_piece("r", 1, 1)
-        rs_pass(0, LATE, 1)
-        weave("r", 2, 0, S, 0, PAIR)
-
-        weave("r", 2, 0, V, PAIR, NB)
-        quant_piece("s", 2, 0)
-        weave("r", 2, 1, S, 0, PAIR)
-        quant_piece("r", 2, 0, PAIR, NB)
-        rs_pass(0, TILES[2:4], 2)
-        quant_piece("r", 2, 0, 0, PAIR)
-        rs_pass(0, TILES[0:2], 2)
-        weave("r", 2, 1, V, PAIR, NB)
+        turn("c", 2, 0, 2)
+        drain("c", 2, 0, S, 0)
+        turn_prior()
+        turn("c", 2, 1, 3)
+        drain("c", 2, 1, S, 1)
+        spread_prior(1)
+        turn("c", 3, 0, 4)
+        drain("c", 3, 0, S, 2)
+        spread_prior(0)
+        turn("c", 3, 1, 5)
+        drain("c", 3, 1, S, 3)
+        finish_prior(1)
+        turn("q", 0, 0, 6)
+        drain("q", 0, 0, S, 4)
+        finish_prior(0)
+        turn("q", 0, 1, 7)
+        drain("q", 0, 1, S, 5)
+        spread_prior(2)
+        turn_gain(0)
+        spread_prior(3)
+        turn("q", 1, 0, 4)
+        drain("q", 1, 0, S, 6)
+        finish_prior(2)
+        turn("q", 1, 1, 5)
+        drain("q", 1, 1, S, 7)
+        quant_turned("c", 2, 0)
+        weave("s", 0, 0, S, 0, 128)
+        finish_prior(3)
+        weave_half("r", 0, 0, 1, S, 0, 256, 0)
+        quant_turned("c", 2, 1)
         quant_turned("c", 3, 0)
-        quant_piece("r", 2, 1, PAIR, NB)
-        rs_pass(0, TILES[6:8], 2)
-        quant_piece("r", 2, 1, 0, PAIR)
-        rs_pass(0, TILES[4:6], 2)
         quant_turned("c", 3, 1)
-
+        drain_gain()
+        quant_turned("q", 0, 0)
+        park_pass(0, 0, 0)
+        weave("s", 0, 0, V, 384, 512)
+        park_pass(1, 0, 1)
+        quant_turned("q", 0, 1)
+        park_pass(0, 1, 0)
+        weave("s", 0, 0, V, 128, 384)
+        load_piece("r", 2, 0)
+        park_pass(1, 1, 1)
+        sort("q", 2, V)
+        turn("q", 2, 0, 6)
+        drain("q", 2, 0, S, 1)
+        quant_turned("q", 1, 0)
+        weave_half("r", 0, 0, 0, G, 0, 192, 6)
+        turn("q", 2, 1, 7)
+        drain("q", 2, 1, S, 2)
+        quant_turned("q", 1, 1)
+        park_pass(2, 0, 2)
+        weave_half("r", 0, 0, 0, S, 192, 256, 6)
+        park(0)
+        load_piece("r", 1, 1)
+        park_pass(3, 0, 3)
+        weave_half("s", 1, 0, 1, S, 0, 256, 3)
+        park(1)
+        park_pass(2, 1, 2)
+        sort("q", 3, V)
+        park_pass(3, 1, 3)
+        quant_turned("q", 2, 0)
+        turn("q", 3, 0, 4)
+        drain("q", 3, 0, S, 4)
+        quant_turned("q", 2, 1)
+        weave_half("s", 1, 0, 0, G, 0, 192, 2)
+        turn("q", 3, 1, 5)
+        drain("q", 3, 1, S, 5)
+        quant_half("r", 0, 0, 1)
+        park_pass(4, 0, 0)
+        weave_half("s", 1, 0, 0, S, 192, 256, 2)
+        park(2)
+        load_piece("r", 2, 1)
+        park_pass(5, 0, 1)
+        park(3)
+        park_pass(4, 1, 0)
+        quant_piece("s", 0, 0, 0, 512)
+        park_pass(5, 1, 1)
+        quant_turned("q", 3, 0)
+        turn("c", 0, 0, 6)
+        drain("c", 0, 0, S, 7)
+        quant_turned("q", 3, 1)
+        weave_half("r", 1, 0, 0, G, 0, 192, 5)
+        turn("c", 0, 1, 7)
+        drain("c", 0, 1, S, 1)
+        quant_half("r", 0, 0, 0)
+        park_pass(6, 0, 2)
+        weave_half("r", 1, 0, 0, S, 192, 256, 5)
+        park(4)
+        park_pass(7, 0, 3)
+        weave_half("r", 1, 0, 1, S, 0, 256, 0)
+        park(5)
+        load_piece("s", 0, 1)
+        park_pass(6, 1, 2)
+        quant_half("s", 1, 0, 1)
+        weave_half("r", 0, 1, 0, G, 0, 192, 3)
+        park_pass(7, 1, 3)
+        quant_turned("c", 0, 0)
+        turn("c", 1, 0, 4)
+        drain("c", 1, 0, S, 4)
+        park(6)
+        turn("c", 1, 1, 5)
+        drain("c", 1, 1, S, 6)
+        park(7)
+        rs_pass(0, [0, 1, 2, 3], 0)
+        weave_half("r", 0, 1, 0, S, 192, 256, 3)
+        quant_turned("c", 0, 1)
+        weave_half("r", 0, 1, 1, S, 0, 256, 7)
+        quant_turned("c", 1, 0)
         load_piece("s", 1, 1)
+        qc_pass(0, [0, 1, 2, 3], 0)
+        weave("s", 2, 0, S, 0, 256)
+        quant_turned("c", 1, 1)
+        qc_pass(0, [6, 7], 0)
+        weave("r", 2, 0, S, 0, 256)
+        quant_half("s", 1, 0, 0)
+        qc_pass(0, [4, 5], 0)
+        weave("r", 1, 1, S, 0, 256)
+        quant_half("r", 1, 0, 0)
+        qc_pass(0, [0, 1, 2, 3], 1)
+        weave("r", 2, 1, S, 0, 256)
+        quant_half("r", 1, 0, 1)
+        qc_pass(0, [6, 7], 1)
+        weave_half("s", 0, 1, 0, S, 0, 256, 0)
+        quant_half("r", 0, 1, 0)
+        qc_pass(0, [4, 5], 1)
+        quant_half("r", 0, 1, 1)
+        rs_pass(0, [0, 1, 2, 3], 1)
+        weave("s", 2, 0, V, 256, 512)
         load_piece("s", 2, 1)
         load_two_pieces("s", 0, 2)
         load_pair("c", 4)
@@ -414,94 +554,177 @@ def tile_rocchio_feedback_rescore_s2_kernel(tc, queries, corpus, relevance, sim,
         load_two_pieces("s", 2, 2)
         load_quads(3, 0)
         load_quads(3, 1)
-
-        for m in TILES:
-            if m % 2 == 1:
-                weave("s", 0, 1, S, (m // 2) * P, (m // 2 + 1) * P)
-            finish(0, m)
-            qc_passes(1, [m])
-        weave("s", 1, 1, S)
-        weave("s", 2, 1, V)
-        quant_piece("s", 0, 1)
-        rs_pass(1, TILES, 0)
-        quant_piece("s", 2, 1)
-        weave("s", 0, 2, S)
-        for m in EARLY[1::2]:
-            add_prior(m)
-        quant_piece("s", 1, 1)
-        for m in LATE[1::2]:
-            add_prior(m)
-        rs_pass(1, EARLY, 1)
-        for h in range(2):
-            sort("c", 4 + h)
-        rs_pass(1, EARLY, 2)
-
-        for m in EARLY:
-            finish(1, m)
-            store(1, m)
-        close_late_tile(1, LATE[0])
-        close_late_tile(1, LATE[1])
-        weave("s", 1, 2, S)
-        quant_piece("s", 0, 2)
-        for g in range(E_PASSES):
-            for h in range(2):
-                turn("c", 4 + h, g, EARLY[2 * g + h], S)
-        weave("s", 2, 2, S)
-        quant_corpus(2, 0)
-        finish(1, LATE[0])
-        close_late_tile(1, LATE[2])
-        quant_corpus(2, 1)
-        finish(1, LATE[1])
-        close_late_tile(1, LATE[3])
-        quant_piece("s", 1, 2)
-        finish(1, LATE[2])
-        finish(1, LATE[3])
-        rs_pass(2, EARLY, 0)
-        weave("s", 0, 3, S)
-        quant_piece("s", 2, 2)
-        qc_passes(2, EARLY)
-        rs_pass(2, EARLY, 1)
+        rs_pass(0, [4, 5, 6, 7], 0)
+        weave("r", 2, 0, V, 256, 512)
+        quant_piece("s", 2, 0, 0, 512)
+        weave("s", 1, 1, S, 0, 512)
+        weave("r", 1, 1, V, 256, 512)
+        weave_half("s", 2, 1, 1, S, 0, 256, 3)
+        quant_piece("r", 2, 0, 0, 512)
+        rs_pass(0, [0, 1, 2, 3], 2)
+        weave("s", 0, 2, S, 0, 512)
+        weave("r", 2, 1, V, 256, 512)
+        quant_piece("r", 1, 1, 0, 512)
+        rs_pass(0, [4, 5, 6, 7], 1)
+        weave("s", 1, 2, S, 0, 512)
+        weave_half("s", 0, 1, 1, V, 0, 256, 7)
+        quant_piece("r", 2, 1, 0, 512)
+        rs_pass(0, [4, 5, 6, 7], 2)
+        quant_half("s", 0, 1, 0)
+        weave_half("s", 2, 1, 0, G, 0, 256, 0)
+        quant_half("s", 0, 1, 1)
+        finish(0, 0, 0, 512)
+        finish(0, 1, 0, 512)
+        finish(0, 2, 0, 512)
+        finish(0, 3, 0, 512)
+        rs_pass(1, [0, 1, 2, 3], 0)
+        quant_piece("s", 1, 1, 0, 512)
+        rs_pass(1, [0, 1, 2, 3], 1)
+        finish(0, 4, 0, 512)
+        finish(0, 5, 0, 512)
+        finish(0, 6, 0, 512)
+        finish(0, 7, 0, 512)
+        rs_pass(1, [4, 5, 6, 7], 0)
+        quant_half("s", 2, 1, 0)
+        quant_half("s", 2, 1, 1)
+        rs_pass(1, [0, 1, 2, 3], 2)
+        sort("c", 4, V)
+        rs_pass(1, [4], 1)
+        sort("c", 5, V)
+        rs_pass(1, [4], 2)
+        finish(1, 0, 0, 512)
+        store(1, 0, 0, 512)
+        rs_pass(1, [5], 1)
+        finish(1, 1, 0, 512)
+        store(1, 1, 0, 512)
+        rs_pass(1, [5], 2)
+        finish(1, 2, 0, 512)
+        store(1, 2, 0, 512)
+        turn("c", 4, 0, 0)
+        drain("c", 4, 0, S, 0)
+        finish(1, 3, 0, 512)
+        store(1, 3, 0, 512)
+        turn("c", 5, 0, 1)
+        drain("c", 5, 0, S, 1)
+        quant_piece("s", 0, 2, 0, 512)
+        turn("c", 4, 1, 2)
+        drain("c", 4, 1, S, 2)
+        quant_turned("c", 4, 0)
+        turn("c", 5, 1, 3)
+        drain("c", 5, 1, S, 3)
+        quant_turned("c", 5, 0)
+        rs_pass(1, [6], 1)
+        weave("s", 2, 2, S, 0, 512)
+        finish(1, 4, 0, 512)
+        store(1, 4, 0, 512)
+        rs_pass(1, [6], 2)
+        weave("s", 0, 3, S, 0, 512)
+        quant_turned("c", 4, 1)
+        rs_pass(1, [7], 1)
+        weave("s", 1, 3, S, 0, 512)
+        quant_turned("c", 5, 1)
+        rs_pass(1, [7], 2)
+        finish(1, 5, 0, 512)
+        store(1, 5, 0, 512)
+        rs_pass(2, [0, 1, 2, 3], 0)
+        quant_piece("s", 1, 2, 0, 512)
+        qc_pass(2, [0, 1, 2, 3], 0)
+        finish(1, 6, 0, 512)
+        store(1, 6, 0, 512)
+        qc_pass(2, [0, 1, 2, 3], 1)
+        finish(1, 7, 0, 512)
+        store(1, 7, 0, 512)
+        rs_pass(2, [0, 1, 2, 3], 1)
+        quant_piece("s", 2, 2, 0, 512)
+        rs_pass(2, [0, 1, 2, 3], 2)
         sort_quads(3, 0, V)
+        qc_pass(2, [4], 0)
         sort_quads(3, 1, V)
+        qc_pass(2, [4], 1)
         turn_quads(3, 0)
-        rs_pass(2, EARLY, 2)
-
-        for m in LATE:
-            store(1, m)
-        weave("s", 1, 3, S)
+        rs_pass(2, [4], 0)
         pair_quads(3, 0, S)
-        for m in EARLY:
-            finish(2, m)
-            store(2, m)
-        weave("s", 2, 3, S)
-        for m in LATE:
-            close_late_tile(2, m)
-        quant_piece("s", 0, 3)
+        finish(2, 0, 0, 512)
+        store(2, 0, 0, 512)
+        rs_pass(2, [4], 1)
+        weave("s", 2, 3, S, 0, 512)
+        finish(2, 1, 0, 512)
+        store(2, 1, 0, 512)
+        rs_pass(2, [4], 2)
+        finish(2, 2, 0, 512)
+        store(2, 2, 0, 512)
+        qc_pass(2, [5], 0)
+        finish(2, 3, 0, 512)
+        store(2, 3, 0, 512)
+        qc_pass(2, [5], 1)
+        quant_piece("s", 0, 3, 0, 512)
+        rs_pass(2, [5], 0)
         turn_quads(3, 1)
+        rs_pass(2, [5], 1)
         pair_quads(3, 1, S)
-        quant_piece("s", 1, 3)
+        quant_piece("s", 1, 3, 0, 512)
+        rs_pass(2, [5], 2)
         quant_quads(3, 0)
-        finish(2, LATE[0])
-        quant_piece("s", 2, 3)
-        finish(2, LATE[1])
+        qc_pass(2, [6], 0)
+        finish(2, 4, 0, 512)
+        store(2, 4, 0, 512)
+        qc_pass(2, [6], 1)
+        quant_piece("s", 2, 3, 0, 512)
+        rs_pass(2, [6], 0)
+        finish(2, 5, 0, 512)
+        store(2, 5, 0, 512)
+        rs_pass(2, [6], 1)
         quant_quads(3, 1)
-        finish(2, LATE[2])
-        finish(2, LATE[3])
-        rs_pass(3, EARLY, 0)
-        rs_pass(3, EARLY, 1)
-        qc_pass(3, EARLY, 0)
-        rs_pass(3, EARLY, 2)
-        qc_pass(3, EARLY, 1)
-        for m in LATE:
-            store(2, m)
-        for m in EARLY:
-            finish(3, m)
-            store(3, m)
-        for m in LATE[:3]:
-            close_late_tile(3, m)
-            finish(3, m)
-            store(3, m)
-        close_late_tile(3, LATE[3])
-        for lo in (0, PAIR):
-            finish(3, LATE[3], lo, lo + PAIR)
-            store(3, LATE[3], lo, lo + PAIR)
+        rs_pass(2, [6], 2)
+        finish(2, 6, 0, 512)
+        store(2, 6, 0, 512)
+        qc_pass(2, [7], 0)
+        qc_pass(2, [7], 1)
+        rs_pass(2, [7], 0)
+        rs_pass(2, [7], 1)
+        rs_pass(2, [7], 2)
+        finish(2, 7, 0, 512)
+        store(2, 7, 0, 512)
+        rs_pass(3, [0, 1, 2, 3], 0)
+        rs_pass(3, [0, 1, 2, 3], 1)
+        qc_pass(3, [0, 1, 2, 3], 0)
+        rs_pass(3, [0, 1, 2, 3], 2)
+        qc_pass(3, [0, 1, 2, 3], 1)
+        finish(3, 0, 0, 512)
+        store(3, 0, 0, 512)
+        qc_pass(3, [4], 0)
+        finish(3, 1, 0, 512)
+        store(3, 1, 0, 512)
+        qc_pass(3, [4], 1)
+        finish(3, 2, 0, 512)
+        store(3, 2, 0, 512)
+        rs_pass(3, [4], 0)
+        finish(3, 3, 0, 512)
+        store(3, 3, 0, 512)
+        rs_pass(3, [4], 1)
+        rs_pass(3, [4], 2)
+        finish(3, 4, 0, 512)
+        store(3, 4, 0, 512)
+        qc_pass(3, [5], 0)
+        qc_pass(3, [5], 1)
+        rs_pass(3, [5], 0)
+        rs_pass(3, [5], 1)
+        rs_pass(3, [5], 2)
+        finish(3, 5, 0, 512)
+        store(3, 5, 0, 512)
+        qc_pass(3, [6], 0)
+        qc_pass(3, [6], 1)
+        rs_pass(3, [6], 0)
+        rs_pass(3, [6], 1)
+        rs_pass(3, [6], 2)
+        finish(3, 6, 0, 512)
+        store(3, 6, 0, 512)
+        qc_pass(3, [7], 0)
+        qc_pass(3, [7], 1)
+        rs_pass(3, [7], 0)
+        rs_pass(3, [7], 1)
+        rs_pass(3, [7], 2)
+        finish(3, 7, 0, 256)
+        store(3, 7, 0, 256)
+        finish(3, 7, 256, 512)
+        store(3, 7, 256, 512)

@@ -228,12 +228,12 @@ def tile_rocchio_feedback_rescore_s2_kernel(tc, queries, corpus, relevance, sim,
         def weave_half(x, c, b, h, engine, lo, hi, slot):
             if (x, c, b, h) not in half_woven:
                 half_woven[x, c, b, h] = slot_tile(slot)
-            dst = half_woven[x, c, b, h][:].rearrange("p (w i) -> p w i", i=4)
-            copy(
-                engine,
-                dst[:, lo:hi, :].rearrange("p (w j) i -> p w i j", j=4),
-                piece_raw[x, c, b][:, :, h * PAIR + lo : h * PAIR + hi].rearrange("p i (w j) -> p w i j", j=4),
-            )
+            dst = half_woven[x, c, b, h][:].rearrange("p (w i) -> p w i", i=4)[:, lo:hi, :]
+            src = piece_raw[x, c, b][:, :, h * PAIR + lo : h * PAIR + hi]
+            if engine == G:
+                copy(engine, dst, src.rearrange("p i w -> p w i"))
+            else:
+                copy(engine, dst.rearrange("p (w j) i -> p w i j", j=4), src.rearrange("p i (w j) -> p w i j", j=4))
 
         def quant_half(x, c, b, h):
             if x == "r":
@@ -318,6 +318,30 @@ def tile_rocchio_feedback_rescore_s2_kernel(tc, queries, corpus, relevance, sim,
                     s_codes[c, n].bitcast(E4M3X4), s_scales[c, n],
                 )
 
+        def last_part(lo, hi, bank):
+            n, m = STRIPS - 1, TILES[-1]
+            a, h = divmod(m, 2)
+            acc["last", lo] = bank_tile(bank, (P, hi - lo))
+            stationary = [
+                (q_codes[:, a, g, h * P : (h + 1) * P].bitcast(E4M3X4), q_scales[:, a, g, h * P : (h + 1) * P])
+                for g in range(E_PASSES)
+            ] + [
+                (r_codes[:, c, m * P : (m + 1) * P].bitcast(E5M2X4), r_scales[:, c, m * P : (m + 1) * P])
+                for c in range(J_PASSES)
+            ]
+            moving = [(c_codes[n, g], c_scales[n, g]) for g in range(E_PASSES)]
+            moving = moving + [(s_codes[c, n], s_scales[c, n]) for c in range(J_PASSES)]
+            for j in range(E_PASSES + J_PASSES):
+                nc.tensor.matmul_mx(
+                    out=acc["last", lo][:],
+                    lhsT=stationary[j][0],
+                    lhsT_scale=stationary[j][1],
+                    rhs=moving[j][0][:, lo:hi].bitcast(E4M3X4),
+                    rhs_scale=moving[j][1][:, lo:hi],
+                    start=(j == 0),
+                    stop=(j == E_PASSES + J_PASSES - 1),
+                )
+
         def close_late_tile(n, m):
             if n > 1:
                 qc_passes(n, [m])
@@ -378,7 +402,7 @@ def tile_rocchio_feedback_rescore_s2_kernel(tc, queries, corpus, relevance, sim,
             rest = result[n, m][:, lo:hi] if n == 1 and m in parked else prior_all[:, n * NB + lo : n * NB + hi]
             nc.vector.scalar_tensor_tensor(
                 out=result[n, m][:, lo:hi],
-                in0=acc[n, m][:, lo:hi],
+                in0=acc[n, m][:, lo:hi] if (n, m) in acc else acc["last", lo][:],
                 scalar=gain_col[:, m : m + 1],
                 in1=rest,
                 op0=MULT,
@@ -408,14 +432,14 @@ def tile_rocchio_feedback_rescore_s2_kernel(tc, queries, corpus, relevance, sim,
         load_pair_in_halves("q", 0)
         load_gain()
         load_pair("q", 1)
-        load_piece("s", 0, 0)
         load_pair("q", 2)
-        load_piece("r", 0, 0)
+        load_piece("s", 0, 0)
         load_pair("q", 3)
-        load_piece("s", 1, 0)
+        load_piece("r", 0, 0)
         load_pair("c", 0)
-        load_piece("r", 1, 0)
         load_pair("c", 1)
+        load_piece("s", 1, 0)
+        load_piece("r", 1, 0)
         load_piece("r", 0, 1)
         load_piece("s", 2, 0)
         turn("c", 2, 0, 2)
@@ -444,106 +468,99 @@ def tile_rocchio_feedback_rescore_s2_kernel(tc, queries, corpus, relevance, sim,
         turn("q", 1, 1, 5)
         drain("q", 1, 1, S, 7)
         quant_turned("c", 2, 0)
-        weave("s", 0, 0, S, 0, 128)
+        weave_half("s", 0, 0, 1, S, 0, 128, 0)
         finish_prior(3)
-        weave_half("r", 0, 0, 1, S, 0, 256, 0)
         quant_turned("c", 2, 1)
         quant_turned("c", 3, 0)
         quant_turned("c", 3, 1)
         drain_gain()
         quant_turned("q", 0, 0)
         park_pass(0, 0, 0)
-        weave("s", 0, 0, V, 384, 512)
+        sort("q", 2, V)
         park_pass(1, 0, 1)
         quant_turned("q", 0, 1)
         park_pass(0, 1, 0)
-        weave("s", 0, 0, V, 128, 384)
-        load_piece("r", 2, 0)
+        weave_half("s", 0, 0, 1, V, 128, 256, 0)
         park_pass(1, 1, 1)
-        sort("q", 2, V)
-        turn("q", 2, 0, 6)
-        drain("q", 2, 0, S, 1)
         quant_turned("q", 1, 0)
-        weave_half("r", 0, 0, 0, G, 0, 192, 6)
-        turn("q", 2, 1, 7)
-        drain("q", 2, 1, S, 2)
+        turn("q", 2, 0, 6)
         quant_turned("q", 1, 1)
-        park_pass(2, 0, 2)
-        weave_half("r", 0, 0, 0, S, 192, 256, 6)
-        park(0)
-        load_piece("r", 1, 1)
-        park_pass(3, 0, 3)
-        weave_half("s", 1, 0, 1, S, 0, 256, 3)
-        park(1)
-        park_pass(2, 1, 2)
+        weave_half("s", 0, 0, 0, G, 0, 192, 7)
+        turn("q", 2, 1, 7)
+        weave_half("s", 0, 0, 0, S, 192, 256, 7)
         sort("q", 3, V)
-        park_pass(3, 1, 3)
-        quant_turned("q", 2, 0)
+        load_piece("r", 2, 0)
         turn("q", 3, 0, 4)
-        drain("q", 3, 0, S, 4)
-        quant_turned("q", 2, 1)
-        weave_half("s", 1, 0, 0, G, 0, 192, 2)
+        drain("q", 2, 0, S, 1)
+        park(0)
         turn("q", 3, 1, 5)
+        drain("q", 2, 1, S, 2)
+        park(1)
+        park_pass(2, 0, 2)
+        drain("q", 3, 0, S, 4)
+        quant_half("s", 0, 0, 1)
+        park_pass(3, 0, 3)
         drain("q", 3, 1, S, 5)
-        quant_half("r", 0, 0, 1)
-        park_pass(4, 0, 0)
-        weave_half("s", 1, 0, 0, S, 192, 256, 2)
-        park(2)
-        load_piece("r", 2, 1)
-        park_pass(5, 0, 1)
-        park(3)
-        park_pass(4, 1, 0)
-        quant_piece("s", 0, 0, 0, 512)
-        park_pass(5, 1, 1)
-        quant_turned("q", 3, 0)
+        quant_turned("q", 2, 0)
+        park_pass(2, 1, 2)
+        weave_half("r", 0, 0, 1, S, 0, 256, 3)
+        quant_turned("q", 2, 1)
+        weave_half("r", 0, 0, 0, G, 0, 192, 2)
+        park_pass(3, 1, 3)
+        weave_half("r", 0, 0, 0, S, 192, 256, 2)
+        quant_half("s", 0, 0, 0)
+        load_piece("r", 1, 1)
         turn("c", 0, 0, 6)
-        drain("c", 0, 0, S, 7)
-        quant_turned("q", 3, 1)
-        weave_half("r", 1, 0, 0, G, 0, 192, 5)
+        drain("c", 0, 0, S, 6)
+        park(2)
         turn("c", 0, 1, 7)
         drain("c", 0, 1, S, 1)
-        quant_half("r", 0, 0, 0)
-        park_pass(6, 0, 2)
-        weave_half("r", 1, 0, 0, S, 192, 256, 5)
-        park(4)
-        park_pass(7, 0, 3)
-        weave_half("r", 1, 0, 1, S, 0, 256, 0)
-        park(5)
-        load_piece("s", 0, 1)
-        park_pass(6, 1, 2)
-        quant_half("s", 1, 0, 1)
-        weave_half("r", 0, 1, 0, G, 0, 192, 3)
-        park_pass(7, 1, 3)
-        quant_turned("c", 0, 0)
+        park(3)
         turn("c", 1, 0, 4)
-        drain("c", 1, 0, S, 4)
-        park(6)
+        drain("c", 1, 0, S, 0)
+        quant_turned("q", 3, 0)
         turn("c", 1, 1, 5)
-        drain("c", 1, 1, S, 6)
-        park(7)
-        rs_pass(0, [0, 1, 2, 3], 0)
-        weave_half("r", 0, 1, 0, S, 192, 256, 3)
+        drain("c", 1, 1, S, 7)
+        quant_turned("q", 3, 1)
+        park_pass(4, 0, 0)
+        weave_half("s", 1, 0, 0, S, 0, 256, 5)
+        weave_half("s", 1, 0, 1, V, 0, 256, 4)
+        load_piece("r", 2, 1)
+        park_pass(5, 0, 1)
+        quant_turned("c", 0, 0)
+        park_pass(4, 1, 0)
+        quant_half("r", 0, 0, 0)
+        park_pass(5, 1, 1)
         quant_turned("c", 0, 1)
-        weave_half("r", 0, 1, 1, S, 0, 256, 7)
+        park_pass(6, 0, 2)
+        weave_half("r", 1, 0, 1, S, 128, 256, 1)
         quant_turned("c", 1, 0)
-        load_piece("s", 1, 1)
-        qc_pass(0, [0, 1, 2, 3], 0)
-        weave("s", 2, 0, S, 0, 256)
+        park_pass(7, 0, 3)
+        weave("r", 0, 1, S, 0, 512)
         quant_turned("c", 1, 1)
-        qc_pass(0, [6, 7], 0)
+        weave_half("r", 1, 0, 0, G, 0, 256, 7)
+        park_pass(6, 1, 2)
+        weave("s", 2, 0, S, 0, 256)
+        quant_half("r", 0, 0, 1)
+        weave_half("r", 1, 0, 1, G, 0, 128, 1)
+        load_piece("s", 0, 1)
+        load_piece("s", 1, 1)
+        park_pass(7, 1, 3)
         weave("r", 2, 0, S, 0, 256)
-        quant_half("s", 1, 0, 0)
-        qc_pass(0, [4, 5], 0)
+        park(4)
+        qc_pass(0, [4, 5, 6, 7], 0)
         weave("r", 1, 1, S, 0, 256)
-        quant_half("r", 1, 0, 0)
+        park(5)
+        qc_pass(0, [4, 5, 6, 7], 1)
+        park(6)
+        park(7)
+        qc_pass(0, [0, 1, 2, 3], 0)
+        quant_half("s", 1, 0, 0)
         qc_pass(0, [0, 1, 2, 3], 1)
-        weave("r", 2, 1, S, 0, 256)
+        quant_half("s", 1, 0, 1)
+        rs_pass(0, [0, 1, 2, 3], 0)
+        quant_half("r", 1, 0, 0)
         quant_half("r", 1, 0, 1)
-        qc_pass(0, [6, 7], 1)
-        weave_half("s", 0, 1, 0, S, 0, 256, 0)
-        quant_half("r", 0, 1, 0)
-        qc_pass(0, [4, 5], 1)
-        quant_half("r", 0, 1, 1)
         rs_pass(0, [0, 1, 2, 3], 1)
         weave("s", 2, 0, V, 256, 512)
         load_piece("s", 2, 1)
@@ -554,131 +571,148 @@ def tile_rocchio_feedback_rescore_s2_kernel(tc, queries, corpus, relevance, sim,
         load_two_pieces("s", 2, 2)
         load_quads(3, 0)
         load_quads(3, 1)
+        quant_piece("r", 0, 1, 0, 512)
         rs_pass(0, [4, 5, 6, 7], 0)
+        weave("r", 2, 1, S, 0, 256)
         weave("r", 2, 0, V, 256, 512)
+        weave_half("s", 0, 1, 0, S, 0, 256, 0)
         quant_piece("s", 2, 0, 0, 512)
-        weave("s", 1, 1, S, 0, 512)
         weave("r", 1, 1, V, 256, 512)
-        weave_half("s", 2, 1, 1, S, 0, 256, 3)
         quant_piece("r", 2, 0, 0, 512)
         rs_pass(0, [0, 1, 2, 3], 2)
-        weave("s", 0, 2, S, 0, 512)
+        scale_only(1)
         weave("r", 2, 1, V, 256, 512)
+        scale_only(3)
         quant_piece("r", 1, 1, 0, 512)
         rs_pass(0, [4, 5, 6, 7], 1)
-        weave("s", 1, 2, S, 0, 512)
-        weave_half("s", 0, 1, 1, V, 0, 256, 7)
+        weave_half("s", 1, 1, 1, S, 128, 256, 3)
+        weave_half("s", 0, 1, 1, V, 0, 256, 2)
         quant_piece("r", 2, 1, 0, 512)
         rs_pass(0, [4, 5, 6, 7], 2)
-        quant_half("s", 0, 1, 0)
-        weave_half("s", 2, 1, 0, G, 0, 256, 0)
+        scale_only(5)
         quant_half("s", 0, 1, 1)
+        weave_half("s", 1, 1, 0, G, 0, 256, 2)
+        scale_only(7)
+        quant_half("s", 0, 1, 0)
+        weave_half("s", 1, 1, 1, G, 0, 128, 3)
+        weave_half("s", 2, 1, 0, S, 0, 256, 4)
         finish(0, 0, 0, 512)
-        finish(0, 1, 0, 512)
+        sort("c", 4, S)
         finish(0, 2, 0, 512)
-        finish(0, 3, 0, 512)
         rs_pass(1, [0, 1, 2, 3], 0)
-        quant_piece("s", 1, 1, 0, 512)
-        rs_pass(1, [0, 1, 2, 3], 1)
+        sort("c", 5, S)
         finish(0, 4, 0, 512)
-        finish(0, 5, 0, 512)
+        weave_half("s", 0, 2, 1, S, 128, 256, 7)
         finish(0, 6, 0, 512)
-        finish(0, 7, 0, 512)
         rs_pass(1, [4, 5, 6, 7], 0)
+        weave("s", 1, 2, S, 0, 512)
+        quant_half("s", 1, 1, 0)
+        quant_half("s", 1, 1, 1)
+        rs_pass(1, [0, 1, 2, 3], 1)
+        weave_half("s", 2, 1, 1, V, 0, 256, 5)
         quant_half("s", 2, 1, 0)
         quant_half("s", 2, 1, 1)
+        weave_half("s", 0, 2, 0, G, 0, 256, 5)
         rs_pass(1, [0, 1, 2, 3], 2)
-        sort("c", 4, V)
+        add_prior(0, 1)
+        weave_half("s", 0, 2, 1, G, 0, 128, 7)
         rs_pass(1, [4], 1)
-        sort("c", 5, V)
-        rs_pass(1, [4], 2)
         finish(1, 0, 0, 512)
         store(1, 0, 0, 512)
-        rs_pass(1, [5], 1)
+        rs_pass(1, [4], 2)
         finish(1, 1, 0, 512)
         store(1, 1, 0, 512)
-        rs_pass(1, [5], 2)
+        rs_pass(1, [5], 1)
         finish(1, 2, 0, 512)
         store(1, 2, 0, 512)
+        rs_pass(1, [5], 2)
+        finish(1, 3, 0, 512)
         turn("c", 4, 0, 0)
         drain("c", 4, 0, S, 0)
-        finish(1, 3, 0, 512)
-        store(1, 3, 0, 512)
+        quant_half("s", 0, 2, 0)
         turn("c", 5, 0, 1)
         drain("c", 5, 0, S, 1)
-        quant_piece("s", 0, 2, 0, 512)
+        quant_half("s", 0, 2, 1)
         turn("c", 4, 1, 2)
         drain("c", 4, 1, S, 2)
-        quant_turned("c", 4, 0)
+        add_prior(0, 3)
+        store(1, 3, 0, 512)
         turn("c", 5, 1, 3)
         drain("c", 5, 1, S, 3)
-        quant_turned("c", 5, 0)
+        quant_turned("c", 4, 0)
         rs_pass(1, [6], 1)
-        weave("s", 2, 2, S, 0, 512)
+        weave_half("s", 2, 2, 0, S, 0, 256, 4)
+        quant_turned("c", 5, 0)
+        rs_pass(1, [6], 2)
+        weave_half("s", 2, 2, 1, S, 0, 256, 6)
         finish(1, 4, 0, 512)
         store(1, 4, 0, 512)
-        rs_pass(1, [6], 2)
-        weave("s", 0, 3, S, 0, 512)
-        quant_turned("c", 4, 1)
         rs_pass(1, [7], 1)
-        weave("s", 1, 3, S, 0, 512)
-        quant_turned("c", 5, 1)
+        sort_quads(3, 0, S)
+        quant_turned("c", 4, 1)
         rs_pass(1, [7], 2)
-        finish(1, 5, 0, 512)
-        store(1, 5, 0, 512)
+        weave("s", 0, 3, S, 0, 512)
+        quant_turned("c", 5, 1)
         rs_pass(2, [0, 1, 2, 3], 0)
-        quant_piece("s", 1, 2, 0, 512)
+        sort_quads(3, 1, S)
+        finish(1, 5, 0, 512)
         qc_pass(2, [0, 1, 2, 3], 0)
+        quant_piece("s", 1, 2, 0, 512)
+        qc_pass(2, [0, 1, 2, 3], 1)
         finish(1, 6, 0, 512)
         store(1, 6, 0, 512)
-        qc_pass(2, [0, 1, 2, 3], 1)
-        finish(1, 7, 0, 512)
-        store(1, 7, 0, 512)
         rs_pass(2, [0, 1, 2, 3], 1)
-        quant_piece("s", 2, 2, 0, 512)
+        finish(1, 7, 0, 512)
+        quant_half("s", 2, 2, 0)
+        weave_half("s", 1, 3, 0, G, 0, 256, 4)
+        quant_half("s", 2, 2, 1)
+        weave_half("s", 1, 3, 1, G, 0, 256, 6)
         rs_pass(2, [0, 1, 2, 3], 2)
-        sort_quads(3, 0, V)
-        qc_pass(2, [4], 0)
-        sort_quads(3, 1, V)
-        qc_pass(2, [4], 1)
         turn_quads(3, 0)
-        rs_pass(2, [4], 0)
+        qc_pass(2, [4], 0)
         pair_quads(3, 0, S)
         finish(2, 0, 0, 512)
         store(2, 0, 0, 512)
-        rs_pass(2, [4], 1)
+        qc_pass(2, [4], 1)
         weave("s", 2, 3, S, 0, 512)
         finish(2, 1, 0, 512)
         store(2, 1, 0, 512)
-        rs_pass(2, [4], 2)
+        rs_pass(2, [4], 0)
         finish(2, 2, 0, 512)
         store(2, 2, 0, 512)
-        qc_pass(2, [5], 0)
+        rs_pass(2, [4], 1)
         finish(2, 3, 0, 512)
         store(2, 3, 0, 512)
+        rs_pass(2, [4], 2)
+        add_prior(0, 5)
+        store(1, 5, 0, 512)
+        qc_pass(2, [5], 0)
+        add_prior(0, 7)
+        store(1, 7, 0, 512)
         qc_pass(2, [5], 1)
         quant_piece("s", 0, 3, 0, 512)
         rs_pass(2, [5], 0)
         turn_quads(3, 1)
         rs_pass(2, [5], 1)
         pair_quads(3, 1, S)
-        quant_piece("s", 1, 3, 0, 512)
+        quant_half("s", 1, 3, 0)
         rs_pass(2, [5], 2)
-        quant_quads(3, 0)
+        quant_half("s", 1, 3, 1)
         qc_pass(2, [6], 0)
+        quant_quads(3, 0)
+        qc_pass(2, [6], 1)
         finish(2, 4, 0, 512)
         store(2, 4, 0, 512)
-        qc_pass(2, [6], 1)
-        quant_piece("s", 2, 3, 0, 512)
         rs_pass(2, [6], 0)
+        quant_piece("s", 2, 3, 0, 512)
+        rs_pass(2, [6], 1)
         finish(2, 5, 0, 512)
         store(2, 5, 0, 512)
-        rs_pass(2, [6], 1)
-        quant_quads(3, 1)
         rs_pass(2, [6], 2)
+        quant_quads(3, 1)
+        qc_pass(2, [7], 0)
         finish(2, 6, 0, 512)
         store(2, 6, 0, 512)
-        qc_pass(2, [7], 0)
         qc_pass(2, [7], 1)
         rs_pass(2, [7], 0)
         rs_pass(2, [7], 1)
@@ -719,12 +753,9 @@ def tile_rocchio_feedback_rescore_s2_kernel(tc, queries, corpus, relevance, sim,
         rs_pass(3, [6], 2)
         finish(3, 6, 0, 512)
         store(3, 6, 0, 512)
-        qc_pass(3, [7], 0)
-        qc_pass(3, [7], 1)
-        rs_pass(3, [7], 0)
-        rs_pass(3, [7], 1)
-        rs_pass(3, [7], 2)
+        last_part(0, 256, 7)
         finish(3, 7, 0, 256)
         store(3, 7, 0, 256)
+        last_part(256, 512, 0)
         finish(3, 7, 256, 512)
         store(3, 7, 256, 512)

@@ -20,14 +20,17 @@ P = 128
 E_PASSES = E // 512
 J_PASSES = J // 512
 NB = 512
+HALF = NB // 2
+QUARTER = NB // 4
 TILES = range(M // P)
-EARLY, LATE = range(0, 4), range(4, 8)
-STRIPS = N // NB
-PAIR = 2 * P
+EARLY, LATE = TILES[:4], TILES[4:]
+PARKED, LAST = 1, 3
 PASS_WORDS = 256
 QUAD = 32
 STRIP_ROWS = NB // (2 * QUAD)
 ALIGN = 256
+SHORT_RUN = 192
+V, S, G = "vector", "scalar", "gpsimd"
 
 
 def tile_rocchio_feedback_rescore_s2_kernel(tc, queries, corpus, relevance, sim, gain, prior, out):
@@ -38,7 +41,6 @@ def tile_rocchio_feedback_rescore_s2_kernel(tc, queries, corpus, relevance, sim,
         stage = ctx.enter_context(tc.tile_pool(name="stage", bufs=1))
         psum = ctx.enter_context(tc.psum_pool(name="psum", bufs=1))
         ctx.enter_context(tc.manual_schedule())
-        V, S, G = "vector", "scalar", "gpsimd"
 
         ident = keep.tile([P, P], F32, name="ident")
         ident_bf = keep.tile([P, P], BF16, name="ident_bf")
@@ -55,8 +57,8 @@ def tile_rocchio_feedback_rescore_s2_kernel(tc, queries, corpus, relevance, sim,
 
         by_pair = "p (a g r) -> p a g r"
         by_pass = "p (c m) -> p c m"
-        q_codes = operand_tile(keep, E_PASSES * M, U32, "q_codes").rearrange(by_pair, g=E_PASSES, r=PAIR)
-        q_scales = operand_tile(keep, E_PASSES * M, U8, "q_scales").rearrange(by_pair, g=E_PASSES, r=PAIR)
+        q_codes = operand_tile(keep, E_PASSES * M, U32, "q_codes").rearrange(by_pair, g=E_PASSES, r=HALF)
+        q_scales = operand_tile(keep, E_PASSES * M, U8, "q_scales").rearrange(by_pair, g=E_PASSES, r=HALF)
         r_codes = operand_tile(keep, J_PASSES * M, U32, "r_codes").rearrange(by_pass, c=J_PASSES)
         r_scales = operand_tile(keep, J_PASSES * M, U8, "r_scales").rearrange(by_pass, c=J_PASSES)
 
@@ -68,45 +70,50 @@ def tile_rocchio_feedback_rescore_s2_kernel(tc, queries, corpus, relevance, sim,
             "r": relevance.rearrange("(c p i) m -> c p i m", p=P, i=4),
             "s": sim.rearrange("(c p i) n -> c p i n", p=P, i=4),
         }
-        pair_raw, piece_raw, half_raw = {}, {}, {}
+        quad_view = corpus.rearrange("(n a i) (g q e) -> n g q i a e", a=NB // QUAD, i=QUAD, g=E_PASSES, q=P // QUAD)
+        pair_raw, pass_raw, piece_raw, quad_raw = {}, {}, {}, {}
+
+        def pair_buffer(width=E):
+            return raw.tile([P, 2, width], BF16, name="pair_raw_t", bufs=8, align_bytes=ALIGN)
 
         def load_pair(x, a):
-            pair_raw[x, a] = raw.tile([P, 2, E], BF16, name="pair_raw_t", bufs=8, align_bytes=ALIGN)
+            pair_raw[x, a] = pair_buffer()
             nc.sync.dma_start(out=pair_raw[x, a][:], in_=pair_view[x][a])
 
-        def load_prior():
-            for quad in range(P // QUAD):
-                nc.scalar.dma_start(
-                    out=prior_raw[quad * QUAD : (quad + 1) * QUAD, :], in_=prior.rearrange("(p i) -> p i", p=QUAD)
-                )
-
-        def load_gain():
-            nc.sync.dma_start(out=gain_rows[0 : len(TILES), :], in_=gain.rearrange("(m p) -> m p", p=P))
-
-        def load_pair_in_halves(x, a):
-            pair_raw[x, a] = raw.tile([P, 2, E], BF16, name="pair_raw_t", bufs=8, align_bytes=ALIGN)
-            for t in range(2):
-                nc.sync.dma_start(out=pair_raw[x, a][:, t, :], in_=pair_view[x][a, :, t, :])
+        def load_pair_by_pass(x, a):
+            for g in range(E_PASSES):
+                pass_raw[x, a, g] = pair_buffer(NB)
+                nc.sync.dma_start(out=pass_raw[x, a, g][:], in_=pair_view[x][a, :, :, g * NB : (g + 1) * NB])
 
         def load_piece(x, c, b):
             piece = raw.tile([P, 4, NB], BF16, name="piece_raw_t", bufs=6, align_bytes=ALIGN)
             nc.sync.dma_start(out=piece[:], in_=piece_view[x][c, :, :, b * NB : (b + 1) * NB])
             piece_raw[x, c, b] = piece[:]
 
-        def load_piece_in_halves(x, c, b):
-            piece = raw.tile([P, 2, 4, PAIR], BF16, name="piece_raw_t", bufs=6, align_bytes=ALIGN)
+        def load_two_pieces(c):
+            both = raw.tile([P, 4, 2 * NB], BF16, name="two_pieces_raw_t", bufs=J_PASSES, align_bytes=ALIGN)
+            nc.sync.dma_start(out=both[:], in_=piece_view["s"][c, :, :, 2 * NB :])
             for h in range(2):
-                nc.sync.dma_start(out=piece[:, h], in_=piece_view[x][c, :, :, b * NB + h * PAIR : b * NB + (h + 1) * PAIR])
-            half_raw[x, c, b] = piece
+                piece_raw["s", c, 2 + h] = both[:, :, h * NB : (h + 1) * NB]
 
-        def load_two_pieces(x, c, b):
-            both = raw.tile([P, 4, 2 * NB], BF16, name="two_pieces_raw_t", bufs=3, align_bytes=ALIGN)
-            nc.sync.dma_start(out=both[:], in_=piece_view[x][c, :, :, b * NB : (b + 2) * NB])
-            for h in range(2):
-                piece_raw[x, c, b + h] = both[:, :, h * NB : (h + 1) * NB]
+        def load_quads(g):
+            quad_raw[g] = pair_buffer()
+            rows = quad_raw[g][:].rearrange("p t e -> p (t e)").rearrange("p (a e) -> p a e", a=NB // QUAD)
+            for q in (0, 2, 1, 3):
+                nc.sync.dma_start(out=rows[q * QUAD : (q + 1) * QUAD], in_=quad_view[LAST, g, q])
+
+        def load_prior():
+            for q in range(P // QUAD):
+                nc.sync.dma_start(out=prior_raw[q * QUAD : (q + 1) * QUAD, :], in_=prior.rearrange("(p i) -> p i", p=QUAD))
+
+        def load_gain():
+            nc.sync.dma_start(out=gain_rows[0 : len(TILES), :], in_=gain.rearrange("(m p) -> m p", p=P))
 
         def bank_tile(bank, shape=(P, NB), dtype=F32):
             return psum.tile(list(shape), dtype, name="bank_t", tag=f"bank{bank}")
+
+        def slot_tile(slot):
+            return stage.tile([P, HALF * 4], BF16, name="slot_t", tag=f"slot{slot}", align_bytes=ALIGN)
 
         def copy(engine, dst, src):
             if engine == S:
@@ -116,10 +123,17 @@ def tile_rocchio_feedback_rescore_s2_kernel(tc, queries, corpus, relevance, sim,
             else:
                 nc.vector.tensor_copy(out=dst, in_=src)
 
-        pair_sorted, turned, drained = {}, {}, {}
+        def quantize(codes, scales, values):
+            nc.vector.quantize_mx(out=codes, scales=scales, in_=values)
 
-        def sort(x, a, engine=V):
-            pair_sorted[x, a] = raw.tile([P, 4, 2, P], F32, name="sorted_t", bufs=2, align_bytes=ALIGN)
+        pair_sorted, turned, drained = {}, {}, {}
+        c_codes, c_scales, s_codes, s_scales = {}, {}, {}, {}
+
+        def sorted_buffer():
+            return raw.tile([P, 4, 2, P], F32, name="sorted_t", bufs=2, align_bytes=ALIGN)
+
+        def sort(x, a, engine):
+            pair_sorted[x, a] = sorted_buffer()
             words = pair_raw[x, a][:].rearrange("p t e -> p (t e)").bitcast(F32)
             copy(engine, pair_sorted[x, a][:], words.rearrange("p (s w u) -> p s u w", s=4, u=2))
 
@@ -129,63 +143,32 @@ def tile_rocchio_feedback_rescore_s2_kernel(tc, queries, corpus, relevance, sim,
                 for u in range(2):
                     if (x, a) in pair_sorted:
                         words = pair_sorted[x, a][:, E_PASSES * t + g, u, :]
+                    elif (x, a, g) in pass_raw:
+                        words = pass_raw[x, a, g][:, t, :].bitcast(F32)[:, u::2]
                     else:
                         words = pair_raw[x, a][:, t, :].bitcast(F32)[:, PASS_WORDS * g + u : PASS_WORDS * (g + 1) : 2]
-                    slot = 2 * t + u
-                    nc.tensor.transpose(turned[x, a, g][:, slot * P : (slot + 1) * P], words, ident[:])
+                    quarter = 2 * t + u
+                    nc.tensor.transpose(turned[x, a, g][:, quarter * P : (quarter + 1) * P], words, ident[:])
 
-        def slot_tile(slot):
-            return stage.tile([P, PAIR * 4], BF16, name="slot_t", tag=f"slot{slot}", align_bytes=ALIGN)
-
-        def drain(x, a, g, engine, slot):
+        def drain(x, a, g, slot):
             drained[x, a, g] = slot_tile(slot)
             copy(
-                engine,
+                S,
                 drained[x, a, g][:].bitcast(F32).rearrange("p (r s) -> p r s", s=4),
                 turned[x, a, g][:].rearrange("p (s r) -> p r s", s=4),
             )
 
-        quad_view = corpus.rearrange("(n a i) (g q e) -> n g q i a e", a=NB // QUAD, i=QUAD, g=E_PASSES, q=P // QUAD)
-        quad_raw, quad_sorted, quad_turned, quad_ready = {}, {}, {}, {}
+        def turn_pair(x, a, bank):
+            for g in range(E_PASSES):
+                turn(x, a, g, bank + g)
 
-        def load_quads(n, g):
-            quad_raw[n, g] = raw.tile([P, 2, E], BF16, name="pair_raw_t", bufs=8, align_bytes=ALIGN)
-            rows = quad_raw[n, g][:].rearrange("p t e -> p (t e)").rearrange("p (a e) -> p a e", a=NB // QUAD)
-            for q in (0, 2, 1, 3):
-                nc.sync.dma_start(out=rows[q * QUAD : (q + 1) * QUAD], in_=quad_view[n, g, q])
+        def drain_pair(x, a, slots):
+            for g in range(E_PASSES):
+                drain(x, a, g, slots[g])
 
-        def sort_quads(n, g, engine):
-            quad_sorted[n, g] = raw.tile([P, 4, 2, P], F32, name="sorted_t", bufs=2, align_bytes=ALIGN)
-            words = quad_raw[n, g][:].rearrange("p t e -> p (t e)").bitcast(F32)
-            copy(
-                engine,
-                quad_sorted[n, g][:].rearrange("p s u w -> p (s u w)").rearrange("p (a u j) -> p a u j", u=2, j=QUAD),
-                words.rearrange("p (a j u) -> p a u j", u=2, j=QUAD),
-            )
-
-        def turn_quads(n, g):
-            quad_turned[n, g] = raw.tile([P, 2, E], BF16, name="pair_raw_t", bufs=8, align_bytes=ALIGN)
-            nc.vector.transpose(
-                out=quad_turned[n, g][:].rearrange("p t e -> p (t e)").bitcast(F32),
-                in_=quad_sorted[n, g][:].rearrange("p s u w -> p (s u w)"),
-            )
-
-        def pair_quads(n, g, engine):
-            quad_ready[n, g] = stage.tile([P, NB, 4], BF16, name="woven_t", bufs=4, align_bytes=ALIGN)
-            copy(
-                engine,
-                quad_ready[n, g][:].rearrange("p w i -> p (w i)").bitcast(F32).rearrange("p (a i u) -> p a i u", i=QUAD, u=2),
-                quad_turned[n, g][:].rearrange("p t e -> p (t e)").bitcast(F32).rearrange("p (a u i) -> p a i u", i=QUAD, u=2),
-            )
-
-        def quant_quads(n, g):
+        def new_corpus_operand(n, g):
             c_codes[n, g] = operand_tile(stage, NB, U32, "c_codes_t", 4)
             c_scales[n, g] = operand_tile(stage, NB, U8, "c_scales_t", 4)
-            nc.vector.quantize_mx(
-                out=c_codes[n, g].bitcast(E4M3X4), scales=c_scales[n, g], in_=quad_ready[n, g][:].rearrange("p w i -> p (w i)")
-            )
-
-        c_codes, c_scales, s_codes, s_scales = {}, {}, {}, {}
 
         def quant_turned(x, a, g):
             if x == "q":
@@ -193,118 +176,116 @@ def tile_rocchio_feedback_rescore_s2_kernel(tc, queries, corpus, relevance, sim,
             else:
                 n, h = divmod(a, 2)
                 if h == 0:
-                    c_codes[n, g] = operand_tile(stage, NB, U32, "c_codes_t", 4)
-                    c_scales[n, g] = operand_tile(stage, NB, U8, "c_scales_t", 4)
-                cols = slice(h * PAIR, (h + 1) * PAIR)
+                    new_corpus_operand(n, g)
+                cols = slice(h * HALF, (h + 1) * HALF)
                 codes, scales = c_codes[n, g][:, cols], c_scales[n, g][:, cols]
-            nc.vector.quantize_mx(out=codes.bitcast(E4M3X4), scales=scales, in_=drained[x, a, g][:])
+            quantize(codes.bitcast(E4M3X4), scales, drained[x, a, g][:])
 
         def quant_pair(x, a):
             for g in range(E_PASSES):
                 quant_turned(x, a, g)
 
-        def quant_corpus(n, g):
-            for h in range(2):
-                quant_turned("c", 2 * n + h, g)
+        quad_sorted, quad_turned, quad_ready = {}, {}, {}
 
-        woven = {}
+        def woven_buffer():
+            return stage.tile([P, NB, 4], BF16, name="woven_t", bufs=4, align_bytes=ALIGN)
 
-        def weave(x, c, b, engine, lo=0, hi=NB):
-            if (x, c, b) not in woven:
-                woven[x, c, b] = stage.tile([P, NB, 4], BF16, name="woven_t", bufs=4, align_bytes=ALIGN)
-            if (x, c, b) in half_raw:
-                h = lo // PAIR
-                rows = half_raw[x, c, b][:, h, :, lo - h * PAIR : hi - h * PAIR]
-            else:
-                rows = piece_raw[x, c, b][:, :, lo:hi]
+        def sort_quads(g):
+            quad_sorted[g] = sorted_buffer()
+            words = quad_raw[g][:].rearrange("p t e -> p (t e)").bitcast(F32)
             copy(
-                engine,
-                woven[x, c, b][:, lo:hi, :].rearrange("p (w j) i -> p w i j", j=4),
-                rows.rearrange("p i (w j) -> p w i j", j=4),
+                S,
+                quad_sorted[g][:].rearrange("p s u w -> p (s u w)").rearrange("p (a u j) -> p a u j", u=2, j=QUAD),
+                words.rearrange("p (a j u) -> p a u j", u=2, j=QUAD),
             )
 
-        half_woven = {}
+        def turn_quads(g):
+            quad_turned[g] = pair_buffer()
+            nc.vector.transpose(
+                out=quad_turned[g][:].rearrange("p t e -> p (t e)").bitcast(F32),
+                in_=quad_sorted[g][:].rearrange("p s u w -> p (s u w)"),
+            )
 
-        def weave_half(x, c, b, h, engine, lo, hi, slot):
-            if (x, c, b, h) not in half_woven:
-                half_woven[x, c, b, h] = slot_tile(slot)
-            dst = half_woven[x, c, b, h][:].rearrange("p (w i) -> p w i", i=4)[:, lo:hi, :]
-            src = piece_raw[x, c, b][:, :, h * PAIR + lo : h * PAIR + hi]
+        def pair_quads(g):
+            quad_ready[g] = woven_buffer()
+            ready = quad_ready[g][:].rearrange("p w i -> p (w i)").bitcast(F32)
+            words = quad_turned[g][:].rearrange("p t e -> p (t e)").bitcast(F32)
+            copy(S, ready.rearrange("p (a i u) -> p a i u", i=QUAD, u=2), words.rearrange("p (a u i) -> p a i u", i=QUAD, u=2))
+
+        def quant_quads(g):
+            new_corpus_operand(LAST, g)
+            quantize(c_codes[LAST, g].bitcast(E4M3X4), c_scales[LAST, g], quad_ready[g][:].rearrange("p w i -> p (w i)"))
+
+        woven, half_woven = {}, {}
+
+        def interleave(engine, dst, src):
             if engine == G:
                 copy(engine, dst, src.rearrange("p i w -> p w i"))
             else:
                 copy(engine, dst.rearrange("p (w j) i -> p w i j", j=4), src.rearrange("p i (w j) -> p w i j", j=4))
 
-        def quant_half(x, c, b, h):
-            if x == "r":
-                cols = slice(b * NB + h * PAIR, b * NB + (h + 1) * PAIR)
-                codes, scales = r_codes[:, c, cols].bitcast(E5M2X4), r_scales[:, c, cols]
-            else:
-                if (c, b) not in s_codes:
-                    s_codes[c, b] = operand_tile(stage, NB, U32, "s_codes_t", 7)
-                    s_scales[c, b] = operand_tile(stage, NB, U8, "s_scales_t", 7)
-                cols = slice(h * PAIR, (h + 1) * PAIR)
-                codes, scales = s_codes[c, b][:, cols].bitcast(E4M3X4), s_scales[c, b][:, cols]
-            nc.vector.quantize_mx(out=codes, scales=scales, in_=half_woven[x, c, b, h][:])
+        def weave(x, c, b, engine, lo=0, hi=NB):
+            if (x, c, b) not in woven:
+                woven[x, c, b] = woven_buffer()
+            interleave(engine, woven[x, c, b][:, lo:hi, :], piece_raw[x, c, b][:, :, lo:hi])
 
-        def weave_shared(x, c, b, share):
-            weave(x, c, b, S, 0, share)
-            weave(x, c, b, V, share, NB)
+        def weave_half(x, c, b, h, engine, slot, lo=0, hi=HALF):
+            if (x, c, b, h) not in half_woven:
+                half_woven[x, c, b, h] = slot_tile(slot)
+            dst = half_woven[x, c, b, h][:].rearrange("p (w i) -> p w i", i=4)
+            interleave(engine, dst[:, lo:hi, :], piece_raw[x, c, b][:, :, h * HALF + lo : h * HALF + hi])
 
-        def quant_piece(x, c, b, lo=0, hi=NB):
+        def piece_operand(x, c, b, lo, hi):
             if x == "r":
                 cols = slice(b * NB + lo, b * NB + hi)
-                codes, scales = r_codes[:, c, cols].bitcast(E5M2X4), r_scales[:, c, cols]
-            else:
+                return r_codes[:, c, cols].bitcast(E5M2X4), r_scales[:, c, cols]
+            if (c, b) not in s_codes:
                 s_codes[c, b] = operand_tile(stage, NB, U32, "s_codes_t", 7)
                 s_scales[c, b] = operand_tile(stage, NB, U8, "s_scales_t", 7)
-                codes, scales = s_codes[c, b].bitcast(E4M3X4), s_scales[c, b]
-            nc.vector.quantize_mx(out=codes, scales=scales, in_=woven[x, c, b][:, lo:hi, :].rearrange("p w i -> p (w i)"))
+            return s_codes[c, b][:, lo:hi].bitcast(E4M3X4), s_scales[c, b][:, lo:hi]
 
-        acc, passes_done = {}, {}
+        def quant_piece(x, c, b):
+            quantize(*piece_operand(x, c, b, 0, NB), woven[x, c, b][:].rearrange("p w i -> p (w i)"))
 
-        parked = set()
+        def quant_half(x, c, b, h):
+            quantize(*piece_operand(x, c, b, h * HALF, (h + 1) * HALF), half_woven[x, c, b, h][:])
 
-        def park_pass(m, g, bank, lo=0, hi=NB):
-            if m not in parked:
-                acc["park", m] = bank_tile(bank)
-                parked.add(m)
+        def quant_halves(x, c, b, order=(0, 1)):
+            for h in order:
+                quant_half(x, c, b, h)
+
+        acc, parked_acc, last_acc, passes_done = {}, {}, {}, {}
+
+        def mx_pass(dst, stationary, moving, start, stop):
+            nc.tensor.matmul_mx(
+                out=dst, lhsT=stationary[0], lhsT_scale=stationary[1], rhs=moving[0], rhs_scale=moving[1], start=start, stop=stop
+            )
+
+        def q_operand(m, g):
             a, h = divmod(m, 2)
             cols = slice(h * P, (h + 1) * P)
-            nc.tensor.matmul_mx(
-                out=acc["park", m][:, lo:hi],
-                lhsT=q_codes[:, a, g, cols].bitcast(E4M3X4),
-                lhsT_scale=q_scales[:, a, g, cols],
-                rhs=c_codes[1, g][:, lo:hi].bitcast(E4M3X4),
-                rhs_scale=c_scales[1, g][:, lo:hi],
-                start=(g == 0),
-                stop=(g == E_PASSES - 1),
-            )
+            return q_codes[:, a, g, cols].bitcast(E4M3X4), q_scales[:, a, g, cols]
 
-        def mx_pass(n, m, lhsT, lhsT_scale, rhs, rhs_scale):
-            passes = J_PASSES if n == 1 and m in parked else E_PASSES + J_PASSES
+        def r_operand(m, c):
+            cols = slice(m * P, (m + 1) * P)
+            return r_codes[:, c, cols].bitcast(E5M2X4), r_scales[:, c, cols]
+
+        def c_operand(n, g, lo=0, hi=NB):
+            return c_codes[n, g][:, lo:hi].bitcast(E4M3X4), c_scales[n, g][:, lo:hi]
+
+        def s_operand(n, c, lo=0, hi=NB):
+            return s_codes[c, n][:, lo:hi].bitcast(E4M3X4), s_scales[c, n][:, lo:hi]
+
+        def tile_pass(n, m, stationary, moving):
             if (n, m) not in acc:
                 acc[n, m] = bank_tile(m)
-                passes_done[n, m] = 0
-            passes_done[n, m] = passes_done[n, m] + 1
-            nc.tensor.matmul_mx(
-                out=acc[n, m][:],
-                lhsT=lhsT,
-                lhsT_scale=lhsT_scale,
-                rhs=rhs,
-                rhs_scale=rhs_scale,
-                start=(passes_done[n, m] == 1),
-                stop=(passes_done[n, m] == passes),
-            )
+            passes_done[n, m] = passes_done.get((n, m), 0) + 1
+            passes = J_PASSES if n == PARKED else E_PASSES + J_PASSES
+            mx_pass(acc[n, m][:], stationary, moving, passes_done[n, m] == 1, passes_done[n, m] == passes)
 
         def qc_pass(n, tiles, g):
             for m in tiles:
-                a, h = divmod(m, 2)
-                cols = slice(h * P, (h + 1) * P)
-                mx_pass(
-                    n, m, q_codes[:, a, g, cols].bitcast(E4M3X4), q_scales[:, a, g, cols],
-                    c_codes[n, g].bitcast(E4M3X4), c_scales[n, g],
-                )
+                tile_pass(n, m, q_operand(m, g), c_operand(n, g))
 
         def qc_passes(n, tiles):
             for g in range(E_PASSES):
@@ -312,41 +293,29 @@ def tile_rocchio_feedback_rescore_s2_kernel(tc, queries, corpus, relevance, sim,
 
         def rs_pass(n, tiles, c):
             for m in tiles:
-                cols = slice(m * P, (m + 1) * P)
-                mx_pass(
-                    n, m, r_codes[:, c, cols].bitcast(E5M2X4), r_scales[:, c, cols],
-                    s_codes[c, n].bitcast(E4M3X4), s_scales[c, n],
-                )
+                tile_pass(n, m, r_operand(m, c), s_operand(n, c))
 
-        def last_part(lo, hi, bank):
-            n, m = STRIPS - 1, TILES[-1]
-            a, h = divmod(m, 2)
-            acc["last", lo] = bank_tile(bank, (P, hi - lo))
-            stationary = [
-                (q_codes[:, a, g, h * P : (h + 1) * P].bitcast(E4M3X4), q_scales[:, a, g, h * P : (h + 1) * P])
-                for g in range(E_PASSES)
-            ] + [
-                (r_codes[:, c, m * P : (m + 1) * P].bitcast(E5M2X4), r_scales[:, c, m * P : (m + 1) * P])
-                for c in range(J_PASSES)
-            ]
-            moving = [(c_codes[n, g], c_scales[n, g]) for g in range(E_PASSES)]
-            moving = moving + [(s_codes[c, n], s_scales[c, n]) for c in range(J_PASSES)]
-            for j in range(E_PASSES + J_PASSES):
-                nc.tensor.matmul_mx(
-                    out=acc["last", lo][:],
-                    lhsT=stationary[j][0],
-                    lhsT_scale=stationary[j][1],
-                    rhs=moving[j][0][:, lo:hi].bitcast(E4M3X4),
-                    rhs_scale=moving[j][1][:, lo:hi],
-                    start=(j == 0),
-                    stop=(j == E_PASSES + J_PASSES - 1),
-                )
-
-        def close_late_tile(n, m):
-            if n > 1:
+        def close_tile(n, m, first=0):
+            if n != PARKED:
                 qc_passes(n, [m])
-            for c in range(0 if n > 1 else 1, J_PASSES):
+            for c in range(first, J_PASSES):
                 rs_pass(n, [m], c)
+
+        def park_passes(a, bank):
+            for g in range(E_PASSES):
+                for h in range(2):
+                    m = 2 * a + h
+                    if g == 0:
+                        parked_acc[m] = bank_tile(bank + h)
+                    mx_pass(parked_acc[m][:], q_operand(m, g), c_operand(PARKED, g), g == 0, g == E_PASSES - 1)
+
+        def close_last_half(h, bank):
+            m, lo, hi = TILES[-1], h * HALF, (h + 1) * HALF
+            last_acc[h] = bank_tile(bank, (P, HALF))
+            operands = [(q_operand(m, g), c_operand(LAST, g, lo, hi)) for g in range(E_PASSES)]
+            operands = operands + [(r_operand(m, c), s_operand(LAST, c, lo, hi)) for c in range(J_PASSES)]
+            for j, (stationary, moving) in enumerate(operands):
+                mx_pass(last_acc[h][:], stationary, moving, j == 0, j == len(operands) - 1)
 
         gain_turned = {}
 
@@ -360,13 +329,13 @@ def tile_rocchio_feedback_rescore_s2_kernel(tc, queries, corpus, relevance, sim,
         def turn_prior():
             nc.vector.transpose(out=prior_turned[:], in_=prior_raw[:].bitcast(F32))
 
-        def spread_prior(n):
+        def repeat_prior(n):
             rows = slice(n * STRIP_ROWS, (n + 1) * STRIP_ROWS)
             nc.vector.tensor_copy(
                 out=prior_repeated[:, rows, :], in_=prior_turned[:, rows].unsqueeze(2).to_broadcast([P, STRIP_ROWS, QUAD])
             )
 
-        def finish_prior(n):
+        def spread_prior(n):
             rows = slice(n * STRIP_ROWS, (n + 1) * STRIP_ROWS)
             nc.vector.transpose(
                 out=prior_words[:, rows, :].rearrange("p b i -> p (b i)"),
@@ -377,48 +346,39 @@ def tile_rocchio_feedback_rescore_s2_kernel(tc, queries, corpus, relevance, sim,
 
         result, result_01 = {}, {}
 
-        def result_pair(m):
-            if m not in result_01:
-                result_01[m] = stage.tile([P, 2 * NB], F32, name="result_01_t", bufs=len(TILES))
-                result[0, m], result[1, m] = result_01[m][:, :NB], result_01[m][:, NB:]
+        def result_tile(n, m):
+            if (n, m) not in result:
+                if n < 2:
+                    result_01[m] = stage.tile([P, 2 * NB], F32, name="result_01_t", bufs=len(TILES))
+                    result[0, m], result[1, m] = result_01[m][:, :NB], result_01[m][:, NB:]
+                else:
+                    single = stage.tile([P, NB], F32, name="result_t", bufs=len(TILES))
+                    result[n, m] = single[:]
+            return result[n, m]
 
-        def park(m):
-            result_pair(m)
-            nc.vector.scalar_tensor_tensor(
-                out=result[1, m], in0=acc["park", m][:], scalar=gain_col[:, m : m + 1], in1=prior_all[:, NB : 2 * NB],
-                op0=MULT, op1=ADD,
-            )
+        def scale_and_add(dst, sums, m, rest):
+            nc.vector.scalar_tensor_tensor(out=dst, in0=sums, scalar=gain_col[:, m : m + 1], in1=rest, op0=MULT, op1=ADD)
 
-        def park_scaled(m):
-            result_pair(m)
-            nc.scalar.activation(out=result[1, m], in_=acc["park", m][:], func=COPY, scale=gain_col[:, m : m + 1])
+        def strip_prior(n, lo=0, hi=NB):
+            return prior_all[:, n * NB + lo : n * NB + hi]
 
-        def finish(n, m, lo=0, hi=NB):
-            if n < 2:
-                result_pair(m)
-            elif lo == 0:
-                single = stage.tile([P, NB], F32, name="result_t", bufs=len(TILES))
-                result[n, m] = single[:]
-            rest = result[n, m][:, lo:hi] if n == 1 and m in parked else prior_all[:, n * NB + lo : n * NB + hi]
-            nc.vector.scalar_tensor_tensor(
-                out=result[n, m][:, lo:hi],
-                in0=acc[n, m][:, lo:hi] if (n, m) in acc else acc["last", lo][:],
-                scalar=gain_col[:, m : m + 1],
-                in1=rest,
-                op0=MULT,
-                op1=ADD,
-            )
+        def park(tiles):
+            for m in tiles:
+                scale_and_add(result_tile(PARKED, m), parked_acc[m][:], m, strip_prior(PARKED))
+
+        def finish(n, m):
+            dst = result_tile(n, m)
+            scale_and_add(dst, acc[n, m][:], m, dst if n == PARKED else strip_prior(n))
 
         def scale_only(m):
-            result_pair(m)
-            nc.scalar.activation(out=result[0, m], in_=acc[0, m][:], func=COPY, scale=gain_col[:, m : m + 1])
+            nc.scalar.activation(out=result_tile(0, m), in_=acc[0, m][:], func=COPY, scale=gain_col[:, m : m + 1])
 
-        def add_prior(n, m):
-            nc.vector.tensor_tensor(out=result[n, m], in0=result[n, m], in1=prior_all[:, n * NB : (n + 1) * NB], op=ADD)
+        def add_prior(m):
+            nc.vector.tensor_tensor(out=result[0, m], in0=result[0, m], in1=strip_prior(0), op=ADD)
 
         def store(n, m, lo=0, hi=NB):
             rows = slice(m * P, (m + 1) * P)
-            if n == 1:
+            if n == PARKED:
                 nc.sync.dma_start(out=out[rows, : 2 * NB], in_=result_01[m][:])
             else:
                 nc.sync.dma_start(out=out[rows, n * NB + lo : n * NB + hi], in_=result[n, m][:, lo:hi])
@@ -426,10 +386,11 @@ def tile_rocchio_feedback_rescore_s2_kernel(tc, queries, corpus, relevance, sim,
         make_identity(nc, ident[:])
         nc.gpsimd.memset(gain_rows[:], 0.0)
         make_identity(nc, ident_bf[:])
-        load_pair_in_halves("c", 2)
+
+        load_pair_by_pass("c", 2)
         load_prior()
-        load_pair_in_halves("c", 3)
-        load_pair_in_halves("q", 0)
+        load_pair("c", 3)
+        load_pair("q", 0)
         load_gain()
         load_pair("q", 1)
         load_pair("q", 2)
@@ -437,325 +398,220 @@ def tile_rocchio_feedback_rescore_s2_kernel(tc, queries, corpus, relevance, sim,
         load_pair("q", 3)
         load_piece("r", 0, 0)
         load_pair("c", 0)
+
+        turn_prior()
+        repeat_prior(1)
+        repeat_prior(0)
+        spread_prior(1)
+        spread_prior(0)
+        repeat_prior(2)
+        repeat_prior(3)
+        spread_prior(2)
+
+        turn_pair("c", 2, 2)
         load_pair("c", 1)
         load_piece("s", 1, 0)
         load_piece("r", 1, 0)
         load_piece("r", 0, 1)
         load_piece("s", 2, 0)
-        turn("c", 2, 0, 2)
-        drain("c", 2, 0, S, 0)
-        turn_prior()
-        turn("c", 2, 1, 3)
-        drain("c", 2, 1, S, 1)
-        spread_prior(1)
-        turn("c", 3, 0, 4)
-        drain("c", 3, 0, S, 2)
-        spread_prior(0)
-        turn("c", 3, 1, 5)
-        drain("c", 3, 1, S, 3)
-        finish_prior(1)
-        turn("q", 0, 0, 6)
-        drain("q", 0, 0, S, 4)
-        finish_prior(0)
-        turn("q", 0, 1, 7)
-        drain("q", 0, 1, S, 5)
-        spread_prior(2)
-        turn_gain(0)
-        spread_prior(3)
-        turn("q", 1, 0, 4)
-        drain("q", 1, 0, S, 6)
-        finish_prior(2)
-        turn("q", 1, 1, 5)
-        drain("q", 1, 1, S, 7)
+        drain_pair("c", 2, (0, 1))
         quant_turned("c", 2, 0)
-        weave_half("s", 0, 0, 1, S, 0, 128, 0)
-        finish_prior(3)
+        spread_prior(3)
         quant_turned("c", 2, 1)
-        quant_turned("c", 3, 0)
-        quant_turned("c", 3, 1)
+        turn_pair("c", 3, 4)
+        drain_pair("c", 3, (2, 3))
+        quant_pair("c", 3)
+        turn_pair("q", 0, 6)
+        drain_pair("q", 0, (4, 5))
+        turn_gain(0)
         drain_gain()
+        turn_pair("q", 1, 4)
+        drain_pair("q", 1, (6, 7))
         quant_turned("q", 0, 0)
-        park_pass(0, 0, 0)
         sort("q", 2, V)
-        park_pass(1, 0, 1)
         quant_turned("q", 0, 1)
-        park_pass(0, 1, 0)
-        weave_half("s", 0, 0, 1, V, 128, 256, 0)
-        park_pass(1, 1, 1)
-        quant_turned("q", 1, 0)
-        turn("q", 2, 0, 6)
-        quant_turned("q", 1, 1)
-        weave_half("s", 0, 0, 0, G, 0, 192, 7)
-        turn("q", 2, 1, 7)
-        weave_half("s", 0, 0, 0, S, 192, 256, 7)
+
+        park_passes(0, 0)
+        weave_half("s", 0, 0, 1, V, 0, QUARTER, HALF)
+        weave_half("s", 0, 0, 1, S, 0, 0, QUARTER)
+        quant_pair("q", 1)
         sort("q", 3, V)
+        weave_half("s", 0, 0, 0, G, 7, 0, SHORT_RUN)
+        weave_half("s", 0, 0, 0, S, 7, SHORT_RUN, HALF)
         load_piece("r", 2, 0)
-        turn("q", 3, 0, 4)
-        drain("q", 2, 0, S, 1)
-        park(0)
-        turn("q", 3, 1, 5)
-        drain("q", 2, 1, S, 2)
-        park(1)
-        park_pass(2, 0, 2)
-        drain("q", 3, 0, S, 4)
+        park(TILES[0:2])
+
+        turn_pair("q", 2, 6)
+        park_passes(1, 2)
+        drain_pair("q", 2, (1, 2))
+        weave_half("r", 0, 0, 1, S, 3)
         quant_half("s", 0, 0, 1)
-        park_pass(3, 0, 3)
-        drain("q", 3, 1, S, 5)
-        quant_turned("q", 2, 0)
-        park_pass(2, 1, 2)
-        weave_half("r", 0, 0, 1, S, 0, 256, 3)
-        quant_turned("q", 2, 1)
-        weave_half("r", 0, 0, 0, G, 0, 192, 2)
-        park_pass(3, 1, 3)
-        weave_half("r", 0, 0, 0, S, 192, 256, 2)
+        quant_pair("q", 2)
         quant_half("s", 0, 0, 0)
+        weave_half("r", 0, 0, 0, G, 2, 0, SHORT_RUN)
+        park(TILES[2:4])
+
+        turn_pair("q", 3, 4)
+        turn_pair("c", 0, 6)
+        park_passes(2, 0)
+        drain_pair("q", 3, (4, 5))
+        weave_half("r", 0, 0, 0, S, 2, SHORT_RUN, HALF)
         load_piece("r", 1, 1)
-        turn("c", 0, 0, 6)
-        drain("c", 0, 0, S, 6)
-        park(2)
-        turn("c", 0, 1, 7)
-        drain("c", 0, 1, S, 1)
-        park(3)
-        turn("c", 1, 0, 4)
-        drain("c", 1, 0, S, 0)
-        quant_turned("q", 3, 0)
-        turn("c", 1, 1, 5)
-        drain("c", 1, 1, S, 7)
-        quant_turned("q", 3, 1)
-        park_pass(4, 0, 0)
-        weave_half("s", 1, 0, 0, S, 0, 256, 5)
-        weave_half("s", 1, 0, 1, V, 0, 256, 4)
-        load_piece("r", 2, 1)
-        park_pass(5, 0, 1)
-        quant_turned("c", 0, 0)
-        park_pass(4, 1, 0)
-        quant_half("r", 0, 0, 0)
-        park_pass(5, 1, 1)
-        quant_turned("c", 0, 1)
-        park_pass(6, 0, 2)
-        weave_half("r", 1, 0, 1, S, 128, 256, 1)
-        quant_turned("c", 1, 0)
-        park_pass(7, 0, 3)
-        weave("r", 0, 1, S, 0, 512)
-        quant_turned("c", 1, 1)
-        weave_half("r", 1, 0, 0, G, 0, 256, 7)
-        park_pass(6, 1, 2)
-        weave("s", 2, 0, S, 0, 256)
-        quant_half("r", 0, 0, 1)
-        weave_half("r", 1, 0, 1, G, 0, 128, 1)
-        load_piece("s", 0, 1)
-        load_piece("s", 1, 1)
-        park_pass(7, 1, 3)
-        weave("r", 2, 0, S, 0, 256)
-        park(4)
-        qc_pass(0, [4, 5, 6, 7], 0)
-        weave("r", 1, 1, S, 0, 256)
-        park(5)
-        qc_pass(0, [4, 5, 6, 7], 1)
-        park(6)
-        park(7)
-        qc_pass(0, [0, 1, 2, 3], 0)
-        quant_half("s", 1, 0, 0)
-        qc_pass(0, [0, 1, 2, 3], 1)
+        quant_pair("q", 3)
+        drain_pair("c", 0, (6, 1))
+        weave_half("s", 1, 0, 1, V, 4)
+        weave_half("s", 1, 0, 0, S, 5, 0, QUARTER)
+        for h in range(2):
+            quant_turned("c", 0, h)
+            quant_half("r", 0, 0, h)
+
+        turn_pair("c", 1, 4)
+        park_passes(3, 2)
+        drain_pair("c", 1, (0, 7))
+        quant_pair("c", 1)
         quant_half("s", 1, 0, 1)
-        rs_pass(0, [0, 1, 2, 3], 0)
-        quant_half("r", 1, 0, 0)
-        quant_half("r", 1, 0, 1)
-        rs_pass(0, [0, 1, 2, 3], 1)
-        weave("s", 2, 0, V, 256, 512)
+        weave_half("s", 1, 0, 0, S, 5, QUARTER, HALF)
+        load_piece("r", 2, 1)
+        weave_half("r", 1, 0, 0, G, 7)
+        weave_half("r", 1, 0, 1, G, 1, 0, QUARTER)
+        weave_half("r", 1, 0, 1, S, 1, QUARTER, HALF)
+        load_piece("s", 0, 1)
+        park(LATE)
+
+        qc_passes(0, [6, 7, 4, 5])
+        qc_passes(0, EARLY)
+        quant_half("s", 1, 0, 0)
+        quant_halves("r", 1, 0)
+        rs_pass(0, EARLY, 0)
+        rs_pass(0, EARLY, 1)
+        weave("r", 0, 1, S)
+        load_piece("s", 1, 1)
+        behind = ("r", 0, 1)
+        for piece in (("s", 2, 0), ("r", 2, 0), ("r", 1, 1), ("r", 2, 1)):
+            weave(*piece, S, 0, HALF)
+            weave(*piece, V, HALF, NB)
+            quant_piece(*behind)
+            behind = piece
+        weave_half("s", 0, 1, 0, S, 0)
+        weave_half("s", 0, 1, 1, V, 2)
+        quant_piece(*behind)
+        quant_halves("s", 0, 1, (1, 0))
+        rs_pass(0, LATE, 0)
+        rs_pass(0, EARLY, 2)
+        rs_pass(0, LATE, 1)
+        rs_pass(0, LATE, 2)
+
         load_piece("s", 2, 1)
-        load_two_pieces("s", 0, 2)
+        load_two_pieces(0)
         load_pair("c", 4)
         load_pair("c", 5)
-        load_two_pieces("s", 1, 2)
-        load_two_pieces("s", 2, 2)
-        load_quads(3, 0)
-        load_quads(3, 1)
-        quant_piece("r", 0, 1, 0, 512)
-        rs_pass(0, [4, 5, 6, 7], 0)
-        weave("r", 2, 1, S, 0, 256)
-        weave("r", 2, 0, V, 256, 512)
-        weave_half("s", 0, 1, 0, S, 0, 256, 0)
-        quant_piece("s", 2, 0, 0, 512)
-        weave("r", 1, 1, V, 256, 512)
-        quant_piece("r", 2, 0, 0, 512)
-        rs_pass(0, [0, 1, 2, 3], 2)
-        scale_only(1)
-        weave("r", 2, 1, V, 256, 512)
-        scale_only(3)
-        quant_piece("r", 1, 1, 0, 512)
-        rs_pass(0, [4, 5, 6, 7], 1)
-        weave_half("s", 1, 1, 1, S, 128, 256, 3)
-        weave_half("s", 0, 1, 1, V, 0, 256, 2)
-        quant_piece("r", 2, 1, 0, 512)
-        rs_pass(0, [4, 5, 6, 7], 2)
-        scale_only(5)
-        quant_half("s", 0, 1, 1)
-        weave_half("s", 1, 1, 0, G, 0, 256, 2)
-        scale_only(7)
-        quant_half("s", 0, 1, 0)
-        weave_half("s", 1, 1, 1, G, 0, 128, 3)
-        weave_half("s", 2, 1, 0, S, 0, 256, 4)
-        finish(0, 0, 0, 512)
-        sort("c", 4, S)
-        finish(0, 2, 0, 512)
-        rs_pass(1, [0, 1, 2, 3], 0)
-        sort("c", 5, S)
-        finish(0, 4, 0, 512)
-        weave_half("s", 0, 2, 1, S, 128, 256, 7)
-        finish(0, 6, 0, 512)
-        rs_pass(1, [4, 5, 6, 7], 0)
-        weave("s", 1, 2, S, 0, 512)
-        quant_half("s", 1, 1, 0)
-        quant_half("s", 1, 1, 1)
-        rs_pass(1, [0, 1, 2, 3], 1)
-        weave_half("s", 2, 1, 1, V, 0, 256, 5)
-        quant_half("s", 2, 1, 0)
-        quant_half("s", 2, 1, 1)
-        weave_half("s", 0, 2, 0, G, 0, 256, 5)
-        rs_pass(1, [0, 1, 2, 3], 2)
-        add_prior(0, 1)
-        weave_half("s", 0, 2, 1, G, 0, 128, 7)
-        rs_pass(1, [4], 1)
-        finish(1, 0, 0, 512)
-        store(1, 0, 0, 512)
-        rs_pass(1, [4], 2)
-        finish(1, 1, 0, 512)
-        store(1, 1, 0, 512)
-        rs_pass(1, [5], 1)
-        finish(1, 2, 0, 512)
-        store(1, 2, 0, 512)
-        rs_pass(1, [5], 2)
-        finish(1, 3, 0, 512)
-        turn("c", 4, 0, 0)
-        drain("c", 4, 0, S, 0)
-        quant_half("s", 0, 2, 0)
-        turn("c", 5, 0, 1)
-        drain("c", 5, 0, S, 1)
-        quant_half("s", 0, 2, 1)
-        turn("c", 4, 1, 2)
-        drain("c", 4, 1, S, 2)
-        add_prior(0, 3)
-        store(1, 3, 0, 512)
-        turn("c", 5, 1, 3)
-        drain("c", 5, 1, S, 3)
-        quant_turned("c", 4, 0)
-        rs_pass(1, [6], 1)
-        weave_half("s", 2, 2, 0, S, 0, 256, 4)
-        quant_turned("c", 5, 0)
-        rs_pass(1, [6], 2)
-        weave_half("s", 2, 2, 1, S, 0, 256, 6)
-        finish(1, 4, 0, 512)
-        store(1, 4, 0, 512)
-        rs_pass(1, [7], 1)
-        sort_quads(3, 0, S)
-        quant_turned("c", 4, 1)
-        rs_pass(1, [7], 2)
-        weave("s", 0, 3, S, 0, 512)
-        quant_turned("c", 5, 1)
-        rs_pass(2, [0, 1, 2, 3], 0)
-        sort_quads(3, 1, S)
-        finish(1, 5, 0, 512)
-        qc_pass(2, [0, 1, 2, 3], 0)
-        quant_piece("s", 1, 2, 0, 512)
-        qc_pass(2, [0, 1, 2, 3], 1)
-        finish(1, 6, 0, 512)
-        store(1, 6, 0, 512)
-        rs_pass(2, [0, 1, 2, 3], 1)
-        finish(1, 7, 0, 512)
-        quant_half("s", 2, 2, 0)
-        weave_half("s", 1, 3, 0, G, 0, 256, 4)
-        quant_half("s", 2, 2, 1)
-        weave_half("s", 1, 3, 1, G, 0, 256, 6)
-        rs_pass(2, [0, 1, 2, 3], 2)
-        turn_quads(3, 0)
-        qc_pass(2, [4], 0)
-        pair_quads(3, 0, S)
-        finish(2, 0, 0, 512)
-        store(2, 0, 0, 512)
-        qc_pass(2, [4], 1)
-        weave("s", 2, 3, S, 0, 512)
-        finish(2, 1, 0, 512)
-        store(2, 1, 0, 512)
-        rs_pass(2, [4], 0)
-        finish(2, 2, 0, 512)
-        store(2, 2, 0, 512)
-        rs_pass(2, [4], 1)
-        finish(2, 3, 0, 512)
-        store(2, 3, 0, 512)
-        rs_pass(2, [4], 2)
-        add_prior(0, 5)
-        store(1, 5, 0, 512)
-        qc_pass(2, [5], 0)
-        add_prior(0, 7)
-        store(1, 7, 0, 512)
-        qc_pass(2, [5], 1)
-        quant_piece("s", 0, 3, 0, 512)
-        rs_pass(2, [5], 0)
-        turn_quads(3, 1)
-        rs_pass(2, [5], 1)
-        pair_quads(3, 1, S)
-        quant_half("s", 1, 3, 0)
-        rs_pass(2, [5], 2)
-        quant_half("s", 1, 3, 1)
-        qc_pass(2, [6], 0)
-        quant_quads(3, 0)
-        qc_pass(2, [6], 1)
-        finish(2, 4, 0, 512)
-        store(2, 4, 0, 512)
-        rs_pass(2, [6], 0)
-        quant_piece("s", 2, 3, 0, 512)
-        rs_pass(2, [6], 1)
-        finish(2, 5, 0, 512)
-        store(2, 5, 0, 512)
-        rs_pass(2, [6], 2)
-        quant_quads(3, 1)
-        qc_pass(2, [7], 0)
-        finish(2, 6, 0, 512)
-        store(2, 6, 0, 512)
-        qc_pass(2, [7], 1)
-        rs_pass(2, [7], 0)
-        rs_pass(2, [7], 1)
-        rs_pass(2, [7], 2)
-        finish(2, 7, 0, 512)
-        store(2, 7, 0, 512)
-        rs_pass(3, [0, 1, 2, 3], 0)
-        rs_pass(3, [0, 1, 2, 3], 1)
-        qc_pass(3, [0, 1, 2, 3], 0)
-        rs_pass(3, [0, 1, 2, 3], 2)
-        qc_pass(3, [0, 1, 2, 3], 1)
-        finish(3, 0, 0, 512)
-        store(3, 0, 0, 512)
-        qc_pass(3, [4], 0)
-        finish(3, 1, 0, 512)
-        store(3, 1, 0, 512)
-        qc_pass(3, [4], 1)
-        finish(3, 2, 0, 512)
-        store(3, 2, 0, 512)
-        rs_pass(3, [4], 0)
-        finish(3, 3, 0, 512)
-        store(3, 3, 0, 512)
-        rs_pass(3, [4], 1)
-        rs_pass(3, [4], 2)
-        finish(3, 4, 0, 512)
-        store(3, 4, 0, 512)
-        qc_pass(3, [5], 0)
-        qc_pass(3, [5], 1)
-        rs_pass(3, [5], 0)
-        rs_pass(3, [5], 1)
-        rs_pass(3, [5], 2)
-        finish(3, 5, 0, 512)
-        store(3, 5, 0, 512)
-        qc_pass(3, [6], 0)
-        qc_pass(3, [6], 1)
-        rs_pass(3, [6], 0)
-        rs_pass(3, [6], 1)
-        rs_pass(3, [6], 2)
-        finish(3, 6, 0, 512)
-        store(3, 6, 0, 512)
-        last_part(0, 256, 7)
-        finish(3, 7, 0, 256)
-        store(3, 7, 0, 256)
-        last_part(256, 512, 0)
-        finish(3, 7, 256, 512)
-        store(3, 7, 256, 512)
+        load_two_pieces(1)
+        load_two_pieces(2)
+        for g in range(E_PASSES):
+            load_quads(g)
+
+        weave_half("s", 1, 1, 0, G, 2)
+        weave_half("s", 1, 1, 1, G, 3, 0, QUARTER)
+        for m in EARLY[0::2]:
+            finish(0, m)
+            scale_only(m + 1)
+        weave_half("s", 1, 1, 1, S, 3, QUARTER, HALF)
+        for m in LATE[0::2]:
+            finish(0, m)
+            scale_only(m + 1)
+        rs_pass(1, TILES, 0)
+        quant_halves("s", 1, 1)
+        rs_pass(1, EARLY, 1)
+        weave_half("s", 2, 1, 0, S, 4)
+        weave_half("s", 2, 1, 1, V, 5)
+        quant_halves("s", 2, 1)
+        add_prior(1)
+        rs_pass(1, EARLY, 2)
+        for a in (4, 5):
+            sort("c", a, S)
+        weave_half("s", 0, 2, 0, G, 5)
+        weave_half("s", 0, 2, 1, G, 7, 0, QUARTER)
+        weave_half("s", 0, 2, 1, S, 7, QUARTER, HALF)
+        for m in EARLY:
+            finish(1, m)
+        store(1, 0)
+        store(1, 1)
+        store(1, 2)
+        weave("s", 1, 2, S)
+        quant_halves("s", 0, 2)
+        add_prior(3)
+        store(1, 3)
+
+        for m in LATE[:2]:
+            close_tile(1, m, 1)
+        for g in range(E_PASSES):
+            for h in range(2):
+                turn("c", 4 + h, g, EARLY[2 * g + h])
+                drain("c", 4 + h, g, 2 * g + h)
+        for m in LATE[2:]:
+            close_tile(1, m, 1)
+        for g in range(E_PASSES):
+            for a in (4, 5):
+                quant_turned("c", a, g)
+            finish(1, LATE[g])
+        store(1, 4)
+        quant_piece("s", 1, 2)
+        for m in LATE[2:]:
+            finish(1, m)
+        store(1, 6)
+
+        rs_pass(2, EARLY, 0)
+        qc_passes(2, EARLY)
+        rs_pass(2, EARLY, 1)
+        weave_half("s", 2, 2, 0, S, 4)
+        weave_half("s", 2, 2, 1, S, 6)
+        quant_halves("s", 2, 2)
+        rs_pass(2, EARLY, 2)
+        sort_quads(0)
+        weave_half("s", 1, 3, 0, G, 4)
+        weave_half("s", 1, 3, 1, G, 6)
+        turn_quads(0)
+        weave("s", 0, 3, S)
+        pair_quads(0)
+        for m in EARLY:
+            finish(2, m)
+            store(2, m)
+        for m in LATE[1::2]:
+            add_prior(m)
+            store(1, m)
+        for m in LATE:
+            close_tile(2, m)
+        quant_piece("s", 0, 3)
+        sort_quads(1)
+        turn_quads(1)
+        quant_halves("s", 1, 3)
+        quant_quads(0)
+        weave("s", 2, 3, S)
+        pair_quads(1)
+        finish(2, LATE[0])
+        quant_piece("s", 2, 3)
+        finish(2, LATE[1])
+        quant_quads(1)
+        for m in LATE[2:]:
+            finish(2, m)
+        for m in LATE:
+            store(2, m)
+
+        rs_pass(LAST, EARLY, 0)
+        rs_pass(LAST, EARLY, 1)
+        qc_pass(LAST, EARLY, 0)
+        rs_pass(LAST, EARLY, 2)
+        qc_pass(LAST, EARLY, 1)
+        for m in EARLY:
+            finish(LAST, m)
+            store(LAST, m)
+        for m in LATE[:-1]:
+            close_tile(LAST, m)
+            finish(LAST, m)
+            store(LAST, m)
+        m = TILES[-1]
+        for h, bank in enumerate((m, 0)):
+            lo, hi = h * HALF, (h + 1) * HALF
+            close_last_half(h, bank)
+            scale_and_add(result_tile(LAST, m)[:, lo:hi], last_acc[h][:], m, strip_prior(LAST, lo, hi))
+            store(LAST, m, lo, hi)

@@ -30,6 +30,7 @@ QUAD = 32
 STRIP_ROWS = NB // (2 * QUAD)
 ALIGN = 256
 SHORT_RUN = 192
+LONG_RUN = 352
 V, S, G = "vector", "scalar", "gpsimd"
 
 
@@ -511,11 +512,11 @@ def tile_rocchio_feedback_rescore_s2_kernel(tc, queries, corpus, relevance, sim,
             load_quads(g)
 
         weave_half("s", 1, 1, 0, G, 2)
-        weave_half("s", 1, 1, 1, G, 3, 0, QUARTER)
+        weave_half("s", 1, 1, 1, G, 3, 0, LONG_RUN - HALF)
         for m in EARLY[0::2]:
             finish(0, m)
             scale_only(m + 1)
-        weave_half("s", 1, 1, 1, S, 3, QUARTER, HALF)
+        weave_half("s", 1, 1, 1, S, 3, LONG_RUN - HALF, HALF)
         for m in LATE[0::2]:
             finish(0, m)
             scale_only(m + 1)
@@ -530,8 +531,8 @@ def tile_rocchio_feedback_rescore_s2_kernel(tc, queries, corpus, relevance, sim,
         for a in (4, 5):
             sort("c", a, S)
         weave_half("s", 0, 2, 0, G, 5)
-        weave_half("s", 0, 2, 1, G, 7, 0, QUARTER)
-        weave_half("s", 0, 2, 1, S, 7, QUARTER, HALF)
+        weave_half("s", 0, 2, 1, G, 7, 0, SHORT_RUN)
+        weave_half("s", 0, 2, 1, S, 7, SHORT_RUN, HALF)
         for m in EARLY:
             finish(1, m)
         store(1, 0)

from contextlib import ExitStack

import concourse.mybir as mybir
from concourse.masks import make_identity

F32 = mybir.dt.float32
BF16 = mybir.dt.bfloat16
U32 = mybir.dt.uint32
U8 = mybir.dt.uint8
E4M3X4 = mybir.dt.float8_e4m3fn_x4
E5M2X4 = mybir.dt.float8_e5m2_x4
MULT = mybir.AluOpType.mult
ADD = mybir.AluOpType.add
COPY = mybir.ActivationFunctionType.Copy

M, N, E, J = 1024, 2048, 1024, 1536
FLOPS = 2 * M * N * (E + J)

P = 128
E_PASSES = E // 512
J_PASSES = J // 512
NB = 512
HALF = NB // 2
QUARTER = NB // 4
TILES = range(M // P)
EARLY, LATE = TILES[:4], TILES[4:]
PARKED, LAST = 1, 3
PASS_WORDS = 256
QUAD = 32
STRIP_ROWS = NB // (2 * QUAD)
ALIGN = 256
SHORT_RUN = 192
LONG_RUN = 352
V, S, G = "vector", "scalar", "gpsimd"


def tile_rocchio_feedback_rescore_s2_kernel(tc, queries, corpus, relevance, sim, gain, prior, out):
    nc = tc.nc
    with ExitStack() as ctx:
        keep = ctx.enter_context(tc.tile_pool(name="keep", bufs=1))
        raw = ctx.enter_context(tc.tile_pool(name="raw", bufs=1))
        stage = ctx.enter_context(tc.tile_pool(name="stage", bufs=1))
        psum = ctx.enter_context(tc.psum_pool(name="psum", bufs=1))
        ctx.enter_context(tc.manual_schedule())

        ident = keep.tile([P, P], F32, name="ident")
        ident_bf = keep.tile([P, P], BF16, name="ident_bf")
        gain_rows = keep.tile([P, P], BF16, name="gain_rows")
        gain_col = keep.tile([P, len(TILES)], F32, name="gain_col")
        prior_raw = keep.tile([P, 2 * QUAD], BF16, name="prior_raw", align_bytes=ALIGN)
        prior_turned = keep.tile([P, QUAD], F32, name="prior_turned", align_bytes=ALIGN)
        prior_repeated = keep.tile([P, QUAD, QUAD], F32, name="prior_repeated", align_bytes=ALIGN)
        prior_words = keep.tile([P, QUAD, QUAD], F32, name="prior_words", align_bytes=ALIGN)

        def operand_tile(pool, width, dtype, name, bufs=1):
            flat = pool.tile([P, width], dtype, name=name, bufs=bufs, align_bytes=ALIGN)
            return flat[:]

        by_pair = "p (a g r) -> p a g r"
        by_pass = "p (c m) -> p c m"
        q_codes = operand_tile(keep, E_PASSES * M, U32, "q_codes").rearrange(by_pair, g=E_PASSES, r=HALF)
        q_scales = operand_tile(keep, E_PASSES * M, U8, "q_scales").rearrange(by_pair, g=E_PASSES, r=HALF)
        r_codes = operand_tile(keep, J_PASSES * M, U32, "r_codes").rearrange(by_pass, c=J_PASSES)
        r_scales = operand_tile(keep, J_PASSES * M, U8, "r_scales").rearrange(by_pass, c=J_PASSES)

        pair_view = {
            "q": queries.rearrange("(a p t) e -> a p t e", p=P, t=2),
            "c": corpus.rearrange("(a p t) e -> a p t e", p=P, t=2),
        }
        piece_view = {
            "r": relevance.rearrange("(c p i) m -> c p i m", p=P, i=4),
            "s": sim.rearrange("(c p i) n -> c p i n", p=P, i=4),
        }
        quad_view = corpus.rearrange("(n a i) (g q e) -> n g q i a e", a=NB // QUAD, i=QUAD, g=E_PASSES, q=P // QUAD)
        pair_raw, pass_raw, piece_raw, quad_raw = {}, {}, {}, {}

        def pair_buffer(width=E):
            return raw.tile([P, 2, width], BF16, name="pair_raw_t", bufs=8, align_bytes=ALIGN)

        def load_pair(x, a):
            pair_raw[x, a] = pair_buffer()
            nc.sync.dma_start(out=pair_raw[x, a][:], in_=pair_view[x][a])

        def load_pair_by_pass(x, a):
            for g in range(E_PASSES):
                pass_raw[x, a, g] = pair_buffer(NB)
                nc.sync.dma_start(out=pass_raw[x, a, g][:], in_=pair_view[x][a, :, :, g * NB : (g + 1) * NB])

        def load_piece(x, c, b):
            piece = raw.tile([P, 4, NB], BF16, name="piece_raw_t", bufs=6, align_bytes=ALIGN)
            nc.sync.dma_start(out=piece[:], in_=piece_view[x][c, :, :, b * NB : (b + 1) * NB])
            piece_raw[x, c, b] = piece[:]

        def load_two_pieces(c):
            both = raw.tile([P, 4, 2 * NB], BF16, name="two_pieces_raw_t", bufs=J_PASSES, align_bytes=ALIGN)
            nc.sync.dma_start(out=both[:], in_=piece_view["s"][c, :, :, 2 * NB :])
            for h in range(2):
                piece_raw["s", c, 2 + h] = both[:, :, h * NB : (h + 1) * NB]

        def load_quads(g):
            quad_raw[g] = pair_buffer()
            rows = quad_raw[g][:].rearrange("p t e -> p (t e)").rearrange("p (a e) -> p a e", a=NB // QUAD)
            for q in (0, 2, 1, 3):
                nc.sync.dma_start(out=rows[q * QUAD : (q + 1) * QUAD], in_=quad_view[LAST, g, q])

        def load_prior():
            for q in range(P // QUAD):
                nc.sync.dma_start(out=prior_raw[q * QUAD : (q + 1) * QUAD, :], in_=prior.rearrange("(p i) -> p i", p=QUAD))

        def load_gain():
            nc.sync.dma_start(out=gain_rows[0 : len(TILES), :], in_=gain.rearrange("(m p) -> m p", p=P))

        def bank_tile(bank, shape=(P, NB), dtype=F32):
            return psum.tile(list(shape), dtype, name="bank_t", tag=f"bank{bank}")

        def slot_tile(slot):
            return stage.tile([P, HALF * 4], BF16, name="slot_t", tag=f"slot{slot}", align_bytes=ALIGN)

        def copy(engine, dst, src):
            if engine == S:
                nc.scalar.copy(out=dst, in_=src)
            elif engine == G:
                nc.gpsimd.tensor_scalar(out=dst, in0=src, scalar1=1.0, scalar2=0.0, op0=MULT, op1=ADD)
            else:
                nc.vector.tensor_copy(out=dst, in_=src)

        def quantize(codes, scales, values):
            nc.vector.quantize_mx(out=codes, scales=scales, in_=values)

        pair_sorted, turned, drained = {}, {}, {}
        c_codes, c_scales, s_codes, s_scales = {}, {}, {}, {}

        def sorted_buffer():
            return raw.tile([P, 4, 2, P], F32, name="sorted_t", bufs=2, align_bytes=ALIGN)

        def sort(x, a, engine):
            pair_sorted[x, a] = sorted_buffer()
            words = pair_raw[x, a][:].rearrange("p t e -> p (t e)").bitcast(F32)
            copy(engine, pair_sorted[x, a][:], words.rearrange("p (s w u) -> p s u w", s=4, u=2))

        def turn(x, a, g, bank):
            turned[x, a, g] = bank_tile(bank)
            for t in range(2):
                for u in range(2):
                    if (x, a) in pair_sorted:
                        words = pair_sorted[x, a][:, E_PASSES * t + g, u, :]
                    elif (x, a, g) in pass_raw:
                        words = pass_raw[x, a, g][:, t, :].bitcast(F32)[:, u::2]
                    else:
                        words = pair_raw[x, a][:, t, :].bitcast(F32)[:, PASS_WORDS * g + u : PASS_WORDS * (g + 1) : 2]
                    quarter = 2 * t + u
                    nc.tensor.transpose(turned[x, a, g][:, quarter * P : (quarter + 1) * P], words, ident[:])

        def drain(x, a, g, slot):
            drained[x, a, g] = slot_tile(slot)
            copy(
                S,
                drained[x, a, g][:].bitcast(F32).rearrange("p (r s) -> p r s", s=4),
                turned[x, a, g][:].rearrange("p (s r) -> p r s", s=4),
            )

        def turn_pair(x, a, bank):
            for g in range(E_PASSES):
                turn(x, a, g, bank + g)

        def drain_pair(x, a, slots):
            for g in range(E_PASSES):
                drain(x, a, g, slots[g])

        def new_corpus_operand(n, g):
            c_codes[n, g] = operand_tile(stage, NB, U32, "c_codes_t", 4)
            c_scales[n, g] = operand_tile(stage, NB, U8, "c_scales_t", 4)

        def quant_turned(x, a, g):
            if x == "q":
                codes, scales = q_codes[:, a, g, :], q_scales[:, a, g, :]
            else:
                n, h = divmod(a, 2)
                if h == 0:
                    new_corpus_operand(n, g)
                cols = slice(h * HALF, (h + 1) * HALF)
                codes, scales = c_codes[n, g][:, cols], c_scales[n, g][:, cols]
            quantize(codes.bitcast(E4M3X4), scales, drained[x, a, g][:])

        def quant_pair(x, a):
            for g in range(E_PASSES):
                quant_turned(x, a, g)

        quad_sorted, quad_turned, quad_ready = {}, {}, {}

        def woven_buffer():
            return stage.tile([P, NB, 4], BF16, name="woven_t", bufs=4, align_bytes=ALIGN)

        def sort_quads(g):
            quad_sorted[g] = sorted_buffer()
            words = quad_raw[g][:].rearrange("p t e -> p (t e)").bitcast(F32)
            copy(
                S,
                quad_sorted[g][:].rearrange("p s u w -> p (s u w)").rearrange("p (a u j) -> p a u j", u=2, j=QUAD),
                words.rearrange("p (a j u) -> p a u j", u=2, j=QUAD),
            )

        def turn_quads(g):
            quad_turned[g] = pair_buffer()
            nc.vector.transpose(
                out=quad_turned[g][:].rearrange("p t e -> p (t e)").bitcast(F32),
                in_=quad_sorted[g][:].rearrange("p s u w -> p (s u w)"),
            )

        def pair_quads(g):
            quad_ready[g] = woven_buffer()
            ready = quad_ready[g][:].rearrange("p w i -> p (w i)").bitcast(F32)
            words = quad_turned[g][:].rearrange("p t e -> p (t e)").bitcast(F32)
            copy(S, ready.rearrange("p (a i u) -> p a i u", i=QUAD, u=2), words.rearrange("p (a u i) -> p a i u", i=QUAD, u=2))

        def quant_quads(g):
            new_corpus_operand(LAST, g)
            quantize(c_codes[LAST, g].bitcast(E4M3X4), c_scales[LAST, g], quad_ready[g][:].rearrange("p w i -> p (w i)"))

        woven, half_woven = {}, {}

        def interleave(engine, dst, src):
            if engine == G:
                copy(engine, dst, src.rearrange("p i w -> p w i"))
            else:
                copy(engine, dst.rearrange("p (w j) i -> p w i j", j=4), src.rearrange("p i (w j) -> p w i j", j=4))

        def weave(x, c, b, engine, lo=0, hi=NB):
            if (x, c, b) not in woven:
                woven[x, c, b] = woven_buffer()
            interleave(engine, woven[x, c, b][:, lo:hi, :], piece_raw[x, c, b][:, :, lo:hi])

        def weave_half(x, c, b, h, engine, slot, lo=0, hi=HALF):
            if (x, c, b, h) not in half_woven:
                half_woven[x, c, b, h] = slot_tile(slot)
            dst = half_woven[x, c, b, h][:].rearrange("p (w i) -> p w i", i=4)
            interleave(engine, dst[:, lo:hi, :], piece_raw[x, c, b][:, :, h * HALF + lo : h * HALF + hi])

        def piece_operand(x, c, b, lo, hi):
            if x == "r":
                cols = slice(b * NB + lo, b * NB + hi)
                return r_codes[:, c, cols].bitcast(E5M2X4), r_scales[:, c, cols]
            if (c, b) not in s_codes:
                s_codes[c, b] = operand_tile(stage, NB, U32, "s_codes_t", 7)
                s_scales[c, b] = operand_tile(stage, NB, U8, "s_scales_t", 7)
            return s_codes[c, b][:, lo:hi].bitcast(E4M3X4), s_scales[c, b][:, lo:hi]

        def quant_piece(x, c, b):
            quantize(*piece_operand(x, c, b, 0, NB), woven[x, c, b][:].rearrange("p w i -> p (w i)"))

        def quant_half(x, c, b, h):
            quantize(*piece_operand(x, c, b, h * HALF, (h + 1) * HALF), half_woven[x, c, b, h][:])

        def quant_halves(x, c, b, order=(0, 1)):
            for h in order:
                quant_half(x, c, b, h)

        acc, parked_acc, last_acc, passes_done = {}, {}, {}, {}

        def mx_pass(dst, stationary, moving, start, stop):
            nc.tensor.matmul_mx(
                out=dst, lhsT=stationary[0], lhsT_scale=stationary[1], rhs=moving[0], rhs_scale=moving[1], start=start, stop=stop
            )

        def q_operand(m, g):
            a, h = divmod(m, 2)
            cols = slice(h * P, (h + 1) * P)
            return q_codes[:, a, g, cols].bitcast(E4M3X4), q_scales[:, a, g, cols]

        def r_operand(m, c):
            cols = slice(m * P, (m + 1) * P)
            return r_codes[:, c, cols].bitcast(E5M2X4), r_scales[:, c, cols]

        def c_operand(n, g, lo=0, hi=NB):
            return c_codes[n, g][:, lo:hi].bitcast(E4M3X4), c_scales[n, g][:, lo:hi]

        def s_operand(n, c, lo=0, hi=NB):
            return s_codes[c, n][:, lo:hi].bitcast(E4M3X4), s_scales[c, n][:, lo:hi]

        def tile_pass(n, m, stationary, moving):
            if (n, m) not in acc:
                acc[n, m] = bank_tile(m)
            passes_done[n, m] = passes_done.get((n, m), 0) + 1
            passes = J_PASSES if n == PARKED else E_PASSES + J_PASSES
            mx_pass(acc[n, m][:], stationary, moving, passes_done[n, m] == 1, passes_done[n, m] == passes)

        def qc_pass(n, tiles, g):
            for m in tiles:
                tile_pass(n, m, q_operand(m, g), c_operand(n, g))

        def qc_passes(n, tiles):
            for g in range(E_PASSES):
                qc_pass(n, tiles, g)

        def rs_pass(n, tiles, c):
            for m in tiles:
                tile_pass(n, m, r_operand(m, c), s_operand(n, c))

        def close_tile(n, m, first=0):
            if n != PARKED:
                qc_passes(n, [m])
            for c in range(first, J_PASSES):
                rs_pass(n, [m], c)

        def park_passes(a, bank):
            for g in range(E_PASSES):
                for h in range(2):
                    m = 2 * a + h
                    if g == 0:
                        parked_acc[m] = bank_tile(bank + h)
                    mx_pass(parked_acc[m][:], q_operand(m, g), c_operand(PARKED, g), g == 0, g == E_PASSES - 1)

        def close_last_half(h, bank):
            m, lo, hi = TILES[-1], h * HALF, (h + 1) * HALF
            last_acc[h] = bank_tile(bank, (P, HALF))
            operands = [(q_operand(m, g), c_operand(LAST, g, lo, hi)) for g in range(E_PASSES)]
            operands = operands + [(r_operand(m, c), s_operand(LAST, c, lo, hi)) for c in range(J_PASSES)]
            for j, (stationary, moving) in enumerate(operands):
                mx_pass(last_acc[h][:], stationary, moving, j == 0, j == len(operands) - 1)

        gain_turned = {}

        def turn_gain(bank):
            gain_turned[0] = bank_tile(bank, (P, P), BF16)
            nc.tensor.transpose(gain_turned[0][:], gain_rows[:], ident_bf[:])

        def drain_gain():
            nc.vector.tensor_copy(out=gain_col[:], in_=gain_turned[0][:, 0 : len(TILES)])

        def turn_prior():
            nc.vector.transpose(out=prior_turned[:], in_=prior_raw[:].bitcast(F32))

        def repeat_prior(n):
            rows = slice(n * STRIP_ROWS, (n + 1) * STRIP_ROWS)
            nc.vector.tensor_copy(
                out=prior_repeated[:, rows, :], in_=prior_turned[:, rows].unsqueeze(2).to_broadcast([P, STRIP_ROWS, QUAD])
            )

        def spread_prior(n):
            rows = slice(n * STRIP_ROWS, (n + 1) * STRIP_ROWS)
            nc.vector.transpose(
                out=prior_words[:, rows, :].rearrange("p b i -> p (b i)"),
                in_=prior_repeated[:, rows, :].rearrange("p b i -> p (b i)"),
            )

        prior_all = prior_words[:].rearrange("p w i -> p (w i)").bitcast(BF16)

        result, result_01 = {}, {}

        def result_tile(n, m):
            if (n, m) not in result:
                if n < 2:
                    result_01[m] = stage.tile([P, 2 * NB], F32, name="result_01_t", bufs=len(TILES))
                    result[0, m], result[1, m] = result_01[m][:, :NB], result_01[m][:, NB:]
                else:
                    single = stage.tile([P, NB], F32, name="result_t", bufs=len(TILES))
                    result[n, m] = single[:]
            return result[n, m]

        def scale_and_add(dst, sums, m, rest):
            nc.vector.scalar_tensor_tensor(out=dst, in0=sums, scalar=gain_col[:, m : m + 1], in1=rest, op0=MULT, op1=ADD)

        def strip_prior(n, lo=0, hi=NB):
            return prior_all[:, n * NB + lo : n * NB + hi]

        def park(tiles):
            for m in tiles:
                scale_and_add(result_tile(PARKED, m), parked_acc[m][:], m, strip_prior(PARKED))

        def finish(n, m):
            dst = result_tile(n, m)
            scale_and_add(dst, acc[n, m][:], m, dst if n == PARKED else strip_prior(n))

        def scale_only(m):
            nc.scalar.activation(out=result_tile(0, m), in_=acc[0, m][:], func=COPY, scale=gain_col[:, m : m + 1])

        def add_prior(m):
            nc.vector.tensor_tensor(out=result[0, m], in0=result[0, m], in1=strip_prior(0), op=ADD)

        def store(n, m, lo=0, hi=NB):
            rows = slice(m * P, (m + 1) * P)
            if n == PARKED:
                nc.sync.dma_start(out=out[rows, : 2 * NB], in_=result_01[m][:])
            else:
                nc.sync.dma_start(out=out[rows, n * NB + lo : n * NB + hi], in_=result[n, m][:, lo:hi])

        make_identity(nc, ident[:])
        nc.gpsimd.memset(gain_rows[:], 0.0)
        make_identity(nc, ident_bf[:])

        load_pair_by_pass("c", 2)
        load_prior()
        load_pair("c", 3)
        load_pair("q", 0)
        load_gain()
        load_pair("q", 1)
        load_pair("q", 2)
        load_piece("s", 0, 0)
        load_pair("q", 3)
        load_piece("r", 0, 0)
        load_pair("c", 0)

        turn_prior()
        repeat_prior(1)
        repeat_prior(0)
        spread_prior(1)
        spread_prior(0)
        repeat_prior(2)
        repeat_prior(3)
        spread_prior(2)

        turn_pair("c", 2, 2)
        load_pair("c", 1)
        load_piece("s", 1, 0)
        load_piece("r", 1, 0)
        load_piece("r", 0, 1)
        load_piece("s", 2, 0)
        drain_pair("c", 2, (0, 1))
        quant_turned("c", 2, 0)
        spread_prior(3)
        quant_turned("c", 2, 1)
        turn_pair("c", 3, 4)
        drain_pair("c", 3, (2, 3))
        quant_pair("c", 3)
        turn_pair("q", 0, 6)
        drain_pair("q", 0, (4, 5))
        turn_gain(0)
        drain_gain()
        turn_pair("q", 1, 4)
        drain_pair("q", 1, (6, 7))
        quant_turned("q", 0, 0)
        sort("q", 2, V)
        quant_turned("q", 0, 1)

        park_passes(0, 0)
        weave_half("s", 0, 0, 1, V, 0, QUARTER, HALF)
        weave_half("s", 0, 0, 1, S, 0, 0, QUARTER)
        quant_pair("q", 1)
        sort("q", 3, V)
        weave_half("s", 0, 0, 0, G, 7, 0, SHORT_RUN)
        weave_half("s", 0, 0, 0, S, 7, SHORT_RUN, HALF)
        load_piece("r", 2, 0)
        park(TILES[0:2])

        turn_pair("q", 2, 6)
        park_passes(1, 2)
        drain_pair("q", 2, (1, 2))
        weave_half("r", 0, 0, 1, S, 3)
        quant_half("s", 0, 0, 1)
        quant_pair("q", 2)
        quant_half("s", 0, 0, 0)
        weave_half("r", 0, 0, 0, G, 2, 0, SHORT_RUN)
        park(TILES[2:4])

        turn_pair("q", 3, 4)
        turn_pair("c", 0, 6)
        park_passes(2, 0)
        drain_pair("q", 3, (4, 5))
        weave_half("r", 0, 0, 0, S, 2, SHORT_RUN, HALF)
        load_piece("r", 1, 1)
        quant_pair("q", 3)
        drain_pair("c", 0, (6, 1))
        weave_half("s", 1, 0, 1, V, 4)
        weave_half("s", 1, 0, 0, S, 5, 0, QUARTER)
        for h in range(2):
            quant_turned("c", 0, h)
            quant_half("r", 0, 0, h)

        turn_pair("c", 1, 4)
        park_passes(3, 2)
        drain_pair("c", 1, (0, 7))
        quant_pair("c", 1)
        quant_half("s", 1, 0, 1)
        weave_half("s", 1, 0, 0, S, 5, QUARTER, HALF)
        load_piece("r", 2, 1)
        weave_half("r", 1, 0, 0, G, 7)
        weave_half("r", 1, 0, 1, G, 1, 0, QUARTER)
        weave_half("r", 1, 0, 1, S, 1, QUARTER, HALF)
        load_piece("s", 0, 1)
        park(LATE)

        qc_passes(0, [6, 7, 4, 5])
        qc_passes(0, EARLY)
        quant_half("s", 1, 0, 0)
        quant_halves("r", 1, 0)
        rs_pass(0, EARLY, 0)
        rs_pass(0, EARLY, 1)
        weave("r", 0, 1, S)
        load_piece("s", 1, 1)
        behind = ("r", 0, 1)
        for piece in (("s", 2, 0), ("r", 2, 0), ("r", 1, 1), ("r", 2, 1)):
            weave(*piece, S, 0, HALF)
            weave(*piece, V, HALF, NB)
            quant_piece(*behind)
            behind = piece
        weave_half("s", 0, 1, 0, S, 0)
        weave_half("s", 0, 1, 1, V, 2)
        quant_piece(*behind)
        quant_halves("s", 0, 1, (1, 0))
        rs_pass(0, LATE, 0)
        rs_pass(0, EARLY, 2)
        rs_pass(0, LATE, 1)
        rs_pass(0, LATE, 2)

        load_piece("s", 2, 1)
        load_two_pieces(0)
        load_pair("c", 4)
        load_pair("c", 5)
        load_two_pieces(1)
        load_two_pieces(2)
        for g in range(E_PASSES):
            load_quads(g)

        weave_half("s", 1, 1, 0, G, 2)
        weave_half("s", 1, 1, 1, G, 3, 0, LONG_RUN - HALF)
        for m in EARLY[0::2]:
            finish(0, m)
            scale_only(m + 1)
        weave_half("s", 1, 1, 1, S, 3, LONG_RUN - HALF, HALF)
        for m in LATE[0::2]:
            finish(0, m)
            scale_only(m + 1)
        rs_pass(1, TILES, 0)
        quant_halves("s", 1, 1)
        rs_pass(1, EARLY, 1)
        weave_half("s", 2, 1, 0, S, 4)
        weave_half("s", 2, 1, 1, V, 5)
        quant_halves("s", 2, 1)
        add_prior(1)
        rs_pass(1, EARLY, 2)
        for a in (4, 5):
            sort("c", a, S)
        weave_half("s", 0, 2, 0, G, 5)
        weave_half("s", 0, 2, 1, G, 7, 0, SHORT_RUN)
        weave_half("s", 0, 2, 1, S, 7, SHORT_RUN, HALF)
        for m in EARLY:
            finish(1, m)
        store(1, 0)
        store(1, 1)
        store(1, 2)
        weave("s", 1, 2, S)
        quant_halves("s", 0, 2)
        add_prior(3)
        store(1, 3)

        for m in LATE[:2]:
            close_tile(1, m, 1)
        for g in range(E_PASSES):
            for h in range(2):
                turn("c", 4 + h, g, EARLY[2 * g + h])
                drain("c", 4 + h, g, 2 * g + h)
        for m in LATE[2:]:
            close_tile(1, m, 1)
        for g in range(E_PASSES):
            for a in (4, 5):
                quant_turned("c", a, g)
            finish(1, LATE[g])
        store(1, 4)
        quant_piece("s", 1, 2)
        for m in LATE[2:]:
            finish(1, m)
        store(1, 6)

        rs_pass(2, EARLY, 0)
        qc_passes(2, EARLY)
        rs_pass(2, EARLY, 1)
        weave_half("s", 2, 2, 0, S, 4)
        weave_half("s", 2, 2, 1, S, 6)
        quant_halves("s", 2, 2)
        rs_pass(2, EARLY, 2)
        sort_quads(0)
        weave_half("s", 1, 3, 0, G, 4)
        weave_half("s", 1, 3, 1, G, 6)
        turn_quads(0)
        weave("s", 0, 3, S)
        pair_quads(0)
        for m in EARLY:
            finish(2, m)
            store(2, m)
        for m in LATE[1::2]:
            add_prior(m)
            store(1, m)
        for m in LATE:
            close_tile(2, m)
        quant_piece("s", 0, 3)
        sort_quads(1)
        turn_quads(1)
        quant_halves("s", 1, 3)
        quant_quads(0)
        weave("s", 2, 3, S)
        pair_quads(1)
        finish(2, LATE[0])
        quant_piece("s", 2, 3)
        finish(2, LATE[1])
        quant_quads(1)
        for m in LATE[2:]:
            finish(2, m)
        for m in LATE:
            store(2, m)

        rs_pass(LAST, EARLY, 0)
        rs_pass(LAST, EARLY, 1)
        qc_pass(LAST, EARLY, 0)
        rs_pass(LAST, EARLY, 2)
        qc_pass(LAST, EARLY, 1)
        for m in EARLY:
            finish(LAST, m)
            store(LAST, m)
        for m in LATE[:-1]:
            close_tile(LAST, m)
            finish(LAST, m)
            store(LAST, m)
        m = TILES[-1]
        for h, bank in enumerate((m, 0)):
            lo, hi = h * HALF, (h + 1) * HALF
            close_last_half(h, bank)
            scale_and_add(result_tile(LAST, m)[:, lo:hi], last_acc[h][:], m, strip_prior(LAST, lo, hi))
            store(LAST, m, lo, hi)
